import numpy as np, ml_dtypes
CORES = [48,51,52,55]
N = 4
BF = ml_dtypes.bfloat16
def gentries(a):
    return np.ascontiguousarray(a.reshape(8, 16, -1).transpose(0, 2, 1)).reshape(8, -1)
def gtable(e):
    e = np.asarray(e); return np.ascontiguousarray(e.reshape(8, -1, 16).transpose(0, 2, 1)).reshape(128, -1).astype(np.int32)
W, T, L, RO = 3072, 512, 8, 2
R = W >> 7
def chain(par, a):
    c = [a]
    for i in range(L - 1): c.append(np.take_along_axis(par, c[-1], 1))
    return np.stack(c, axis=1)
def meeting(ca, cb):
    eq = (ca[:, :, None] == cb[:, None]).reshape(8, L * L, T)
    found = np.any(eq, axis=1); first = np.argmax(eq, axis=1); i = first // L
    return found, np.where(found, i, 0), np.where(found, first - L * i, 0)
def one_round(f, par, a, b, own):
    ca, cb = chain(par, a), chain(par, b); found, I, J = meeting(ca, cb)
    pos = np.arange(L)[None, :, None]
    both = np.concatenate([ca, cb], axis=1); on = np.concatenate([pos < I[:, None], pos < J[:, None]], axis=1)
    mine = np.take_along_axis(own, both.reshape(8, -1), 1).reshape(8, 2 * L, T) == np.arange(T)
    kept = np.all(mine | ~on, axis=1)
    v = np.take_along_axis(f, both.reshape(1, 8, 1, -1), 3).reshape(N, 8, 16, 2 * L, T)
    sg = np.repeat(np.array([1, -1]), L)[:, None]
    D = np.sum(v * (sg * on)[None, :, None], axis=3, keepdims=True)
    n = (I + J + 1)[None, :, None, None]
    votes = np.sum((n * v <= sg * D) & on[None, :, None], axis=(0, 2))
    place = np.where(votes > 8 * N, np.tile(np.arange(L), 2)[:, None], -1)
    ka, kb = np.max(place[:, :L], axis=1), np.max(place[:, L:], axis=1)
    side = ka < 0; k = np.where(side, kb, ka); go = kept & found & (k >= 0); k = np.maximum(k, 0)
    s3 = side[:, None]; s5 = side[None, :, None, None]
    P, Q = np.where(s3, cb, ca), np.where(s3, ca, cb); X, Y = np.where(side, J, I), np.where(side, I, J)
    vp, vq = np.where(s5, v[:, :, :, L:], v[:, :, :, :L]), np.where(s5, v[:, :, :, :L], v[:, :, :, L:])
    M = np.take_along_axis(vp, k[None, :, None, None], 3)
    before = np.concatenate([np.zeros_like(M), vp[:, :, :, :-1]], axis=3)
    turn = pos <= k[:, None]
    newp = np.where(turn[None, :, None], M - before, vp - M); newq = vq + M
    g3 = go[:, None]
    to = np.concatenate([np.where(g3 & (pos < X[:, None]), P, W), np.where(g3 & (pos < Y[:, None]), Q, W)], axis=1)
    f2 = np.concatenate([f, np.zeros((N, 8, 16, 1), f.dtype)], axis=3)
    np.put_along_axis(f2, to.reshape(1, 8, 1, -1), np.concatenate([newp, newq], axis=3).reshape(N, 8, 16, -1), 3)
    p2 = np.concatenate([par, np.zeros((8, 1), par.dtype)], axis=1)
    np.put_along_axis(p2, np.where(g3 & turn, P, W).reshape(8, -1), np.concatenate([Q[:, :1], P[:, :-1]], axis=1).reshape(8, -1), 1)
    na = np.where(go, np.take_along_axis(P, k[:, None], 1)[:, 0], a)
    nb = np.where(go, np.take_along_axis(P, np.minimum(k + 1, L - 1)[:, None], 1)[:, 0], b)
    return f2[..., :W], p2[:, :W], na, nb
def forest(rng, q, ends):
    x = np.arange(W)
    pp = np.where(rng.random((8, W)) < q, x - R, x - 1 - (rng.random((8, W)) * np.minimum(x, 3 * R)).astype(np.int64)); pp[:, :R] = x[:R]
    lab = np.argsort(rng.random((8, W)), axis=1)
    if ends:
        for g in range(8):
            for at, num in ((W - 1, 0), (0, W - 1)):
                j = int(np.argmax(lab[g] == num)); lab[g, j] = lab[g, at]; lab[g, at] = num
    return pp, lab
def flows(rng, pp, lab):
    base = np.where(rng.random((W, 8, 1, 1)) < 0.55, np.exp2(6 * rng.random((W, 8, 1, 1))), 0)
    c = (2 * base * rng.random((W, 8, N, 16))).astype(np.int64); ar = np.arange(8)
    for x in range(W - 1, R - 1, -1): c[pp[:, x], ar] += c[x]
    f = np.zeros((N, 8, 16, W), np.int64)
    np.put_along_axis(f, lab[None, :, None], np.minimum(c, 4095).transpose(2, 1, 3, 0), 3)
    return f
def lay(rng, p, lo, spoil, fix=(), hold=()):
    kids = [[] for v in range(W)]
    for v in range(W):
        if p[v] != v: kids[p[v]].append(v)
    leaf = np.array([not c for c in kids])
    o = np.argsort(rng.random(W) + np.where(~leaf & (rng.random(W) < 0.7), 1.0, 0.0)); o = np.concatenate([np.array([0, W - 1]), o[(o != 0) & (o != W - 1)]])
    wi = np.where(rng.random(W) < 0.06, L, rng.integers(lo, L, W)); wj = np.where(rng.random(W) < 0.06, L, rng.integers(lo - 1, L, W))
    num = rng.permutation(T).tolist(); own = rng.integers(0, T, W).tolist(); a, b = rng.integers(0, W, (2, T)); free = [True] * W; made = 0
    for y in hold: free[y] = False
    tops = [v for v in range(W) if p[v] == v]; tops = [tops[i] for i in rng.permutation(len(tops))]; low = []
    for v in tops[:2 * (len(tops) // 4)]:
        for s in range(int(rng.integers(0, L))):
            if kids[v]: v = kids[v][int(rng.integers(0, len(kids[v])))]
        low.append(v)
    pairs = [(u, v) for u, v in fix] + [(u, v) for u, v in zip(low[::2], low[1::2])]
    for u, v in pairs:
        cu, cv = [u], [v]
        for s in range(L - 1):
            cu.append(p[cu[-1]]); cv.append(p[cv[-1]])
        i = next((s for s in range(L) if cu[s] in cv), L); j = cv.index(cu[i]) if i < L else L
        z = num[made]; made += 1; a[z] = u; b[z] = v
        for y in cu[:i] + cv[:j]:
            free[y] = False; own[y] = z
    for v, i, j in zip(o.tolist(), wi.tolist(), wj.tolist()):
        if made >= 15 * T // 16: break
        if not free[v] or p[v] == v: continue
        up = [v]; dn = []; x = p[v]
        while len(up) < i and free[x] and p[x] != x:
            up.append(x); x = p[x]
        while len(dn) < j:
            c = [y for y in kids[x] if free[y] and y != up[-1]]
            if not c: break
            c = [y for y in c if kids[y]] or c
            x = c[made % len(c)]; dn.append(x)
        z = num[made]; made += 1; a[z] = v; b[z] = x
        for y in up + dn:
            free[y] = False; own[y] = z
        if spoil > 0 and rng.random() < (0.5 if z >= T - 2 else spoil):
            near = z >= T - 2 or rng.random() < 0.5
            own[(up + dn)[int(rng.integers(0, len(up) + len(dn)))]] = z ^ 1 if near else (z + 1 + int(rng.integers(0, T - 1))) % T
    for i, z in enumerate(num[made:]):
        x = int(a[z])
        if i % 4 == 0: b[z] = x
        if i % 4 == 1:
            for s in range(1 + (i >> 2) % L): x = p[x]
            b[z] = x
        if i % 4 == 2:
            c = kids[p[p[x]]]
            if c: b[z] = c[i % len(c)]
    sw = rng.random(T) < 0.5; sw[np.array(num[:len(pairs)], np.int64)] = False
    return np.where(sw, b, a), np.where(sw, a, b), np.array(own)
def numbered(rng, up, fp, fix, hold):
    lab = rng.permutation(W); par = np.zeros(W, np.int64); par[lab] = lab[np.array(up)]
    f = np.zeros((N, 16, W), np.int64); f[:, :, lab] = fp
    return par, f, [[(int(lab[u]), int(lab[v])) for u, v in x] for x in fix], [int(lab[y]) for y in hold]
def beads(rng, line=False):
    most = L - 1 if line else 2 * (L - 1); total = min(W - 1, most * T); n = total // T + (np.arange(T) < total % T).astype(np.int64)
    o = rng.permutation(T); x, y = o[:T // 2], o[T // 2:]
    d = (rng.random(T // 2) * (np.minimum(most - n[x], n[y] - 1) + 1)).astype(np.int64); n[x] += d; n[y] -= d
    gap = np.bincount(rng.integers(0, T, W - 1 - total), minlength=T).tolist(); n = n.tolist()
    fp = rng.integers(0, 4096, (N, 16, W)); up = [0]; x = 0; fix = []
    for j in range(T):
        i = n[j] if line else int(rng.integers(max(0, n[j] - L + 1), min(n[j], L - 1) + 1)); br = []
        for c in (i, n[j] - i):
            y = x; z = []
            for s in range(c):
                up.append(y); y = len(up) - 1; z.append(y)
            br.append(z)
        A, B = br; fix.append((A[-1] if A else x, B[-1] if B else x))
        P, Q = (A, B) if len(A) >= len(B) else (B, A)
        fp[:, :, P] = rng.integers(2048, 4096, (N, 16, len(P)))
        if Q: fp[:, :, Q] = rng.integers(0, min(4095, 2048 * (len(P) - 1) // len(Q)) + 1, (N, 16, len(Q)))
        who = (rng.permutation(16 * N) < int(rng.integers(8 * N + 1, 16 * N + 1))).reshape(N, 16)
        m = P[int(rng.integers(0, len(P)))]; fp[:, :, m] = np.where(who, 0, fp[:, :, m]); x = P[-1]
        for s in range(gap[j]):
            up.append(x); x = len(up) - 1
    return numbered(rng, up, fp, [fix] + [[] for t in range(RO - 1)], [])
def straight(rng):
    return beads(rng, True)
def heavy(rng):
    S = L - 1; top = ((L - 2) * 4000 - 4095) // L; light = ((L - 2) * 4095 // S + (L - 2) * (top + 3995) // S) // 2
    up = [0]; fp = rng.integers(0, 4096, (N, 16, W)); fix = [[] for t in range(RO)]
    def put(at, lo, hi):
        up.append(at); fp[:, :, len(up) - 1] = rng.integers(lo, hi + 1, (N, 16))
        return len(up) - 1
    def lift(at, m, weak):
        q = put(at, light - 520, light - 480) if weak else put(at, 4045, 4095); y = at; P = []
        for s in range(S - 1, -1, -1):
            y = put(y, 4000, 4095) if s != m else put(y, 500, 500) if weak else put(y, top - 50, top)
            P.append(y)
        fix[0].append((y, q))
        return q, P[::-1]
    x = 0
    for u in range(16):
        x = put(x, 0, 4095); y1 = put(x, 0, 0); y0 = put(y1, 4000, 4095); fix[0].append((y0, x))
        weak = int(rng.integers(0, S)); y = x
        for i in range(S): y = lift(y, int(rng.integers(0, S)), u % 2 == 1 and i == weak)[0]
        fix[1].append((y, x if u % 2 == 1 else y1))
    if RO > 2:
        for u in range(8):
            x = put(x, 0, 4095); y1 = put(x, 0, 0); y0 = put(y1, 4000, 4095); fix[0].append((y0, x))
            q, P = lift(y0, 1, False); q2 = lift(y1, int(rng.integers(0, S)), False)[0]; q1 = lift(q2, int(rng.integers(0, S)), False)[0]
            fix[1].append((P[1], y0)); fix[1].append((q1, y0)); fix[2].append((P[0], y1))
    hold = [y for y in range(len(up))]
    while len(up) < W: up.append(len(up) - 1 - int(rng.random() * min(len(up), 3 * R)))
    return numbered(rng, up, fp, fix, hold)
def draw(rng, q=0.7, lo=1, spoil=0.12, ends=False, change=None, plant=None, still=False, make=()):
    pp, lab = forest(rng, q, ends); par = np.zeros((8, W), np.int64); np.put_along_axis(par, lab, np.take_along_axis(lab, pp, 1), 1)
    f = flows(rng, pp, lab) if change is None else change(rng)
    ts = []; rs = []; quiet = rng.permutation(8).tolist(); one = int(rng.integers(0, T))
    fix = [[[] for t in range(RO)] for g in range(8)]; hold = [[] for g in range(8)]
    for g, m in zip(quiet[2:], make):
        par[g], f[:, g], fix[g], hold[g] = m(rng)
    now = par
    for t in range(RO):
        z = [lay(rng, now[g].tolist(), lo, spoil, fix[g][t], hold[g]) for g in range(8)]
        a, b, own = [np.stack([y[i] for y in z]) for i in range(3)]
        if still:
            b[quiet[0]] = a[quiet[0]]; own[quiet[1]] = one
        if t == 0:
            if plant is not None: f = plant(rng, f, now, a, b, own)
            f0 = f
        ts.append(np.concatenate([a, b], axis=1)); rs.append(own)
        if t < RO - 1: f, now, a, b = one_round(f, now, a, b, own)
    return {"fl": np.ascontiguousarray(f0.reshape(N, 128, W)).astype(np.float32), "par": np.stack([par] * N).astype(np.int32),
            "tie": np.stack([gtable(np.concatenate(ts, axis=1))] * N), "res": np.stack([np.concatenate(rs, axis=1)] * N).astype(np.int32)}
def exact_votes(rng, f, par, a, b, own):
    f = f.copy(); ca, cb = chain(par, a), chain(par, b); found, I, J = meeting(ca, cb)
    for g in range(8):
        for j in range(T):
            X, Y = int(I[g, j]), int(J[g, j]); P, Q = ca[g, :X, j], cb[g, :Y, j]
            if X + Y == 0 or np.any(own[g, P] != j) or np.any(own[g, Q] != j): continue
            if X == 0 or (Y > 0 and rng.random() < 0.5): X, Y, P, Q = Y, X, Q, P
            m = int(rng.integers(0, X)); z = int(m > 0 and rng.random() < 0.5)
            h = int(rng.integers(1, 4095 // (X + Y) + 1)); top = (X - 1 - z) * h
            c = (8 * N - 1, 8 * N, 8 * N + 1, 8 * N + 2, 0, 16 * N)[(g + j) % 6]
            who = (rng.permutation(16 * N) < c).reshape(N, 16)
            if rng.random() < 0.5: who = rng.permuted((np.arange(16 * N) < c).reshape(N, 16)[rng.permutation(N)], axis=1)
            less = top - rng.integers(0, top + 1, (N, 16)) * rng.integers(0, 2, (N, 16))
            f[:, g, :, P] = (X + Y) * h; f[:, g, :, Q] = 0
            if z: f[:, g, :, int(P[m - 1])] = 0
            f[:, g, :, int(P[m])] = np.where(who, less, top + 1)
    return f
def few(rng):
    vals = np.array([0, 0, 0, 1, 2, 4095]); k = rng.choice(vals, (1, 8, 1, W))
    return np.where(rng.random((N, 8, 16, W)) < 0.15, rng.choice(vals, (N, 8, 16, W)), k)
def uneven(rng):
    return np.minimum((np.exp2(12 * rng.random((1, 8, 1, W))) * rng.random((N, 8, 16, W))).astype(np.int64), 4095)
def setup_inputs(rng):
    return draw(rng)
def setup_inputs_votes(rng):
    return draw(rng, spoil=0.05, plant=exact_votes)
def setup_inputs_ends(rng):
    return draw(rng, q=0.85, lo=L - 1, ends=True, make=(straight, beads))
def setup_inputs_flat(rng):
    return draw(rng, change=few, make=(heavy,))
def setup_inputs_still(rng):
    return draw(rng, q=0.6, spoil=0.0, still=True)
def setup_inputs_spread(rng):
    return draw(rng, q=0.75, change=uneven)
def check_inputs(d):
    bad = []
    for k, lo, hi in (("fl", 0, 4095), ("par", 0, W - 1), ("tie", 0, W - 1), ("res", 0, T - 1)):
        if not (np.min(d[k]) >= lo and np.max(d[k]) <= hi): bad.append("range of " + k)
    if np.any(d["fl"] != np.floor(d["fl"])): bad.append("whole numbers in fl")
    for k in ("par", "tie", "res"):
        if np.any(d[k] != d[k][:1]): bad.append(k + " alike on all ranks")
    if "range of par" not in bad:
        p = d["par"].astype(np.int64).reshape(-1, W); q = p
        for i in range(12): q = np.take_along_axis(q, q, 1)
        if np.any(np.take_along_axis(p, q, 1) != q): bad.append("every bus has a root")
    return bad
def reference(fl, par, tie, res):
    f = fl.astype(np.int64).reshape(N, 8, 16, W); p = par[0].astype(np.int64)
    e = gentries(tie[0]).astype(np.int64).reshape(8, RO, 2, T); own = res[0].astype(np.int64).reshape(8, RO, W); new = np.zeros_like(e)
    for t in range(RO):
        f, p, na, nb = one_round(f, p, e[:, t, 0], e[:, t, 1], own[:, t])
        new[:, t, 0] = na; new[:, t, 1] = nb
    return {"yf": f.reshape(N, 128, W).astype(np.float32), "yp": np.stack([p] * N).astype(np.float32), "yt": np.stack([gtable(new.reshape(8, -1))] * N).astype(np.float32)}

@@ -1,0 +1,640 @@
+import numpy as np
+from concourse.bass import DstId, RemoteDMATransfer
+from concourse.mybir import AluOpType, ActivationFunctionType
+
+S = 3072
+ZC = S
+NEG = S + 64
+WW = NEG + S
+F, B16, H16, I32, U16 = "float32", "bfloat16", "float16", "int32", "uint16"
+
+
+def sb(shape, d=F):
+    return ("sbuf", [128] + list(shape), d)
+
+
+SCRATCH = {
+    "W0": sb([WW]), "W1": sb([WW]), "XA": sb([3584]), "XB": sb([3584]), "C": sb([2, 904]),
+    "VT": sb([2, 14, 128], B16), "RR": sb([4, 128]), "Yg": sb([S]), "Yw": sb([1040]), "CW": sb([1040]),
+    "Win": sb([3088]), "X": sb([2, 160]), "TT": sb([2, 288]), "MI": sb([2176]), "T1": sb([512]), "T2": sb([512]),
+    "EQ": sb([768], B16), "PR": sb([768]), "P": sb([768]), "P2": sb([800]), "M": sb([800]), "VI": sb([768]),
+    "N": sb([768]), "TN": sb([800]), "TW": sb([1568]),
+    "Di": sb([768], I32), "Df": sb([768]), "tiei": sb([4, 32], I32), "ENDS": sb([4, 8]), "CH": sb([16, 16], U16),
+    "CHf": sb([272]), "AA": sb([512]), "NE": sb([512]), "ONES": sb([512]), "KS": sb([512]),
+    "IJ": sb([16], I32), "IJk": sb([16]), "k1": sb([8]), "k2": sb([8]), "k3": sb([8]),
+    "ON": sb([128]), "ONK": sb([128]), "AM": sb([128]), "LF": sb([144]), "t1": sb([128]), "t2": sb([128]),
+    "t3": sb([64]), "t4": sb([2, 32]), "t5": sb([2, 16]), "KK": sb([16]), "KP": sb([8]), "KW": sb([128]),
+    "t6": sb([2, 128]), "t7": sb([2, 64]), "t8": sb([2, 32]), "t9": sb([2, 16]), "PK2": sb([16]), "NG": sb([8]),
+    "u1": sb([16]), "u2": sb([16]), "Mi": sb([56], I32), "Wv": sb([128]),
+    "GL": sb([136], U16), "RL": sb([2, 48], U16), "RF": sb([2, 48]), "ZW": sb([48]), "Zi": sb([48], I32),
+    "SDi": sb([48], I32), "z1": sb([48]), "z2": sb([48]), "TSf": sb([48]), "TS": sb([48], U16), "DD": sb([48]),
+    "IXf": sb([48]), "VD": sb([48]), "D1": sb([48]), "E": sb([4, 128], B16),
+    "LS0": sb([4, 128], U16), "LS1": sb([4, 128], U16), "SB0": sb([128], U16), "SB1": sb([128], U16),
+    "L": sb([60, 8], U16),
+    "SV0": sb([4, 56], H16), "SV1": sb([4, 56], H16), "LV0": sb([4, 56], H16), "LV1": sb([4, 56], H16),
+    "UM0": sb([128], U16), "LU0": sb([4, 128], U16), "HU0": sb([128], U16),
+    "UY1": sb([32], U16), "LY1": sb([4, 32], U16), "UX1": sb([96], U16), "LX1": sb([4, 96], U16),
+    "UL": sb([4, 128], U16), "YTf": sb([4, 4, 8]),
+    "YB": sb([48]), "HB": sb([48]), "LB": sb([4, 48]),
+    "pi": sb([1], I32), "ci": sb([8], I32), "cf": sb([24]), "cn": sb([728]),
+    "PK": sb([4], U16), "WK": sb([4, 4], U16), "AL": sb([32], U16), "BL": sb([32], U16), "BJ": sb([8], U16),
+    "VL": sb([8], U16), "SL": sb([16], U16), "POS1": sb([128]), "TIE": sb([128]), "MK0": sb([4, 16]), "Hs": sb([128], B16),
+    "Sel": sb([4, 128], H16), "Gs": sb([2, 8], B16), "Gf": sb([8]), "Wa": sb([128], B16),
+    "Wb": sb([128], B16), "Wc": sb([128]), "Wd": sb([128]), "RC": sb([16]),
+    "Qp": ("psum", [128, 512], F), "PV": ("psum", [128, 512], F), "VS": ("psum", [128, 512], F),
+    "KE": ("psum", [128, 512], F), "Pp": ("psum", [128, 1024], F), "Dp": ("psum", [128, 1024], F),
+}
+DSEMS = ["d%d" % k for k in range(20)]
+ARR = ["E0", "E1", "V0", "V1", "U0", "Y1", "X1", "B", "hU0", "hB"]
+SEMAPHORES = ["sg", "sv", "ss", "st", "ls"] + DSEMS + ["a" + k for k in ARR]
+BLOCKS = [(0, 0, 8), (0, 8, 24), (0, 24, 48), (1, 0, 24), (1, 24, 48), (2, 0, 24), (2, 24, 48), (3, 0, 24), (3, 24, 40), (3, 40, 48)]
+
+
+def helpers(T, topo):
+    out = []
+    for c in T.cores:
+        free = [x for x in topo.cores_of(c) if x not in T.cores and x not in out and topo.may_write(c, x)]
+        near = [x for x in free if topo.die(x) == topo.die(c)]
+        out.append((near or free)[0])
+    return out
+
+
+def common(topo, me, cs):
+    m = -1
+    for c in cs:
+        m &= topo.mask(me, c)
+    return m
+
+
+def neng(topo, me, cs):
+    return bin(common(topo, me, cs)).count("1")
+
+
+def bcast(g, T, topo, me, src, dsts, name):
+    cs = [c for c, _ in dsts]
+    ids = [DstId(rid=topo.addr(c)[0], pnc=topo.addr(c)[1]) for c in cs]
+    g.remote_dma_fused([RemoteDMATransfer(dst_ids=ids, dma_engine_mask=common(topo, me, cs), remote_sem=T.sem["a" + name],
+                                          srcs=[src], dsts=[a for _, a in dsts])], local_sem=T.sem.ls)
+    return neng(topo, me, cs)
+
+
+def rank_program(g, core, T, topo):
+    o = T.rank_of(core)
+    cores = list(T.cores)
+    hl = helpers(T, topo)
+    if o is None:
+        if core in hl:
+            r = hl.index(core)
+            tot = 0
+            for nm, hb, lb in (("U0", "HU0", "LU0"), ("B", "HB", "LB")):
+                g.wait_ge(T.sem["ah" + nm], neng(topo, cores[r], [core]))
+                tot += bcast(g, T, topo, core, T[hb][:], [(cores[k], T[lb][:, r]) for k in range(4) if k != r], nm)
+            g.wait_ge(T.sem.ls, tot)
+        return
+    peers = [k for k in range(4) if k != o]
+    every = [o] + peers
+    Q = {"g": g, "v": g.vector, "s": g.scalar, "t": g.tensor, "y": g.sync}
+    QS = {"g": "sg", "v": "sv", "s": "ss", "t": "st"}
+    A = AluOpType
+    AF = ActivationFunctionType
+    ops, acc, groups, lsum = [], {}, {}, [0]
+    sl = slice
+
+    def R(name, *idx, p=(0, 128, 1)):
+        sh = SCRATCH[name][1]
+        if len(idx) == 0:
+            idx = (sl(0, sh[1]),)
+        ar = np.arange(int(np.prod(sh[1:]))).reshape(sh[1:])[idx]
+        lo, hi = int(ar.min()), int(ar.max()) + 1
+        p0, p1 = p[0], p[1]
+        if SCRATCH[name][0] == "psum":
+            lo, hi, p0, p1 = lo // 512 * 512, (hi + 511) // 512 * 512, 0, 128
+        ps = sl(p[0], p[1], p[2]) if len(p) > 2 and p[2] != 1 else sl(p[0], p[1])
+        return (T[name][(ps,) + idx], [(name, p0, p1, lo, hi, ar.ravel())])
+
+    def C(name, a, b, *idx, p=(0, 128, 1)):
+        return R(name, sl(a, b), *idx, p=p)
+
+    def ind(w, off):
+        return (w[0].indirect(off[0]), w[1] + off[1])
+
+    def regs(*xs):
+        return [r for x in xs if isinstance(x, tuple) for r in x[1]]
+
+    def val(x):
+        return x[0] if isinstance(x, tuple) else x
+
+    def rec(q, fn, rr, ww, kind="c", group=None):
+        n = len(ops)
+        deps = set()
+        for reg, isw in [(x, False) for x in rr] + [(x, True) for x in ww]:
+            ps = SCRATCH[reg[0]][0] == "psum"
+            for (r2, m, w2) in acc.get(reg[0], []):
+                if m not in deps and r2[1] < reg[2] and reg[1] < r2[2] and r2[3] < reg[4] and reg[3] < r2[4]:
+                    o2 = ops[m]
+                    if o2["q"] == q and o2["kind"] == "c" and kind == "c":
+                        if (w2 or isw) and q != "t" and len(np.intersect1d(reg[5], r2[5])):
+                            deps.add(m)
+                    elif (w2 or isw or ps) and not (kind == "d" and o2["kind"] == "d" and o2["group"] == group):
+                        deps.add(m)
+        for reg in rr:
+            acc.setdefault(reg[0], []).append((reg, n, False))
+        for reg in ww:
+            acc.setdefault(reg[0], []).append((reg, n, True))
+        ops.append({"q": q, "fn": fn, "deps": deps, "kind": kind, "group": group})
+
+    def cp(out, in_):
+        rec("v", lambda: g.vector.tensor_copy(out[0], in_[0]), regs(in_), regs(out))
+
+    def tt(out, a, b, op):
+        rec("v", lambda: g.vector.tensor_tensor(out[0], a[0], b[0], op), regs(a, b), regs(out))
+
+    def ts(out, a, s1, op0, s2=None, op1=None):
+        if s2 is None:
+            rec("v", lambda: g.vector.tensor_scalar(out[0], a[0], val(s1), None, op0), regs(a, s1), regs(out))
+        else:
+            rec("v", lambda: g.vector.tensor_scalar(out[0], a[0], val(s1), val(s2), op0, op1), regs(a, s1, s2), regs(out))
+
+    def scan(out, d0, d1, init, op0, op1):
+        rec("v", lambda: g.vector.tensor_tensor_scan(out[0], d0[0], d1[0], init, op0, op1), regs(d0, d1), regs(out))
+
+    def tr(out, in_):
+        rec("v", lambda: g.vector.transpose(out[0], in_[0]), regs(in_), regs(out))
+
+    def ms(out, c):
+        rec("v", lambda: g.vector.memset(out[0], c), [], regs(out))
+
+    def act(out, in_, bias=0.0, scale=1.0):
+        rec("s", lambda: g.scalar.activation(out[0], in_[0], AF.Identity, bias=val(bias), scale=val(scale)),
+            regs(in_, bias, scale), regs(out))
+
+    def mm(out, l, r, st, sp):
+        rec("t", lambda: g.tensor.matmul(out[0], l[0], r[0], st, sp), regs(l, r), regs(out))
+
+    def iota(out, pat, base):
+        rec("g", lambda: g.iota(out[0], pat, base, 0, allow_small_or_imprecise_dtypes=True), [], regs(out))
+
+    def dma(q, out, in_, group, also=None):
+        if group not in groups:
+            groups[group] = [DSEMS[len([x for x in groups if x not in ARR])], 0]
+        groups[group][1] += 16
+        rec(q, lambda: Q[q].dma_start(val(out), val(in_)), regs(in_, also), regs(out), "d", group)
+
+    def arrive(name, n, land):
+        groups[name] = ["a" + name, n]
+        rec("x", None, [], regs(*[R(land, k) for k in peers]), "a", name)
+
+    def send(name, src, dsts):
+        def fn():
+            lsum[0] += bcast(g, T, topo, core, src[0], dsts, name)
+        rec("g", fn, regs(src), [], "r")
+
+    def to_all(name, src, land):
+        send(name, R(src), [(cores[k], T[land][:, o]) for k in peers])
+
+    def relay(name, src, hb):
+        send("h" + name, R(src), [(hl[o], T[hb][:])])
+
+    n_direct = sum(neng(topo, cores[k], [cores[j] for j in range(4) if j != k]) for k in peers)
+    n_relay = sum(neng(topo, hl[k], [cores[j] for j in range(4) if j != k]) for k in peers)
+
+    def cf(k):
+        return C("cf", k, k + 1)
+
+    def cn(a, n):
+        return C("cn", a, a + n)
+
+    def blk(b):
+        return (32 * b, 32 * b + 32)
+
+    def rows(b, r):
+        return (32 * b + r, 32 * b + 32, 16)
+
+    def wrap768(src):
+        tr(C("TW", 0, 768), C(src, 16, 784))
+        tr(C("TW", 768, 1568), C(src, 0, 800))
+
+    def pick768(out, row):
+        cp(out, ind(R("TW"), R("WK", row, sl(0, 3))))
+
+    def place(dst, own, land):
+        for k in every:
+            for b in range(4):
+                cp(dst(k, b), own(b) if k == o else land(k, b))
+
+    dma("y", R("Di", p=(0, 8)), T.par[2 * o:2 * o + 2, :], "in")
+    dma("s", R("Di", p=(8, 16)), T.res[2 * o:2 * o + 2, 0:S], "in")
+    dma("s", R("Di", p=(16, 24)), T.res[2 * o:2 * o + 2, S:2 * S], "in")
+    dma("y", R("tiei"), T.tie[:], "tie")
+    rec("g", lambda: g.iota(T.pi[:], [[1, 1]], 0, 1), [], regs(R("pi")))
+    iota(C("Win", 0, 772), [[1, 772]], 0)
+    i_wk, i_al, i_bl, i_bj, i_rc, i_tie, i_g, i_sel, i_m, i_mk, i_vl = 160, 176, 208, 240, 248, 264, 392, 400, 528, 656, 720
+    iota(cn(i_g, 8), [[1, 8]], 0)
+    for sd in range(2):
+        iota(cn(16 + 56 * sd, 56), [[2, 4], [8, 7], [1, 2]], 64 * sd)
+    iota(cn(128, 32), [[0, 4], [1, 8]], 128)
+    iota(cn(i_al, 32), [[1, 8], [-32, 4]], 112)
+    iota(cn(i_bl, 32), [[1, 8], [0, 4]], 240)
+    iota(cn(i_bj, 8), [[8, 2], [0, 4]], 0)
+    iota(cn(i_vl, 8), [[32, 8]], 0)
+    iota(cn(i_wk, 16), [[1, 4], [256, 4]], 0)
+    iota(cn(i_tie, 128), [[0, 16], [16, 8]], 0)
+    iota(cn(i_rc, 16), [[1, 16]], 1)
+    iota(R("POS1"), [[0, 2], [1, 8], [0, 8]], 1)
+    iota(R("VI"), [[1, 768]], 0)
+    iota(cn(i_m, 128), [[1, 128]], 0)
+    iota(cn(i_sel, 128), [[32, 4], [1000, 2], [1, 16]], 0)
+    iota(cn(i_mk, 64), [[32, 4], [1, 16]], 0)
+    ms(R("PK"), 0)
+    ms(R("CH"), 0)
+    ms(R("X"), 0.0)
+    for k, (sh, mk) in enumerate(((3, 1), (0, 7), (0, 15), (4, 1), (0, 1), (5, 3), (4, 7), (0, 127))):
+        ts(C("ci", k, k + 1), R("pi"), sh, A.logical_shift_right, mk, A.bitwise_and)
+    cp(C("cf", 0, 8), R("ci"))
+    ms(cn(0, 16), 0.0)
+    ts(cf(9), cf(5), 768.0, A.mult)
+    ms(R("CHf"), 0.0)
+    tt(cf(8), cf(3), cf(4), A.not_equal)
+    for nm in ("Wa", "Wb", "Wc"):
+        ms(R(nm), 0.0)
+    ts(C("Win", 1544, 2316), C("Win", 0, 772), 1544.0, A.add)
+    act(C("Win", 772, 1544), C("Win", 0, 772), bias=772.0)
+    cp(R("Df", p=(0, 24)), R("Di", p=(0, 24)))
+    act(C("Win", 2316, 3088), C("Win", 0, 772), bias=2316.0)
+    k = 0
+    for row, c0 in ((0, 0), (3, 8), (2, 16)):
+        for b in range(4):
+            dma("ys"[k % 2], C("Win", 0, S, p=rows(b, row)), R("Df", p=(c0, c0 + 8)), "win0")
+            k += 1
+    for j in range(4):
+        dma("y", C("W0", 768 * j, 768 * j + 768), T.fl[:, 768 * j:768 * j + 768], "fl", C("Win", 0, 8))
+    ts(cf(10), cf(8), 144.0, A.mult)
+    ts(cf(14), cf(0), -16.0, A.mult)
+    ts(cf(11), cf(1), 16.0, A.mult, cf(10), A.add)
+    ts(cf(15), cf(1), -16.0, A.mult)
+    ts(C("PK", 0, 1), cf(0), 3.0, A.mult, cf(11), A.add)
+    ts(C("PK", 2, 3), cf(0), 2.0, A.mult, cf(11), A.add)
+    for b in range(4):
+        cp(R("ENDS", p=blk(b)), R("tiei", sl(0, 4), sl(8 * b, 8 * b + 8), p=blk(o)))
+    tr(R("TT", 0, sl(0, 128)), cn(16, 128))
+    tr(R("TT", 0, sl(128, 288)), cn(0, 160))
+    ts(R("AL"), cn(i_al, 32), cf(14), A.add)
+    cp(R("SL"), ind(R("TT", 0), C("PK", 0, 1)))
+    ts(R("BL"), cn(i_bl, 32), cf(15), A.add)
+    ts(R("BJ"), cn(i_bj, 8), cf(1), A.add)
+    ts(R("VL"), cn(i_vl, 8), cf(14), A.subtract, cf(1), A.add)
+    ts(cf(12), cf(8), 784.0, A.mult)
+    ms(R("ONES"), 1.0)
+    ts(cf(13), cf(2), 16.0, A.mult, cf(12), A.add)
+    ms(C("LF", 128, 144), 0.0)
+    ts(R("WK"), cn(i_wk, 16), cf(13), A.add)
+    ts(cf(16), cf(5), 128.0, A.mult, cf(2), A.add)
+    ms(C("M", 0, 16), 0.0)
+    ms(C("M", 784, 800), 0.0)
+    ts(R("Gf"), cn(i_g, 8), cf(6), A.is_equal)
+    ts(cf(19), cf(1), 7.0, A.is_lt)
+    ts(cf(20), cf(0), 0.25, A.mult, cf(1), A.add)
+    ts(cf(21), cf(1), 0.0, A.is_equal, float(ZC - NEG), A.mult)
+    ts(cf(22), cf(1), 0.0, A.is_gt, cf(19), A.mult)
+    ts(cf(20), cf(20), 1.0, A.add, cf(19), A.mult)
+    ts(cf(21), cf(21), float(NEG), A.add, cf(19), A.mult)
+
+    def constants_a():
+        ts(R("TIE"), cn(i_tie, 128), cf(16), A.add)
+        rec("v", lambda: g.vector.reciprocal(T.RC[:], cn(i_rc, 16)[0]), regs(cn(i_rc, 16)), regs(R("RC")))
+        ms(C("MI", 2048, 2176), -1.0)
+        ms(C("W0", ZC, NEG), 0.0)
+        ms(R("C", sl(0, 2), sl(0, 8)), 0.0)
+        cp(R("Gs", 0), R("Gf"))
+        ts(R("Gs", 1), R("Gf"), 65.0, A.mult)
+
+    def constants_b():
+        ts(cf(23), cf(2), 2.0, A.is_lt, -1.0, A.mult)
+        for nm, r, c in (("Wa", 0, 20), ("Wb", 2, 20), ("Wb", 1, 21), ("Wc", 0, 19), ("Wc", 1, 22)):
+            ts(R(nm, sl(r, 128, 16)), R("Gf"), cf(c), A.mult)
+        ts(R("Wd"), cn(i_m, 128), cf(7), A.is_equal, cf(23), A.mult)
+        ms(C("P2", 0, 16), 0.0)
+        ms(C("P2", 784, 800), 0.0)
+
+    def constants_c():
+        for u in range(2):
+            for h in range(2):
+                ts(R("Sel", 2 * u + h), cn(i_sel, 128), cf(7), A.subtract, 1000.0 * h - 16.0 * u, A.is_equal)
+        ms(R("Wv"), 0.0)
+        ts(cf(17), cf(3), -16.0, A.mult, cf(7), A.add)
+        ts(C("AA", 0, 128), cn(i_sel, 128), 500.0, A.is_gt)
+        ts(R("MK0"), cn(i_mk, 64), cf(17), A.is_equal)
+        ts(R("Hs"), C("AA", 0, 128), cf(3), A.is_equal)
+
+    def constants_d():
+        ms(C("CW", 1024, 1040), -1.0)
+        ms(C("TN", 0, 16), 0.0)
+        ms(C("TN", 784, 800), 0.0)
+        ms(C("Yw", 1024, 1040), 0.0)
+        ms(C("W1", ZC, NEG), 0.0)
+
+    def load_m(t):
+        for b in range(4):
+            dma("y", C("M", 16, 784, p=blk(b)), C("Win", 768 * b, 768 * b + 768, p=blk(b)), "m%d" % t)
+
+    def y_gather():
+        for b, c0, c1 in BLOCKS:
+            act(C("Yg", 768 * b + 16 * c0, 768 * b + 16 * c1), ind(R("Yw"), R("UL", b, sl(80 + c0, 80 + c1))))
+
+    def update(W, dst, store):
+        for b, c0, c1 in BLOCKS:
+            x0, x1 = 768 * b + 16 * c0, 768 * b + 16 * c1
+            tt(C(dst, x0, x1), ind(R(W), R("UL", b, sl(32 + c0, 32 + c1))), C("Yg", x0, x1), A.add)
+            if store:
+                dma("y", T.yf[:, x0:x1], C(dst, x0, x1), "out")
+
+    def y_window(W):
+        for sd in range(2):
+            for b in range(4):
+                act(C("Yw", 512 * sd + 128 * b, 512 * sd + 128 * b + 128), ind(R(W), R("UL", b, sl(8 * sd, 8 * sd + 8))))
+
+    def ends_out(t):
+        for sd in range(2):
+            cp(R("YTf", 2 * t + sd), C("UL", 0, 4, sl(16 + 8 * sd, 24 + 8 * sd)))
+
+    def per_tie_a():
+        tt(R("t2"), ind(R("KK"), R("BJ")), R("POS1"), A.is_equal)
+        ts(R("NG"), R("KP"), 0.0, A.is_equal)
+        ts(R("u2"), R("KK"), 0.0, A.is_gt, float(NEG), A.mult)
+        tt(R("t6", 0), ind(R("CHf"), R("VL")), R("t2"), A.mult)
+        tt(R("t6", 1), ind(C("CHf", 16, 272), R("VL")), R("t2"), A.mult)
+
+    def per_tie_b(t):
+        ts(C("u1", 0, 8), R("NG"), float(ZC), A.mult)
+        tt(R("t7"), C("t6", 0, 2, sl(0, 64)), C("t6", 0, 2, sl(64, 128)), A.add)
+        for sd in range(2):
+            tt(C("t3", 48 + 8 * sd, 56 + 8 * sd), C("u2", 8 * sd, 8 * sd + 8), C("u1", 0, 8), A.add)
+        tt(R("t8"), C("t7", 0, 2, sl(0, 32)), C("t7", 0, 2, sl(32, 64)), A.add)
+        tt(C("t3", 16, 24), R("NG"), R("ENDS", 2 * t), A.mult)
+        tt(R("t9"), C("t8", 0, 2, sl(0, 16)), C("t8", 0, 2, sl(16, 32)), A.add)
+        tt(C("t3", 24, 32), R("NG"), R("ENDS", 2 * t + 1), A.mult)
+        tt(R("PK2"), C("t9", 0, 2, sl(0, 8)), C("t9", 0, 2, sl(8, 16)), A.add)
+        for sd in range(2):
+            tt(C("t3", 8 * sd, 8 * sd + 8), C("t3", 48 + 8 * sd, 56 + 8 * sd), C("PK2", 0, 8), A.add)
+        tt(C("t3", 16, 32), C("t3", 16, 32), R("PK2"), A.add)
+        cp(C("UM0", 0, 32) if t == 0 else R("UY1"), C("t3", 0, 32))
+
+    def parents():
+        tt(C("Dp", 0, 768), C("Dp", 0, 768), C("TN", 16, 784), A.mult)
+        tt(R("N"), C("Dp", 0, 768), C("M", 16, 784), A.add)
+
+    def sources(ix, iy):
+        wrap768("TN")
+        pick768(R("IXf"), 0)
+        tt(R("z1"), R("IXf"), R("D1"), A.mult)
+        tt(R("z2"), R("IXf"), R("DD"), A.mult)
+        tt(R("z1"), R("z1"), R("VD"), A.add)
+        tt(R("z2"), R("z2"), R("TSf"), A.add)
+        cp(ix, R("z1"))
+        cp(iy, R("z2"))
+
+    def xv(nm, ch, pos):
+        return R(nm, sl(896 * ch + pos, 896 * ch + 896, 7))
+
+    def delta(c0, c1):
+        mm(C("Dp", c0, c1), R("Wb"), C("EQ", c0, c1), True, False)
+        mm(C("Dp", c0, c1), R("Wc"), C("PR", c0, c1), False, False)
+        mm(C("Dp", c0, c1), R("Wd"), C("M", 16 + c0, 16 + c1), False, True)
+
+    for t in range(2):
+        W = "W%d" % t
+        wn = C(W, 0, NEG)
+        pk = C("PK", 2 * t, 2 * t + 1)
+        for sd in range(2):
+            cp(R("CH", 8 * sd, sl(0, 8)), R("ENDS", 2 * t + sd))
+            act(C("CHf", 128 * sd, 128 * sd + 8), R("ENDS", 2 * t + sd))
+        for s in range(7):
+            for sd in range(2):
+                act(R("X", sd, sl(16, 144)), ind(R("Win"), R("CH", 8 * sd + s, sl(0, 8))))
+                if s + sd > 0:
+                    z = 16 * (8 * (1 - sd) + s + sd)
+                    act(C("CHf", z, z + 16), ind(R("TT", 1 - sd), pk))
+                tr(R("TT", sd, sl(0, 128)), R("X", sd, sl(16, 144)))
+                tr(R("TT", sd, sl(128, 288)), R("X", sd))
+                if s < 6:
+                    cp(R("CH", 8 * sd + s + 1), ind(R("TT", sd), pk))
+        act(C("CHf", 240, 256), ind(R("TT", 1), pk))
+        chw = R("CHf")
+        for hf in range(2):
+            act(C("AA", 256 * hf, 256 * hf + 256), ind(chw, C("AL", 16 * hf, 16 * hf + 16)))
+        if t == 0:
+            act(R("VI"), R("VI"), bias=cf(9))
+            constants_a()
+        else:
+            arrive("U0", n_relay, "LU0")
+            place(lambda k, b: R("UL", b, p=blk(k)), lambda b: R("UM0", p=blk(b)), lambda k, b: R("LU0", k, p=blk(b)))
+            y_window("W0")
+            y_gather()
+        ts(R("AM"), ind(chw, R("VL")), -float(ZC), A.add)
+        for hf in range(2):
+            tt(C("NE", 256 * hf, 256 * hf + 256), ind(chw, C("BL", 16 * hf, 16 * hf + 16)), C("AA", 256 * hf, 256 * hf + 256), A.not_equal)
+        scan(R("KS"), R("NE"), R("ONES"), 1.0, A.mult, A.add)
+        ks = R("KS", sl(63, 512, 64))
+        ts(C("IJ", 0, 8), ks, -4.5, A.add, 0.125, A.mult)
+        ts(R("k1"), C("IJ", 0, 8), 8.0, A.mult, 1.0, A.add)
+        tt(C("IJ", 8, 16), ks, R("k1"), A.subtract)
+        tt(R("ON"), ind(R("IJ"), R("BJ")), R("POS1"), A.is_ge)
+        tt(R("k2"), C("IJ", 0, 8), C("IJ", 8, 16), A.add)
+        tt(C("LF", 0, 128), R("AM"), R("ON"), A.mult)
+        ts(C("LF", 128, 136), R("k2"), 15.0, A.min, -float(ZC), A.add)
+        sbf, ls = "SB%d" % t, "LS%d" % t
+        ts(R(sbf), ind(R("LF"), C("SL", 0, 8)), float(ZC), A.add)
+        send("E%d" % t, C(sbf, 0, 120), [(cores[k], T[ls][:, o, 0:120]) for k in peers])
+        if t == 0:
+            load_m(0)
+        tt(R("t1"), ind(C("CHf", 24, 272), R("VL")), R("TIE"), A.not_equal)
+        ts(R("k3"), ks, 65.0, A.is_lt)
+        tt(R("t2"), R("t1"), R("ON"), A.mult)
+        tt(R("t3"), C("t2", 0, 64), C("t2", 64, 128), A.add)
+        tt(R("t8", 0), C("t3", 0, 32), C("t3", 32, 64), A.add)
+        tt(R("u2"), R("t8", 0, sl(0, 16)), R("t8", 0, sl(16, 32)), A.add)
+        tt(C("u1", 8, 16), C("u2", 0, 8), C("u2", 8, 16), A.add)
+        tt(R("NG"), C("u1", 8, 16), R("k3"), A.is_lt)
+        for sd in range(2):
+            tt(C("IJk", 8 * sd, 8 * sd + 8), C("IJ", 8 * sd, 8 * sd + 8), R("NG"), A.mult)
+        tt(R("ONK"), ind(R("IJk"), R("BJ")), R("POS1"), A.is_ge)
+        cp(C("GL", 0, 8), R("CH", 8, sl(0, 8)))
+        tt(R("t2"), R("AM"), R("ONK"), A.mult)
+        ts(C("GL", 8, 136), R("t2"), float(S), A.add)
+        cp(C("GL", 64, 72), R("CH", 0, sl(0, 8)))
+        act(C("MI", 0, 2048), ind(R("Win"), C("GL", 0, 128)))
+        if t == 0:
+            wrap768("M")
+            pick768(R("VD"), 1)
+            for r in range(2):
+                pick768(R("RF", r), 3 - r)
+                cp(R("RL", r), R("RF", r))
+        else:
+            update("W0", "W1", False)
+            ends_out(0)
+        for nm, c0 in (("T1", 128), ("T2", 0)):
+            for b in range(4):
+                for b2 in range(4):
+                    dma("y", C(nm, 128 * b, 128 * b + 128, p=blk(b2)), C("MI", c0, c0 + 2048, p=rows(b, 4)), nm + str(t))
+        arrive("E%d" % t, n_direct, ls)
+        place(lambda k, b: C("L", 0, 60, sl(2 * b, 2 * b + 2), p=blk(k)), lambda b: C(sbf, 0, 120, p=blk(b)),
+              lambda k, b: R(ls, k, sl(0, 120), p=blk(b)))
+        for ch in range(4):
+            for pos in range(7):
+                if ch == 0:
+                    cp(xv("XA", ch, pos), ind(wn, R("L", pos)))
+                else:
+                    act(xv("XA", ch, pos), ind(wn, R("L", 7 * ch + pos)))
+                act(xv("XB", ch, pos), ind(wn, R("L", 28 + 7 * ch + pos)), scale=-1.0)
+            act(R("RR", ch), ind(R("RC"), R("L", 56 + ch)))
+        for ch in range(4):
+            cb = ch % 2
+            scan(R("C", cb, sl(8, 904)), C("XA", 896 * ch, 896 * ch + 896), C("XB", 896 * ch, 896 * ch + 896), 0.0, A.add, A.add)
+            q, qa, qb = C("Qp", 0, 128), C("Qp", 128, 256), C("Qp", 256, 384)
+            tt(q, R("C", cb, sl(14, 904, 7)), R("C", cb, sl(7, 897, 7)), A.subtract)
+            tt(q, q, R("RR", ch), A.mult)
+            ts(qa, q, 0.0625, A.add)
+            ts(qb, q, -0.0625, A.add)
+            for pos in range(7):
+                tt(R("VT", cb, pos), xv("XA", ch, pos), qa, A.is_le)
+                tt(R("VT", cb, 7 + pos), xv("XB", ch, pos), qb, A.is_ge)
+                pv = R("PV", sl(4 * pos + ch, 224, 28))
+                mm(pv, R("VT", cb, pos), R("Gs", 0), True, False)
+                mm(pv, R("VT", cb, 7 + pos), R("Gs", 1), False, True)
+            if ch == 0:
+                if t == 0:
+                    constants_b()
+                tt(R("EQ"), ind(R("T1"), R("RL", t)), R("VI"), A.is_equal)
+                mm(C("Pp", 0, 512), R("Wa"), C("EQ", 0, 512), True, True)
+                mm(C("Pp", 512, 768), R("Wa"), C("EQ", 512, 768), True, True)
+                tt(R("PR"), ind(R("T2"), R("RL", t)), R("EQ"), A.mult)
+            if ch < 3:
+                delta(256 * ch, 256 * ch + 256)
+        act(C("P2", 16, 784), C("Dp", 0, 768))
+        act(R("P"), C("Pp", 0, 768))
+        sv, lv = "SV%d" % t, "LV%d" % t
+        cp(R(sv), C("PV", 0, 224))
+
+        def send_votes(sv=sv, lv=lv, t=t):
+            trs = []
+            for j, k in enumerate(peers):
+                es = topo.engines(core, cores[k])
+                n = len(es) // 4
+                ad = topo.addr(cores[k])
+                trs.append(RemoteDMATransfer(dst_ids=[DstId(rid=ad[0], pnc=ad[1])], dma_engine_mask=sum(1 << e for e in es[n * j:n * j + n]),
+                                             remote_sem=T.sem["aV%d" % t], src=T[sv][:, k], dst=T[lv][:, o]))
+                lsum[0] += n
+            g.remote_dma_fused(trs, local_sem=T.sem.ls)
+        rec("g", send_votes, regs(R(sv)), [], "r")
+        act(C(W, NEG, WW), C(W, 0, S), scale=-1.0)
+        if t == 0:
+            constants_c()
+        tt(R("KW"), R("ONK"), R("POS1"), A.mult)
+        wrap768("P2")
+        pick768(R("ZW"), 2)
+        pick768(R("D1"), 1)
+        ts(R("Zi"), R("ZW"), 4.0, A.mult)
+        ts(R("z2"), R("ZW"), 0.0, A.is_gt)
+        ts(R("SDi"), R("Zi"), 1, A.bitwise_and)
+        ts(R("z1"), R("SDi"), 512.0, A.mult, -1024.0, A.add)
+        ts(R("DD"), R("SDi"), -1024.0, A.mult, 512.0, A.add)
+        tt(R("z1"), R("z1"), R("RF", t), A.add)
+        tt(R("z1"), R("z1"), R("z2"), A.mult)
+        ts(R("TS"), R("z1"), 1024.0, A.add)
+        ts(R("TSf"), R("z1"), 1024.0, A.add)
+        arrive("V%d" % t, sum(len(topo.engines(cores[k], core)) // 4 for k in peers), lv)
+        for u in range(2):
+            n = 0
+            for k in every:
+                for h in range(2):
+                    mm(R("VS", sl(u, 56, 2)), R("Sel", 2 * u + h), R(sv if k == o else lv, k, sl(28 * h, 28 * h + 28)), n == 0, n == 7)
+                    n += 1
+        vs = C("VS", 0, 56)
+        ts(R("Mi"), vs, -32.0, A.add, 1.0 / 65.0, A.mult)
+        ts(C("Wv", 64, 120), vs, 2145.0, A.is_ge)
+        ts(C("t3", 0, 56), R("Mi"), 65.0, A.mult, 33.0, A.add)
+        tt(C("Wv", 0, 56), vs, C("t3", 0, 56), A.is_ge)
+        tt(R("t7"), R("Wv"), R("KW"), A.mult)
+        tt(R("t4"), C("t7", 0, 2, sl(0, 32)), C("t7", 0, 2, sl(32, 64)), A.max)
+        tt(R("t5"), C("t4", 0, 2, sl(0, 16)), C("t4", 0, 2, sl(16, 32)), A.max)
+        tt(R("u2"), C("t5", 0, 2, sl(0, 8)), C("t5", 0, 2, sl(8, 16)), A.max)
+        ts(C("u1", 0, 8), C("u2", 0, 8), 0.0, A.is_equal)
+        tt(C("KK", 8, 16), C("u2", 8, 16), C("u1", 0, 8), A.mult)
+        tt(R("KP"), C("u2", 0, 8), C("KK", 8, 16), A.subtract)
+        for j in range(8):
+            ts(C("E", 0, 4, sl(16 * j, 16 * j + 16)), R("MK0"), C("KP", j, j + 1), A.mult)
+        cp(C("KK", 0, 8), C("u2", 0, 8))
+        for b in range(4):
+            mm(C("KE", 128 * b, 128 * b + 128), R("Hs"), R("E", b), True, True)
+        act(C("CW", 512, 1024), R("KE"), bias=0.5, scale=-1.0)
+        act(C("CW", 0, 512), R("KE"), bias=0.5)
+        per_tie_a()
+        if t == 0:
+            constants_d()
+        else:
+            per_tie_b(1)
+            to_all("Y1", "UY1", "LY1")
+        tt(C("TN", 16, 784), ind(R("CW"), R("TS")), R("P"), A.is_gt)
+        if t == 0:
+            parents()
+            for b in range(4):
+                for b2 in range(4):
+                    dma("ys"[b2 % 2], C("Win", 768 * b, 768 * b + 768, p=rows(b2, 0)), R("N", p=rows(b, 0)), "win1")
+            load_m(1)
+            per_tie_b(0)
+            sources(C("UM0", 32, 80), C("UM0", 80, 128))
+            relay("U0", "UM0", "HU0")
+    sources(C("UX1", 0, 48), C("UX1", 48, 96))
+    to_all("X1", "UX1", "LX1")
+    parents()
+    for b in range(4):
+        for h in range(2):
+            dma("ys"[h], R("YB", p=(64 * h + 16 * b, 64 * h + 16 * b + 16)), R("N", p=(32 * b + 16 * h, 32 * b + 16 * h + 1)), "yb")
+    relay("B", "YB", "HB")
+    arrive("Y1", n_direct, "LY1")
+    place(lambda k, b: R("UL", b, sl(0, 32), p=blk(k)), lambda b: R("UY1", p=blk(b)), lambda k, b: R("LY1", k, p=blk(b)))
+    y_window("W1")
+    arrive("X1", n_direct, "LX1")
+    place(lambda k, b: R("UL", b, sl(32, 128), p=blk(k)), lambda b: R("UX1", p=blk(b)), lambda k, b: R("LX1", k, p=blk(b)))
+    ends_out(1)
+    dma("y", T.yt[:], R("YTf"), "out")
+    dma("y", T.yp[2 * o:2 * o + 2, :], R("YB"), "out")
+    y_gather()
+    arrive("B", n_relay, "LB")
+    for k in peers:
+        dma("s", T.yp[2 * k:2 * k + 2, :], R("LB", k), "out")
+    update("W1", "W0", True)
+
+    need = set(d for op in ops for d in op["deps"] if ops[d]["kind"] == "c")
+    cnt = {q: 0 for q in QS}
+    tok = {}
+    for n, op in enumerate(ops):
+        if n in need:
+            cnt[op["q"]] += 1
+            tok[n] = (QS[op["q"]], cnt[op["q"]])
+        elif op["kind"] in "da":
+            tok[n] = tuple(groups[op["group"]])
+    seen = {q: {} for q in Q}
+    for n, op in enumerate(ops):
+        q = op["q"]
+        if op["kind"] == "a":
+            continue
+        want = {}
+        for d in op["deps"]:
+            if d in tok:
+                want[tok[d][0]] = max(want.get(tok[d][0], 0), tok[d][1])
+        for sname, c in want.items():
+            if seen[q].get(sname, 0) < c:
+                Q[q].wait_ge(T.sem[sname], c)
+                seen[q][sname] = c
+        ins = op["fn"]()
+        if op["kind"] == "d":
+            ins.then_inc(T.sem[groups[op["group"]][0]], 16)
+        elif n in tok:
+            ins.then_inc(T.sem[tok[n][0]], 1)
+    for q in QS:
+        if cnt[q]:
+            g.wait_ge(T.sem[QS[q]], cnt[q])
+    for nm in groups:
+        g.wait_ge(T.sem[groups[nm][0]], groups[nm][1])
+    g.wait_ge(T.sem.ls, lsum[0])

@@ -116,7 +116,7 @@ def rank_program(g, core, T, topo):
         return R(name, sl(a, b), *idx, p=p)
 
     def ind(w, off):
-        return (w[0].indirect(off[0]), w[1] + off[1])
+        return (w[0].indirect(off[0]), w[1] + off[1], True)
 
     def regs(*xs):
         return [r for x in xs if isinstance(x, tuple) for r in x[1]]
@@ -124,7 +124,7 @@ def rank_program(g, core, T, topo):
     def val(x):
         return x[0] if isinstance(x, tuple) else x
 
-    def rec(q, fn, rr, ww, kind="c", group=None):
+    def rec(q, fn, rr, ww, kind="c", group=None, f=1.0):
         n = len(ops)
         deps = set()
         for reg, isw in [(x, False) for x in rr] + [(x, True) for x in ww]:
@@ -141,17 +141,22 @@ def rank_program(g, core, T, topo):
             acc.setdefault(reg[0], []).append((reg, n, False))
         for reg in ww:
             acc.setdefault(reg[0], []).append((reg, n, True))
-        ops.append({"q": q, "fn": fn, "deps": deps, "kind": kind, "group": group})
+        ops.append({"q": q, "fn": fn, "deps": deps, "kind": kind, "group": group,
+                    "dur": max(64, f * len(ww[0][5])) * 0.00092 + (0.06 if f == 1.56 else 0.0) if kind == "c" else 0.1})
+
+    def fac(a, f=1.0):
+        return 1.56 if len(a) > 2 else f
 
     def cp(out, in_):
-        rec("v", lambda: g.vector.tensor_copy(out[0], in_[0]), regs(in_), regs(out))
+        rec("v", lambda: g.vector.tensor_copy(out[0], in_[0]), regs(in_), regs(out), f=fac(in_))
 
     def tt(out, a, b, op):
-        rec("v", lambda: g.vector.tensor_tensor(out[0], a[0], b[0], op), regs(a, b), regs(out))
+        rec("v", lambda: g.vector.tensor_tensor(out[0], a[0], b[0], op), regs(a, b), regs(out),
+            f=fac(a, 1.0 if "psum" in (SCRATCH[a[1][0][0]][0], SCRATCH[b[1][0][0]][0]) else 2.0))
 
     def ts(out, a, s1, op0, s2=None, op1=None):
         if s2 is None:
-            rec("v", lambda: g.vector.tensor_scalar(out[0], a[0], val(s1), None, op0), regs(a, s1), regs(out))
+            rec("v", lambda: g.vector.tensor_scalar(out[0], a[0], val(s1), None, op0), regs(a, s1), regs(out), f=fac(a))
         else:
             rec("v", lambda: g.vector.tensor_scalar(out[0], a[0], val(s1), val(s2), op0, op1), regs(a, s1, s2), regs(out))
 
@@ -166,13 +171,14 @@ def rank_program(g, core, T, topo):
 
     def act(out, in_, bias=0.0, scale=1.0):
         rec("s", lambda: g.scalar.activation(out[0], in_[0], AF.Identity, bias=val(bias), scale=val(scale)),
-            regs(in_, bias, scale), regs(out))
+            regs(in_, bias, scale), regs(out), f=fac(in_))
 
     def mm(out, l, r, st, sp):
-        rec("t", lambda: g.tensor.matmul(out[0], l[0], r[0], st, sp), regs(l, r), regs(out))
+        rec("t", lambda: g.tensor.matmul(out[0], l[0], r[0], st, sp), regs(l, r), regs(out),
+            f=4.0 if SCRATCH[l[1][0][0]][2] == F else 1.0)
 
     def iota(out, pat, base):
-        rec("g", lambda: g.iota(out[0], pat, base, 0, allow_small_or_imprecise_dtypes=True), [], regs(out))
+        rec("g", lambda: g.iota(out[0], pat, base, 0, allow_small_or_imprecise_dtypes=True), [], regs(out), f=3.0)
 
     def dma(q, out, in_, group, also=None):
         if group not in groups:
@@ -187,7 +193,7 @@ def rank_program(g, core, T, topo):
     def send(name, src, dsts):
         def fn():
             lsum[0] += bcast(g, T, topo, core, src[0], dsts, name)
-        rec("g", fn, regs(src), [], "r")
+        rec("g", fn, regs(src), [], "r", name)
 
     def to_all(name, src, land):
         send(name, R(src), [(cores[k], T[land][:, o]) for k in peers])
@@ -301,7 +307,7 @@ def rank_program(g, core, T, topo):
 
     def constants_a():
         ts(R("TIE"), cn(i_tie, 128), cf(16), A.add)
-        rec("v", lambda: g.vector.reciprocal(T.RC[:], cn(i_rc, 16)[0]), regs(cn(i_rc, 16)), regs(R("RC")))
+        rec("v", lambda: g.vector.reciprocal(T.RC[:], cn(i_rc, 16)[0]), regs(cn(i_rc, 16)), regs(R("RC")), f=18.0)
         ms(C("MI", 2048, 2176), -1.0)
         ms(C("W0", ZC, NEG), 0.0)
         ms(R("C", sl(0, 2), sl(0, 8)), 0.0)
@@ -341,10 +347,13 @@ def rank_program(g, core, T, topo):
         for b, c0, c1 in BLOCKS:
             act(C("Yg", 768 * b + 16 * c0, 768 * b + 16 * c1), ind(R("Yw"), R("UL", b, sl(80 + c0, 80 + c1))))
 
-    def update(W, dst, store):
+    def update(W, dst, store, between):
         for b, c0, c1 in BLOCKS:
             x0, x1 = 768 * b + 16 * c0, 768 * b + 16 * c1
             tt(C(dst, x0, x1), ind(R(W), R("UL", b, sl(32 + c0, 32 + c1))), C("Yg", x0, x1), A.add)
+            for x in between[:4]:
+                x()
+            del between[:4]
             if store:
                 dma("y", T.yf[:, x0:x1], C(dst, x0, x1), "out")
 
@@ -401,6 +410,17 @@ def rank_program(g, core, T, topo):
         mm(C("Dp", c0, c1), R("Wc"), C("PR", c0, c1), False, False)
         mm(C("Dp", c0, c1), R("Wd"), C("M", 16 + c0, 16 + c1), False, True)
 
+    def limits(ch):
+        c0 = 256 * (ch % 2)
+        qa, qb = C("Qp", c0, c0 + 128), C("Qp", c0 + 128, c0 + 256)
+        cs = sl(896 * ch, 896 * ch + 896)
+        return [lambda: scan(R("C", ch % 2, sl(8, 904)), R("XA", cs), R("XB", cs), 0.0, A.add, A.add),
+                lambda: tt(qa, R("C", ch % 2, sl(14, 904, 7)), R("C", ch % 2, sl(7, 897, 7)), A.subtract),
+                lambda: tt(qa, qa, R("RR", ch), A.mult),
+                lambda: ts(qb, qa, -0.0625, A.add),
+                lambda: ts(qa, qa, 0.0625, A.add)], qa, qb
+
+    first = len(ops)
     for t in range(2):
         W = "W%d" % t
         wn = C(W, 0, NEG)
@@ -447,30 +467,33 @@ def rank_program(g, core, T, topo):
         send("E%d" % t, C(sbf, 0, 120), [(cores[k], T[ls][:, o, 0:120]) for k in peers])
         if t == 0:
             load_m(0)
-        tt(R("t1"), ind(C("CHf", 24, 272), R("VL")), R("TIE"), A.not_equal)
-        ts(R("k3"), ks, 65.0, A.is_lt)
-        tt(R("t2"), R("t1"), R("ON"), A.mult)
-        tt(R("t3"), C("t2", 0, 64), C("t2", 64, 128), A.add)
-        tt(R("t8", 0), C("t3", 0, 32), C("t3", 32, 64), A.add)
-        tt(R("u2"), R("t8", 0, sl(0, 16)), R("t8", 0, sl(16, 32)), A.add)
-        tt(C("u1", 8, 16), C("u2", 0, 8), C("u2", 8, 16), A.add)
-        tt(R("NG"), C("u1", 8, 16), R("k3"), A.is_lt)
-        for sd in range(2):
-            tt(C("IJk", 8 * sd, 8 * sd + 8), C("IJ", 8 * sd, 8 * sd + 8), R("NG"), A.mult)
-        tt(R("ONK"), ind(R("IJk"), R("BJ")), R("POS1"), A.is_ge)
-        cp(C("GL", 0, 8), R("CH", 8, sl(0, 8)))
-        tt(R("t2"), R("AM"), R("ONK"), A.mult)
-        ts(C("GL", 8, 136), R("t2"), float(S), A.add)
-        cp(C("GL", 64, 72), R("CH", 0, sl(0, 8)))
-        act(C("MI", 0, 2048), ind(R("Win"), C("GL", 0, 128)))
+        kept = [
+            lambda: tt(R("t1"), ind(C("CHf", 24, 272), R("VL")), R("TIE"), A.not_equal),
+            lambda: ts(R("k3"), ks, 65.0, A.is_lt),
+            lambda: tt(R("t2"), R("t1"), R("ON"), A.mult),
+            lambda: tt(R("t3"), C("t2", 0, 64), C("t2", 64, 128), A.add),
+            lambda: tt(R("t8", 0), C("t3", 0, 32), C("t3", 32, 64), A.add),
+            lambda: tt(R("u2"), R("t8", 0, sl(0, 16)), R("t8", 0, sl(16, 32)), A.add),
+            lambda: tt(C("u1", 8, 16), C("u2", 0, 8), C("u2", 8, 16), A.add),
+            lambda: tt(R("NG"), C("u1", 8, 16), R("k3"), A.is_lt),
+            lambda: tt(C("IJk", 0, 8), C("IJ", 0, 8), R("NG"), A.mult),
+            lambda: tt(C("IJk", 8, 16), C("IJ", 8, 16), R("NG"), A.mult),
+            lambda: tt(R("ONK"), ind(R("IJk"), R("BJ")), R("POS1"), A.is_ge),
+            lambda: cp(C("GL", 0, 8), R("CH", 8, sl(0, 8))),
+            lambda: tt(R("t2"), R("AM"), R("ONK"), A.mult),
+            lambda: ts(C("GL", 8, 136), R("t2"), float(S), A.add),
+            lambda: cp(C("GL", 64, 72), R("CH", 0, sl(0, 8))),
+            lambda: act(C("MI", 0, 2048), ind(R("Win"), C("GL", 0, 128)))]
         if t == 0:
+            for x in kept:
+                x()
             wrap768("M")
             pick768(R("VD"), 1)
             for r in range(2):
                 pick768(R("RF", r), 3 - r)
-                cp(R("RL", r), R("RF", r))
+                pick768(R("RL", r), 3 - r)
         else:
-            update("W0", "W1", False)
+            update("W0", "W1", False, kept)
             ends_out(0)
         for nm, c0 in (("T1", 128), ("T2", 0)):
             for b in range(4):
@@ -487,17 +510,16 @@ def rank_program(g, core, T, topo):
                     act(xv("XA", ch, pos), ind(wn, R("L", 7 * ch + pos)))
                 act(xv("XB", ch, pos), ind(wn, R("L", 28 + 7 * ch + pos)), scale=-1.0)
             act(R("RR", ch), ind(R("RC"), R("L", 56 + ch)))
+        for x in limits(0)[0]:
+            x()
         for ch in range(4):
             cb = ch % 2
-            scan(R("C", cb, sl(8, 904)), C("XA", 896 * ch, 896 * ch + 896), C("XB", 896 * ch, 896 * ch + 896), 0.0, A.add, A.add)
-            q, qa, qb = C("Qp", 0, 128), C("Qp", 128, 256), C("Qp", 256, 384)
-            tt(q, R("C", cb, sl(14, 904, 7)), R("C", cb, sl(7, 897, 7)), A.subtract)
-            tt(q, q, R("RR", ch), A.mult)
-            ts(qa, q, 0.0625, A.add)
-            ts(qb, q, -0.0625, A.add)
+            qa, qb = limits(ch)[1:]
             for pos in range(7):
-                tt(R("VT", cb, pos), xv("XA", ch, pos), qa, A.is_le)
+                if 0 < ch < 3 and pos >= 2:
+                    limits(ch + 1)[0][pos - 2]()
                 tt(R("VT", cb, 7 + pos), xv("XB", ch, pos), qb, A.is_ge)
+                tt(R("VT", cb, pos), xv("XA", ch, pos), qa, A.is_le)
                 pv = R("PV", sl(4 * pos + ch, 224, 28))
                 mm(pv, R("VT", cb, pos), R("Gs", 0), True, False)
                 mm(pv, R("VT", cb, 7 + pos), R("Gs", 1), False, True)
@@ -508,8 +530,11 @@ def rank_program(g, core, T, topo):
                 mm(C("Pp", 0, 512), R("Wa"), C("EQ", 0, 512), True, True)
                 mm(C("Pp", 512, 768), R("Wa"), C("EQ", 512, 768), True, True)
                 tt(R("PR"), ind(R("T2"), R("RL", t)), R("EQ"), A.mult)
-            if ch < 3:
-                delta(256 * ch, 256 * ch + 256)
+                for x in limits(1)[0]:
+                    x()
+                delta(0, 256)
+            if ch < 2:
+                delta(256 * ch + 256, 256 * ch + 512)
         act(C("P2", 16, 784), C("Dp", 0, 768))
         act(R("P"), C("Pp", 0, 768))
         sv, lv = "SV%d" % t, "LV%d" % t
@@ -525,11 +550,12 @@ def rank_program(g, core, T, topo):
                                              remote_sem=T.sem["aV%d" % t], src=T[sv][:, k], dst=T[lv][:, o]))
                 lsum[0] += n
             g.remote_dma_fused(trs, local_sem=T.sem.ls)
-        rec("g", send_votes, regs(R(sv)), [], "r")
+        rec("g", send_votes, regs(R(sv)), [], "r", "V%d" % t)
         act(C(W, NEG, WW), C(W, 0, S), scale=-1.0)
         if t == 0:
             constants_c()
         tt(R("KW"), R("ONK"), R("POS1"), A.mult)
+        ts(C("KW", 0, 64), C("KW", 0, 64), 16.0, A.mult)
         wrap768("P2")
         pick768(R("ZW"), 2)
         pick768(R("D1"), 1)
@@ -558,16 +584,15 @@ def rank_program(g, core, T, topo):
         tt(R("t4"), C("t7", 0, 2, sl(0, 32)), C("t7", 0, 2, sl(32, 64)), A.max)
         tt(R("t5"), C("t4", 0, 2, sl(0, 16)), C("t4", 0, 2, sl(16, 32)), A.max)
         tt(R("u2"), C("t5", 0, 2, sl(0, 8)), C("t5", 0, 2, sl(8, 16)), A.max)
-        ts(C("u1", 0, 8), C("u2", 0, 8), 0.0, A.is_equal)
-        tt(C("KK", 8, 16), C("u2", 8, 16), C("u1", 0, 8), A.mult)
-        tt(R("KP"), C("u2", 0, 8), C("KK", 8, 16), A.subtract)
+        tt(R("KP"), C("u2", 0, 8), C("u2", 8, 16), A.subtract)
         for j in range(8):
             ts(C("E", 0, 4, sl(16 * j, 16 * j + 16)), R("MK0"), C("KP", j, j + 1), A.mult)
-        cp(C("KK", 0, 8), C("u2", 0, 8))
+        ts(C("KK", 0, 8), C("u2", 0, 8), 0.0625, A.mult)
+        ts(C("KK", 8, 16), R("KP"), -1.0, A.mult, 0.0, A.max)
         for b in range(4):
             mm(C("KE", 128 * b, 128 * b + 128), R("Hs"), R("E", b), True, True)
         act(C("CW", 512, 1024), R("KE"), bias=0.5, scale=-1.0)
-        act(C("CW", 0, 512), R("KE"), bias=0.5)
+        act(C("CW", 0, 512), R("KE"), bias=0.5, scale=0.0625)
         per_tie_a()
         if t == 0:
             constants_d()
@@ -577,9 +602,8 @@ def rank_program(g, core, T, topo):
         tt(C("TN", 16, 784), ind(R("CW"), R("TS")), R("P"), A.is_gt)
         if t == 0:
             parents()
-            for b in range(4):
-                for b2 in range(4):
-                    dma("ys"[b2 % 2], C("Win", 768 * b, 768 * b + 768, p=rows(b2, 0)), R("N", p=rows(b, 0)), "win1")
+            for z in range(8):
+                dma("ys"[z % 2], C("Win", 0, S, p=(16 * z, 16 * z + 1)), R("N", p=(16 * (z % 2), 128, 32)), "win1")
             load_m(1)
             per_tie_b(0)
             sources(C("UM0", 32, 80), C("UM0", 80, 128))
@@ -603,19 +627,69 @@ def rank_program(g, core, T, topo):
     arrive("B", n_relay, "LB")
     for k in peers:
         dma("s", T.yp[2 * k:2 * k + 2, :], R("LB", k), "out")
-    update("W1", "W0", True)
+    update("W1", "W0", True, [])
+
+    pre = [dict() for op in ops]
+    last, members, sent = {}, {}, {}
+    for n, op in enumerate(ops):
+        if op["kind"] == "d":
+            members.setdefault(op["group"], []).append(n)
+        if op["kind"] == "r":
+            sent[op["group"]] = n
+    for n, op in enumerate(ops):
+        for d in op["deps"]:
+            if ops[d]["kind"] == "d":
+                for m in members[ops[d]["group"]]:
+                    pre[n][m] = 2.2
+            else:
+                pre[n][d] = 0.15
+        if op["kind"] == "a":
+            nm = op["group"]
+            pre[n][sent[nm] if nm in sent else sent["h" + nm]] = 3.0 if nm in sent else 6.0
+    soft = [all(ops[d]["kind"] == "c" for d in op["deps"]) and op["kind"] == "c" and n >= first for n, op in enumerate(ops)]
+    todo = {}
+    for n, op in enumerate(ops):
+        todo.setdefault(op["q"], []).append(n)
+    end, free, order = {}, {q: 0.0 for q in todo}, []
+
+    def ready(n):
+        if any(d not in end for d in pre[n]):
+            return None
+        return max([end[d] + pre[n][d] for d in pre[n]] + [0.0])
+    while len(order) < len(ops):
+        best = None
+        for q in todo:
+            if not todo[q]:
+                continue
+            head = ready(todo[q][0])
+            x = None if head is None else (max(head, free[q]), todo[q][0])
+            if q in "vs" and (head is None or head > free[q]):
+                for m in todo[q][1:30]:
+                    r = ready(m) if soft[m] else None
+                    if r is not None and max(r, free[q]) + ops[m]["dur"] <= (free[q] + 0.15 if head is None else head + 0.05):
+                        x = (max(r, free[q]), m)
+                        break
+            if x is not None and (best is None or x < best):
+                best = x
+        n = best[1]
+        q = ops[n]["q"]
+        end[n] = free[q] = best[0] + ops[n]["dur"]
+        todo[q].remove(n)
+        order.append(n)
 
     need = set(d for op in ops for d in op["deps"] if ops[d]["kind"] == "c")
     cnt = {q: 0 for q in QS}
     tok = {}
-    for n, op in enumerate(ops):
+    for n in order:
+        op = ops[n]
         if n in need:
             cnt[op["q"]] += 1
             tok[n] = (QS[op["q"]], cnt[op["q"]])
         elif op["kind"] in "da":
             tok[n] = tuple(groups[op["group"]])
     seen = {q: {} for q in Q}
-    for n, op in enumerate(ops):
+    for n in order:
+        op = ops[n]
         q = op["q"]
         if op["kind"] == "a":
             continue

@@ -6,6 +6,10 @@ S = 3072
 ZC = S
 NEG = S + 64
 WW = NEG + S
+NPE = (8, 7, 7, 8)
+CUT = ((7, 5, 0, 0), (7, 2, 0, 0))
+EARLY = 2
+OFS = 1032.0
 F, B16, H16, I32, U16 = "float32", "bfloat16", "float16", "int32", "uint16"
 
 
@@ -14,40 +18,43 @@ def sb(shape, d=F):
 
 
 SCRATCH = {
-    "W0": sb([WW]), "W1": sb([WW]), "XA": sb([3584]), "XB": sb([3584]), "C": sb([2, 904]),
-    "VT": sb([2, 14, 128], B16), "RR": sb([4, 128]), "Yg": sb([S]), "Yw": sb([1040]), "CW": sb([1040]),
-    "Win": sb([3088]), "X": sb([2, 160]), "TT": sb([2, 288]), "MI": sb([2176]), "T1": sb([512]), "T2": sb([512]),
-    "EQ": sb([768], B16), "PR": sb([768]), "P": sb([768]), "P2": sb([800]), "M": sb([800]), "VI": sb([768]),
-    "N": sb([768]), "TN": sb([800]), "TW": sb([1568]),
-    "Di": sb([768], I32), "Df": sb([768]), "tiei": sb([4, 32], I32), "ENDS": sb([4, 8]), "CH": sb([16, 16], U16),
-    "CHf": sb([272]), "AA": sb([512]), "NE": sb([512]), "ONES": sb([512]), "KS": sb([512]),
-    "IJ": sb([16], I32), "IJk": sb([16]), "k1": sb([8]), "k2": sb([8]), "k3": sb([8]),
-    "ON": sb([128]), "ONK": sb([128]), "AM": sb([128]), "LF": sb([144]), "t1": sb([128]), "t2": sb([128]),
-    "t3": sb([64]), "t4": sb([2, 32]), "t5": sb([2, 16]), "KK": sb([16]), "KP": sb([8]), "KW": sb([128]),
-    "t6": sb([2, 128]), "t7": sb([2, 64]), "t8": sb([2, 32]), "t9": sb([2, 16]), "PK2": sb([16]), "NG": sb([8]),
-    "u1": sb([16]), "u2": sb([16]), "Mi": sb([56], I32), "Wv": sb([128]),
-    "GL": sb([136], U16), "RL": sb([2, 48], U16), "RF": sb([2, 48]), "ZW": sb([48]), "Zi": sb([48], I32),
-    "SDi": sb([48], I32), "z1": sb([48]), "z2": sb([48]), "TSf": sb([48]), "TS": sb([48], U16), "DD": sb([48]),
-    "IXf": sb([48]), "VD": sb([48]), "D1": sb([48]), "E": sb([4, 128], B16),
+    "W0": sb([WW]), "W1": sb([WW]), "XX": sb([7168]), "VT": sb([4, 14, 128], B16), "RR": sb([4, 128]),
+    "Yg": sb([S]), "Yw": sb([1536]), "CW": sb([1536]), "Win": sb([S]), "X": sb([2, 160]), "TT": sb([4, 288]),
+    "XT": sb([288]), "TP": sb([256]), "T12": sb([1024]), "n1": sb([128]),
+    "EQ": sb([768], B16), "PR": sb([768]), "P": sb([800], B16), "P2": sb([800]), "M": sb([800]), "VI": sb([768]),
+    "N": sb([768]), "TN": sb([800], B16), "TW": sb([1568]), "TB": sb([1568], B16),
+    "Di": sb([384], I32), "Df": sb([384]), "tiei": sb([4, 32], I32), "ENDS": sb([4, 8]), "CH": sb([16, 16], U16),
+    "CH0": sb([272]), "CH1": sb([272]), "AA": sb([512]), "NE": sb([512]), "INC": sb([512]), "KS": sb([512]),
+    "IJ": sb([16], I32), "ON": sb([128]), "AM": sb([128]), "LF": sb([144]), "POSX": sb([128]), "q3": sb([2, 8, 16]),
+    "ON2": sb([128]), "POS2": sb([128]), "CODE": sb([128]), "CODW": sb([128]), "TIE": sb([128]), "RS16": sb([128]),
+    "RS8": sb([128]), "t1": sb([128]), "t2": sb([128]), "t3": sb([32]), "t4": sb([128]), "t5": sb([128]), "t6": sb([256]),
+    "t7": sb([256]), "KW": sb([128]), "Si": sb([56], I32), "Wv": sb([16, 8], I32), "KM": sb([128]),
+    "KP": sb([8]), "cm": sb([8]), "u1": sb([16]), "u2": sb([16]), "u3": sb([32]),
+    "RM": sb([144]), "Ri": sb([192], I32), "RF": sb([96]), "RL": sb([96], U16),
+    "NB": sb([240]), "BV": sb([144]), "ZV": sb([96]), "TS": sb([48], U16), "TK": sb([144]),
+    "IX": sb([144]), "E": sb([8, 4, 16], B16),
     "LS0": sb([4, 128], U16), "LS1": sb([4, 128], U16), "SB0": sb([128], U16), "SB1": sb([128], U16),
-    "L": sb([60, 8], U16),
+    "L": sb([480], U16),
     "SV0": sb([4, 56], H16), "SV1": sb([4, 56], H16), "LV0": sb([4, 56], H16), "LV1": sb([4, 56], H16),
-    "UM0": sb([128], U16), "LU0": sb([4, 128], U16), "HU0": sb([128], U16),
-    "UY1": sb([32], U16), "LY1": sb([4, 32], U16), "UX1": sb([96], U16), "LX1": sb([4, 96], U16),
+    "UY0": sb([16], U16), "LY0": sb([4, 16], U16), "UX0": sb([112], U16), "LX0": sb([4, 112], U16), "HX0": sb([112], U16),
+    "UY1": sb([16], U16), "LY1": sb([4, 16], U16), "UX1": sb([112], U16), "LX1": sb([4, 112], U16),
     "UL": sb([4, 128], U16), "YTf": sb([4, 4, 8]),
-    "YB": sb([48]), "HB": sb([48]), "LB": sb([4, 48]),
-    "pi": sb([1], I32), "ci": sb([8], I32), "cf": sb([24]), "cn": sb([728]),
-    "PK": sb([4], U16), "WK": sb([4, 4], U16), "AL": sb([32], U16), "BL": sb([32], U16), "BJ": sb([8], U16),
-    "VL": sb([8], U16), "SL": sb([16], U16), "POS1": sb([128]), "TIE": sb([128]), "MK0": sb([4, 16]), "Hs": sb([128], B16),
-    "Sel": sb([4, 128], H16), "Gs": sb([2, 8], B16), "Gf": sb([8]), "Wa": sb([128], B16),
-    "Wb": sb([128], B16), "Wc": sb([128]), "Wd": sb([128]), "RC": sb([16]),
-    "Qp": ("psum", [128, 512], F), "PV": ("psum", [128, 512], F), "VS": ("psum", [128, 512], F),
-    "KE": ("psum", [128, 512], F), "Pp": ("psum", [128, 1024], F), "Dp": ("psum", [128, 1024], F),
+    "YB": sb([48]), "UB": sb([48], U16), "HB": sb([48], U16), "LB": sb([4, 48], U16),
+    "ci": sb([16], I32), "cf": sb([40]), "cn": sb([896]),
+    "PK": sb([4], U16), "WM": sb([10], U16), "WP": sb([12], U16), "WT": sb([10], U16), "AL": sb([32], U16),
+    "BL": sb([32], U16), "BJ": sb([8], U16), "VL": sb([8], U16), "SL": sb([16], U16), "LL": sb([6, 8], U16),
+    "XL": sb([16], U16), "MK0": sb([4, 16]), "Hs": sb([128], B16), "Sel": sb([4, 128], H16), "Gs": sb([2, 8], B16),
+    "Gf": sb([8]), "Wa": sb([128], B16), "Wc": sb([128]), "ID": sb([128]), "RC": sb([64]),
+    "Qp": ("psum", [128, 1024], F), "PV": ("psum", [128, 512], F), "VS": ("psum", [128, 512], F),
+    "KE": ("psum", [128, 1024], F), "Dp": ("psum", [128, 1024], F),
 }
 DSEMS = ["d%d" % k for k in range(20)]
-ARR = ["E0", "E1", "V0", "V1", "U0", "Y1", "X1", "B", "hU0", "hB"]
+ARR = ["E0", "E1", "V0", "V1", "Y0", "X0", "Y1", "X1", "B", "hX0", "hB"]
 SEMAPHORES = ["sg", "sv", "ss", "st", "ls"] + DSEMS + ["a" + k for k in ARR]
-BLOCKS = [(0, 0, 8), (0, 8, 24), (0, 24, 48), (1, 0, 24), (1, 24, 48), (2, 0, 24), (2, 24, 48), (3, 0, 24), (3, 24, 40), (3, 40, 48)]
+BLOCKS = [[(0, 0, 8), (0, 8, 16), (0, 16, 24), (0, 24, 36), (0, 36, 48)] + [(b, c, c + 24) for b in (1, 2, 3) for c in (0, 24)],
+          [(0, 0, 8), (0, 8, 24), (0, 24, 48), (1, 0, 24), (1, 24, 48), (2, 0, 24), (2, 24, 48), (3, 0, 24), (3, 24, 40), (3, 40, 48)]]
+CYC, PEC, HOP, DMA, FAR = 0.00085, 0.0005, 0.15, 2.0, 3.2
+SLOW = {"fl": 8.0, "m0": 0.8, "T0": 1.2, "T1": 1.2, "win0": 0.8}
 
 
 def helpers(T, topo):
@@ -78,6 +85,47 @@ def bcast(g, T, topo, me, src, dsts, name):
     return neng(topo, me, cs)
 
 
+def schedule(ops, pre):
+    n_ops = len(ops)
+    post = [dict() for op in ops]
+    for n in range(n_ops):
+        for d in pre[n]:
+            post[d][n] = pre[n][d]
+
+    def lay(before, after, rank):
+        left = [len(x) for x in before]
+        start, busy = [0.0] * n_ops, {}
+        heap = sorted([(rank[n], n) for n in range(n_ops) if left[n] == 0], reverse=True)
+        while heap:
+            n = heap.pop()[1]
+            at = max([start[d] + ops[d]["dur"] + before[n][d] for d in before[n]] + [0.0])
+            row = busy.setdefault(ops[n]["q"], [])
+            k = int(np.searchsorted([e for _, e in row], at, "right"))
+            while k < len(row) and row[k][0] < at + ops[n]["dur"] - 1e-9:
+                at = max(at, row[k][1])
+                k += 1
+            row.insert(k, (at, at + ops[n]["dur"]))
+            start[n] = at
+            for m in after[n]:
+                left[m] -= 1
+                if left[m] == 0:
+                    heap.append((rank[m], m))
+                    heap.sort(reverse=True)
+        return start
+    start = lay(pre, post, [float(n) for n in range(n_ops)])
+    best, rank = None, [0.0] * n_ops
+    for n in sorted(range(n_ops), key=lambda n: -start[n] - ops[n]["dur"]):
+        rank[n] = min([rank[m] - post[n][m] for m in post[n]] + [0.0]) - ops[n]["dur"]
+    for turn in range(2):
+        start = lay(pre, post, rank)
+        span = max(start[n] + ops[n]["dur"] for n in range(n_ops))
+        if best is None or span < best[0]:
+            best = (span, start)
+        back = lay(post, pre, [-start[n] - ops[n]["dur"] for n in range(n_ops)])
+        rank = [-back[n] - ops[n]["dur"] for n in range(n_ops)]
+    return sorted(range(n_ops), key=lambda n: (best[1][n], n))
+
+
 def rank_program(g, core, T, topo):
     o = T.rank_of(core)
     cores = list(T.cores)
@@ -86,7 +134,7 @@ def rank_program(g, core, T, topo):
         if core in hl:
             r = hl.index(core)
             tot = 0
-            for nm, hb, lb in (("U0", "HU0", "LU0"), ("B", "HB", "LB")):
+            for nm, hb, lb in (("X0", "HX0", "LX0"), ("B", "HB", "LB")):
                 g.wait_ge(T.sem["ah" + nm], neng(topo, cores[r], [core]))
                 tot += bcast(g, T, topo, core, T[hb][:], [(cores[k], T[lb][:, r]) for k in range(4) if k != r], nm)
             g.wait_ge(T.sem.ls, tot)
@@ -97,7 +145,7 @@ def rank_program(g, core, T, topo):
     QS = {"g": "sg", "v": "sv", "s": "ss", "t": "st"}
     A = AluOpType
     AF = ActivationFunctionType
-    ops, acc, groups, lsum = [], {}, {}, [0]
+    ops, acc, groups, lsum, bank, line = [], {}, {}, [0], {}, [None]
     sl = slice
 
     def R(name, *idx, p=(0, 128, 1)):
@@ -126,7 +174,7 @@ def rank_program(g, core, T, topo):
 
     def rec(q, fn, rr, ww, kind="c", group=None, f=1.0):
         n = len(ops)
-        deps = set()
+        deps, after = set(), set()
         for reg, isw in [(x, False) for x in rr] + [(x, True) for x in ww]:
             ps = SCRATCH[reg[0]][0] == "psum"
             for (r2, m, w2) in acc.get(reg[0], []):
@@ -137,18 +185,37 @@ def rank_program(g, core, T, topo):
                             deps.add(m)
                     elif (w2 or isw or ps) and not (kind == "d" and o2["kind"] == "d" and o2["group"] == group):
                         deps.add(m)
+        if q == "t":
+            key = (ww[0][0], ww[0][3])
+            if key in bank:
+                after.add(bank[key])
+            bank[key] = n
+        if line[0] and q in line[0]:
+            if (line[0], q) in bank:
+                after.add(bank[(line[0], q)])
+            bank[(line[0], q)] = n
         for reg in rr:
             acc.setdefault(reg[0], []).append((reg, n, False))
         for reg in ww:
             acc.setdefault(reg[0], []).append((reg, n, True))
-        ops.append({"q": q, "fn": fn, "deps": deps, "kind": kind, "group": group,
-                    "dur": max(64, f * len(ww[0][5])) * 0.00092 + (0.06 if f == 1.56 else 0.0) if kind == "c" else 0.1})
+        dur = 0.08
+        if kind == "c":
+            e = len(ww[0][5])
+            dur = f * e * CYC + 0.06 if f == 1.56 else max(64, f * e) * CYC
+            if q == "t":
+                dur = f * max(64, e) * PEC
+            if q == "g":
+                dur = 0.13 + 2 * e * CYC
+        ops.append({"q": q, "fn": fn, "deps": deps, "after": after, "kind": kind, "group": group, "dur": dur})
+
+    def short(*xs):
+        return all(SCRATCH[x[1][0][0]][2] in (B16, H16, U16) for x in xs)
 
     def fac(a, f=1.0):
         return 1.56 if len(a) > 2 else f
 
     def cp(out, in_):
-        rec("v", lambda: g.vector.tensor_copy(out[0], in_[0]), regs(in_), regs(out), f=fac(in_))
+        rec("v", lambda: g.vector.tensor_copy(out[0], in_[0]), regs(in_), regs(out), f=fac(in_, 0.5 if short(out, in_) else 1.0))
 
     def tt(out, a, b, op):
         rec("v", lambda: g.vector.tensor_tensor(out[0], a[0], b[0], op), regs(a, b), regs(out),
@@ -164,10 +231,10 @@ def rank_program(g, core, T, topo):
         rec("v", lambda: g.vector.tensor_tensor_scan(out[0], d0[0], d1[0], init, op0, op1), regs(d0, d1), regs(out))
 
     def tr(out, in_):
-        rec("v", lambda: g.vector.transpose(out[0], in_[0]), regs(in_), regs(out))
+        rec("v", lambda: g.vector.transpose(out[0], in_[0]), regs(in_), regs(out), f=0.5 if short(out, in_) else 1.0)
 
     def ms(out, c):
-        rec("v", lambda: g.vector.memset(out[0], c), [], regs(out))
+        rec("v", lambda: g.vector.memset(out[0], c), [], regs(out), f=0.5 if short(out) else 1.0)
 
     def act(out, in_, bias=0.0, scale=1.0):
         rec("s", lambda: g.scalar.activation(out[0], in_[0], AF.Identity, bias=val(bias), scale=val(scale)),
@@ -178,7 +245,7 @@ def rank_program(g, core, T, topo):
             f=4.0 if SCRATCH[l[1][0][0]][2] == F else 1.0)
 
     def iota(out, pat, base):
-        rec("g", lambda: g.iota(out[0], pat, base, 0, allow_small_or_imprecise_dtypes=True), [], regs(out), f=3.0)
+        rec("g", lambda: g.iota(out[0], pat, base, 0, allow_small_or_imprecise_dtypes=True), [], regs(out))
 
     def dma(q, out, in_, group, also=None):
         if group not in groups:
@@ -207,8 +274,23 @@ def rank_program(g, core, T, topo):
     def cf(k):
         return C("cf", k, k + 1)
 
-    def cn(a, n):
-        return C("cn", a, a + n)
+    used = [160]
+
+    def pattern(pat, base):
+        n = int(np.prod([c for _, c in pat]))
+        x = C("cn", used[0], used[0] + n)
+        used[0] += n
+        iota(x, pat, base)
+        return x
+
+    def bus(name, a, n=1):
+        return C(name, 48 * a, 48 * (a + n))
+
+    def xx(ch, a, n=1):
+        return C("XX", 128 * (14 * ch + a), 128 * (14 * ch + a + n))
+
+    def lst(ch, a, n=1):
+        return C("L", 8 * (15 * ch + a), 8 * (15 * ch + a + n))
 
     def blk(b):
         return (32 * b, 32 * b + 32)
@@ -216,329 +298,299 @@ def rank_program(g, core, T, topo):
     def rows(b, r):
         return (32 * b + r, 32 * b + 32, 16)
 
-    def wrap768(src):
-        tr(C("TW", 0, 768), C(src, 16, 784))
-        tr(C("TW", 768, 1568), C(src, 0, 800))
-
-    def pick768(out, row):
-        cp(out, ind(R("TW"), R("WK", row, sl(0, 3))))
+    def wrap768(src, dst, step=384):
+        for c0 in range(0, 768, step):
+            tr(C(dst, c0, c0 + step), C(src, 16 + c0, 16 + step + c0))
+        for c0 in range(0, 768, step):
+            c1 = c0 + step if c0 + step < 768 else 800
+            tr(C(dst, 768 + c0, 768 + c1), C(src, c0, c1))
 
     def place(dst, own, land):
-        for k in every:
-            for b in range(4):
+        for b in range(4):
+            for k in every:
                 cp(dst(k, b), own(b) if k == o else land(k, b))
 
-    dma("y", R("Di", p=(0, 8)), T.par[2 * o:2 * o + 2, :], "in")
-    dma("s", R("Di", p=(8, 16)), T.res[2 * o:2 * o + 2, 0:S], "in")
-    dma("s", R("Di", p=(16, 24)), T.res[2 * o:2 * o + 2, S:2 * S], "in")
+    dma("y", R("Di", p=(0, 16)), T.par[2 * o:2 * o + 2, :], "in")
+    dma("s", R("Di", p=(16, 32)), T.res[2 * o:2 * o + 2, 0:S], "in")
     dma("y", R("tiei"), T.tie[:], "tie")
-    rec("g", lambda: g.iota(T.pi[:], [[1, 1]], 0, 1), [], regs(R("pi")))
-    iota(C("Win", 0, 772), [[1, 772]], 0)
-    i_wk, i_al, i_bl, i_bj, i_rc, i_tie, i_g, i_sel, i_m, i_mk, i_vl = 160, 176, 208, 240, 248, 264, 392, 400, 528, 656, 720
-    iota(cn(i_g, 8), [[1, 8]], 0)
-    for sd in range(2):
-        iota(cn(16 + 56 * sd, 56), [[2, 4], [8, 7], [1, 2]], 64 * sd)
-    iota(cn(128, 32), [[0, 4], [1, 8]], 128)
-    iota(cn(i_al, 32), [[1, 8], [-32, 4]], 112)
-    iota(cn(i_bl, 32), [[1, 8], [0, 4]], 240)
-    iota(cn(i_bj, 8), [[8, 2], [0, 4]], 0)
-    iota(cn(i_vl, 8), [[32, 8]], 0)
-    iota(cn(i_wk, 16), [[1, 4], [256, 4]], 0)
-    iota(cn(i_tie, 128), [[0, 16], [16, 8]], 0)
-    iota(cn(i_rc, 16), [[1, 16]], 1)
-    iota(R("POS1"), [[0, 2], [1, 8], [0, 8]], 1)
-    iota(R("VI"), [[1, 768]], 0)
-    iota(cn(i_m, 128), [[1, 128]], 0)
-    iota(cn(i_sel, 128), [[32, 4], [1000, 2], [1, 16]], 0)
-    iota(cn(i_mk, 64), [[32, 4], [1, 16]], 0)
+    dma("s", R("Di", p=(32, 48)), T.res[2 * o:2 * o + 2, S:2 * S], "in2")
+    pi = C("ci", 8, 9)
+    rec("g", lambda: g.iota(pi[0], [[1, 1]], 0, 1), [], regs(pi))
+    ms(C("Yw", 768, 1536), 0.0)
+    ms(C("Win", 0, 1024), 0.0)
+    iota(C("Win", 1024, 1536), [[1, 512]], 0)
+    act(C("Win", 1536, 2304), C("Yw", 768, 1536))
+    act(C("Win", 2304, S), C("Yw", 768, 1536))
+    cp(R("Df", p=(0, 32)), R("Di", p=(0, 32)))
+    cp(R("Df", p=(32, 48)), R("Di", p=(32, 48)))
+    line[0] = "y"
+    for row in range(2):
+        for b in range(4):
+            dma("ys"[b % 2], R("Win", p=rows(b, row)), R("Df", p=(16 * row, 16 * row + 16)), "win0")
+    act(C("M", 0, 768), C("Yw", 768, 1536))
+    ms(C("M", 768, 800), 0.0)
+    for row in range(3):
+        for z in range(8):
+            x = 16 * row + 8 * (z % 2) + 2 * (z // 2)
+            dma("y", C("M", 16, 784, p=(16 * z + row, 16 * z + row + 1)), R("Df", p=(x, x + 2)), "m0")
+    for j in range(4):
+        dma("y", C("W0", 768 * j, 768 * j + 768), T.fl[:, 768 * j:768 * j + 768], "fl", C("Win", 0, 8))
+    line[0] = None
+    for k, (sh, mk) in enumerate(((3, 1), (0, 7), (0, 15), (4, 1), (0, 1), (5, 3), (4, 7), (0, 127))):
+        ts(C("ci", k, k + 1), pi, sh, A.logical_shift_right, mk, A.bitwise_and)
+    cp(C("cf", 0, 8), C("ci", 0, 8))
     ms(R("PK"), 0)
     ms(R("CH"), 0)
     ms(R("X"), 0.0)
-    for k, (sh, mk) in enumerate(((3, 1), (0, 7), (0, 15), (4, 1), (0, 1), (5, 3), (4, 7), (0, 127))):
-        ts(C("ci", k, k + 1), R("pi"), sh, A.logical_shift_right, mk, A.bitwise_and)
-    cp(C("cf", 0, 8), R("ci"))
-    ms(cn(0, 16), 0.0)
-    ts(cf(9), cf(5), 768.0, A.mult)
-    ms(R("CHf"), 0.0)
     tt(cf(8), cf(3), cf(4), A.not_equal)
-    for nm in ("Wa", "Wb", "Wc"):
-        ms(R(nm), 0.0)
-    ts(C("Win", 1544, 2316), C("Win", 0, 772), 1544.0, A.add)
-    act(C("Win", 772, 1544), C("Win", 0, 772), bias=772.0)
-    cp(R("Df", p=(0, 24)), R("Di", p=(0, 24)))
-    act(C("Win", 2316, 3088), C("Win", 0, 772), bias=2316.0)
-    k = 0
-    for row, c0 in ((0, 0), (3, 8), (2, 16)):
-        for b in range(4):
-            dma("ys"[k % 2], C("Win", 0, S, p=rows(b, row)), R("Df", p=(c0, c0 + 8)), "win0")
-            k += 1
-    for j in range(4):
-        dma("y", C("W0", 768 * j, 768 * j + 768), T.fl[:, 768 * j:768 * j + 768], "fl", C("Win", 0, 8))
     ts(cf(10), cf(8), 144.0, A.mult)
-    ts(cf(14), cf(0), -16.0, A.mult)
     ts(cf(11), cf(1), 16.0, A.mult, cf(10), A.add)
-    ts(cf(15), cf(1), -16.0, A.mult)
-    ts(C("PK", 0, 1), cf(0), 3.0, A.mult, cf(11), A.add)
-    ts(C("PK", 2, 3), cf(0), 2.0, A.mult, cf(11), A.add)
+    for t in range(2):
+        ts(C("PK", 2 * t, 2 * t + 1), cf(0), 1.0 + t, A.mult, cf(11), A.add)
+        ms(R("CH%d" % t), 0.0)
     for b in range(4):
         cp(R("ENDS", p=blk(b)), R("tiei", sl(0, 4), sl(8 * b, 8 * b + 8), p=blk(o)))
-    tr(R("TT", 0, sl(0, 128)), cn(16, 128))
-    tr(R("TT", 0, sl(128, 288)), cn(0, 160))
-    ts(R("AL"), cn(i_al, 32), cf(14), A.add)
-    cp(R("SL"), ind(R("TT", 0), C("PK", 0, 1)))
-    ts(R("BL"), cn(i_bl, 32), cf(15), A.add)
-    ts(R("BJ"), cn(i_bj, 8), cf(1), A.add)
-    ts(R("VL"), cn(i_vl, 8), cf(14), A.subtract, cf(1), A.add)
-    ts(cf(12), cf(8), 784.0, A.mult)
-    ms(R("ONES"), 1.0)
-    ts(cf(13), cf(2), 16.0, A.mult, cf(12), A.add)
-    ms(C("LF", 128, 144), 0.0)
-    ts(R("WK"), cn(i_wk, 16), cf(13), A.add)
-    ts(cf(16), cf(5), 128.0, A.mult, cf(2), A.add)
-    ms(C("M", 0, 16), 0.0)
-    ms(C("M", 784, 800), 0.0)
-    ts(R("Gf"), cn(i_g, 8), cf(6), A.is_equal)
+    ms(C("cn", 0, 16), 0.0)
+    ms(C("cn", 136, 160), 128.0)
+    iota(C("cn", 16, 136), [[1, 4], [8, 15], [4, 2]], 0)
+    tr(C("TW", 0, 128), C("cn", 16, 144))
+    tr(C("TW", 128, 288), C("cn", 0, 160))
+    cp(R("SL"), ind(C("TW", 0, 288), C("PK", 0, 1)))
+    ts(cf(14), cf(0), -16.0, A.mult)
+    ts(cf(15), cf(1), -16.0, A.mult)
+    ts(R("AL"), pattern([[1, 8], [-32, 4]], 112), cf(14), A.add)
+    ts(R("BL"), pattern([[1, 8], [0, 4]], 240), cf(15), A.add)
+    ts(R("BJ"), pattern([[8, 2], [0, 4]], 0), cf(1), A.add)
+    ts(R("VL"), pattern([[32, 8]], 0), cf(14), A.subtract, cf(1), A.add)
+    c8, c16 = pattern([[1, 8]], 0), pattern([[16, 16]], 0)
     ts(cf(19), cf(1), 7.0, A.is_lt)
-    ts(cf(20), cf(0), 0.25, A.mult, cf(1), A.add)
-    ts(cf(21), cf(1), 0.0, A.is_equal, float(ZC - NEG), A.mult)
-    ts(cf(22), cf(1), 0.0, A.is_gt, cf(19), A.mult)
-    ts(cf(20), cf(20), 1.0, A.add, cf(19), A.mult)
-    ts(cf(21), cf(21), float(NEG), A.add, cf(19), A.mult)
+    ts(cf(20), cf(0), 8.0, A.mult)
+    ts(cf(21), cf(2), 16.0, A.mult)
+    ts(cf(22), cf(2), 8.0, A.mult, -128.0, A.add)
+    ts(cf(22), cf(22), cf(19), A.mult, 128.0, A.add)
+    ts(cf(23), cf(2), 0.0, A.is_equal, 144.0, A.mult)
+    ts(cf(24), cf(2), 8.0, A.is_equal, -112.0, A.mult)
+    ts(cf(23), cf(23), cf(24), A.add, cf(21), A.add)
+    BJ2, VL2, REP, CL, T1L, PVL = [R("LL", k) for k in range(6)]
+    ts(BJ2, c8, cf(20), A.add)
+    ts(VL2, c8, cf(21), A.add)
+    cp(REP, pattern([[16, 8]], 15))
+    cp(CL, c8)
+    ts(T1L, c8, cf(19), A.mult, cf(22), A.add)
+    ts(PVL, c8, cf(23), A.add, -16.0, A.add)
+    ts(cf(25), cf(3), -544.0, A.mult, 272.0, A.add)
+    ts(cf(26), cf(3), 272.0, A.mult, cf(2), A.add)
+    ts(C("t1", 0, 16), pattern([[0, 8], [1, 2]], 0), cf(25), A.mult, cf(26), A.add)
+    tt(C("t1", 16, 32), C("t1", 0, 16), c16, A.add)
+    cp(R("XL"), C("t1", 16, 32))
+    ts(cf(12), cf(8), 784.0, A.mult)
+    ts(cf(13), cf(2), 16.0, A.mult, cf(12), A.add)
+    ts(C("WM", 0, 9), pattern([[1, 3], [256, 3]], 0), cf(13), A.add)
+    ts(C("WT", 0, 9), pattern([[0, 3], [256, 3]], 0), cf(13), A.add)
+    ts(C("WP", 0, 9), C("WM", 0, 9), 1.0, A.add)
+    ms(R("INC"), 1.0)
+    ms(R("INC", sl(0, 512, 64)), -1000.0)
+    for nm, step in (("RS16", 16), ("RS8", 8)):
+        ms(R(nm), 1.0)
+        ms(R(nm, sl(0, SCRATCH[nm][1][1], step)), 0.0)
+    iota(C("POSX", 64, 128), [[1, 8], [0, 8]], 1)
+    iota(C("POSX", 0, 64), [[8, 8], [0, 8]], 8)
+    p8 = pattern([[0, 8], [1, 8]], 1)
+    for sd, (a, c) in enumerate(((8.0, 8.0), (1.0, 0.5))):
+        ts(R("q3", 0, sl(0, 8), sl(8 * sd, 8 * sd + 8)), p8, a, A.mult)
+        ts(R("q3", 1, sl(0, 8), sl(8 * sd, 8 * sd + 8)), p8, c, A.mult)
+    cp(R("POS2"), R("q3", 0))
+    cp(R("CODE"), R("q3", 1))
+    ts(R("CODW"), R("CODE"), 1.0 / 64.0, A.mult)
+    ts(cf(16), cf(5), 128.0, A.mult, cf(2), A.add)
+    iota(R("TIE"), [[16, 8], [0, 16]], 0)
+    ts(R("TIE"), R("TIE"), cf(16), A.add)
+    rc = pattern([[1, 8], [1, 8]], 1)
+    rec("v", lambda: g.vector.reciprocal(T.RC[:], rc[0]), regs(rc), regs(R("RC")), f=10.0)
+    iota(R("VI"), [[1, 768]], -ZC)
+    ts(cf(9), cf(5), 768.0, A.mult)
+    act(R("VI"), R("VI"), bias=cf(9))
+    ts(bus("BV", 1), pattern([[16, 48]], 0), cf(9), A.add, cf(2), A.add)
+    ts(bus("ZV", 0), bus("BV", 1), -1.0, A.mult, float(ZC), A.add)
+    for nm, a, b, c in (("P", 0, 16, 0.0), ("P", 784, 800, 0.0), ("LF", 120, 144, 0.0), ("P2", 0, 16, 0.0), ("P2", 784, 800, 0.0),
+                        ("TN", 0, 16, 0.0), ("TN", 784, 800, 0.0), ("XT", 0, 16, 0.0), ("XT", 272, 288, 0.0),
+                        ("W0", ZC, NEG, 0.0), ("W1", ZC, NEG, 0.0)):
+        ms(C(nm, a, b), c)
+    act(C("CW", 1024, 1536), C("Yw", 1024, 1536), bias=-1.0)
+    ms(R("Wv"), 0)
+    ts(R("Gf"), c8, cf(6), A.is_equal)
+    cp(R("Gs", 0), R("Gf"))
+    ts(R("Gs", 1), R("Gf"), 128.0, A.mult)
+    ts(R("ID"), pattern([[1, 128]], 0), cf(7), A.is_equal)
+    for nm in ("Wa", "Wc"):
+        ms(R(nm), 0.0)
+    ts(cf(27), cf(1), 1.0, A.add)
+    ts(cf(28), cf(0), 512.0, A.mult, -1024.0, A.add)
+    ts(cf(29), cf(0), -1024.0, A.mult, 512.0, A.add)
+    ts(cf(30), cf(1), 0.0, A.is_gt)
+    for nm, r, c in (("Wa", 0, 27), ("Wa", 1, 28), ("Wa", 2, 30), ("Wa", 3, 29), ("Wc", 0, 19)):
+        ts(R(nm, sl(r, 128, 16)), R("Gf"), cf(c), A.mult)
+    sel = pattern([[16, 4], [1000, 2], [1, 16]], 0)
+    for u in range(2):
+        for h in range(2):
+            ts(R("Sel", 2 * u + h), sel, cf(7), A.subtract, 1000.0 * h - 64.0 * u, A.is_equal)
+    ts(cf(17), cf(3), -16.0, A.mult, cf(7), A.add)
+    ts(R("t2"), sel, 500.0, A.is_gt)
+    ts(R("Hs"), R("t2"), cf(3), A.is_equal)
+    ts(R("MK0"), pattern([[32, 4], [1, 16]], 0), cf(17), A.is_equal)
+    wrap768("M", "TW", 128)
+    act(R("RM"), ind(R("TW"), C("WM", 0, 9)))
+    ts(bus("BV", 2), bus("RM", 0), float(NEG - ZC), A.add)
+    ts(R("RF"), bus("RM", 1, 2), 1024.0, A.add)
+    cp(bus("Ri", 0, 2), bus("RM", 1, 2))
+    ts(bus("Ri", 2, 2), bus("Ri", 0, 2), 7, A.logical_shift_right)
+    ts(bus("TK", 0, 2), bus("Ri", 2, 2), 128.0, A.mult)
+    tt(bus("IX", 0, 2), bus("TK", 0, 2), bus("RM", 1, 2), A.add)
+    cp(R("RL"), bus("IX", 0, 2))
 
-    def constants_a():
-        ts(R("TIE"), cn(i_tie, 128), cf(16), A.add)
-        rec("v", lambda: g.vector.reciprocal(T.RC[:], cn(i_rc, 16)[0]), regs(cn(i_rc, 16)), regs(R("RC")), f=18.0)
-        ms(C("MI", 2048, 2176), -1.0)
-        ms(C("W0", ZC, NEG), 0.0)
-        ms(R("C", sl(0, 2), sl(0, 8)), 0.0)
-        cp(R("Gs", 0), R("Gf"))
-        ts(R("Gs", 1), R("Gf"), 65.0, A.mult)
-
-    def constants_b():
-        ts(cf(23), cf(2), 2.0, A.is_lt, -1.0, A.mult)
-        for nm, r, c in (("Wa", 0, 20), ("Wb", 2, 20), ("Wb", 1, 21), ("Wc", 0, 19), ("Wc", 1, 22)):
-            ts(R(nm, sl(r, 128, 16)), R("Gf"), cf(c), A.mult)
-        ts(R("Wd"), cn(i_m, 128), cf(7), A.is_equal, cf(23), A.mult)
-        ms(C("P2", 0, 16), 0.0)
-        ms(C("P2", 784, 800), 0.0)
-
-    def constants_c():
-        for u in range(2):
-            for h in range(2):
-                ts(R("Sel", 2 * u + h), cn(i_sel, 128), cf(7), A.subtract, 1000.0 * h - 16.0 * u, A.is_equal)
-        ms(R("Wv"), 0.0)
-        ts(cf(17), cf(3), -16.0, A.mult, cf(7), A.add)
-        ts(C("AA", 0, 128), cn(i_sel, 128), 500.0, A.is_gt)
-        ts(R("MK0"), cn(i_mk, 64), cf(17), A.is_equal)
-        ts(R("Hs"), C("AA", 0, 128), cf(3), A.is_equal)
-
-    def constants_d():
-        ms(C("CW", 1024, 1040), -1.0)
-        ms(C("TN", 0, 16), 0.0)
-        ms(C("TN", 784, 800), 0.0)
-        ms(C("Yw", 1024, 1040), 0.0)
-        ms(C("W1", ZC, NEG), 0.0)
-
-    def load_m(t):
-        for b in range(4):
-            dma("y", C("M", 16, 784, p=blk(b)), C("Win", 768 * b, 768 * b + 768, p=blk(b)), "m%d" % t)
-
-    def y_gather():
-        for b, c0, c1 in BLOCKS:
-            act(C("Yg", 768 * b + 16 * c0, 768 * b + 16 * c1), ind(R("Yw"), R("UL", b, sl(80 + c0, 80 + c1))))
-
-    def update(W, dst, store, between):
-        for b, c0, c1 in BLOCKS:
-            x0, x1 = 768 * b + 16 * c0, 768 * b + 16 * c1
-            tt(C(dst, x0, x1), ind(R(W), R("UL", b, sl(32 + c0, 32 + c1))), C("Yg", x0, x1), A.add)
-            for x in between[:4]:
-                x()
-            del between[:4]
-            if store:
-                dma("y", T.yf[:, x0:x1], C(dst, x0, x1), "out")
-
-    def y_window(W):
+    def update(t, W, dst):
+        for nm, c0, c1, n in (("Y%d" % t, 0, 16, n_direct), ("X%d" % t, 16, 128, n_direct if t else n_relay)):
+            arrive(nm, n, "L" + nm)
+            place(lambda k, b: R("UL", b, sl(c0, c1), p=blk(k)), lambda b: R("U" + nm, p=blk(b)),
+                  lambda k, b: R("L" + nm, k, p=blk(b)))
         for sd in range(2):
             for b in range(4):
                 act(C("Yw", 512 * sd + 128 * b, 512 * sd + 128 * b + 128), ind(R(W), R("UL", b, sl(8 * sd, 8 * sd + 8))))
-
-    def ends_out(t):
+        for b, c0, c1 in BLOCKS[t]:
+            x0, x1 = 768 * b + 16 * c0, 768 * b + 16 * c1
+            act(C("Yg", x0, x1), ind(R("Yw"), R("UL", b, sl(32 + c0, 32 + c1))))
+            tt(C(dst, x0, x1), ind(R(W), R("UL", b, sl(80 + c0, 80 + c1))), C("Yg", x0, x1), A.add)
+            if t:
+                dma("y", T.yf[:, x0:x1], C(dst, x0, x1), "out")
         for sd in range(2):
             cp(R("YTf", 2 * t + sd), C("UL", 0, 4, sl(16 + 8 * sd, 24 + 8 * sd)))
 
-    def per_tie_a():
-        tt(R("t2"), ind(R("KK"), R("BJ")), R("POS1"), A.is_equal)
-        ts(R("NG"), R("KP"), 0.0, A.is_equal)
-        ts(R("u2"), R("KK"), 0.0, A.is_gt, float(NEG), A.mult)
-        tt(R("t6", 0), ind(R("CHf"), R("VL")), R("t2"), A.mult)
-        tt(R("t6", 1), ind(C("CHf", 16, 272), R("VL")), R("t2"), A.mult)
-
-    def per_tie_b(t):
-        ts(C("u1", 0, 8), R("NG"), float(ZC), A.mult)
-        tt(R("t7"), C("t6", 0, 2, sl(0, 64)), C("t6", 0, 2, sl(64, 128)), A.add)
-        for sd in range(2):
-            tt(C("t3", 48 + 8 * sd, 56 + 8 * sd), C("u2", 8 * sd, 8 * sd + 8), C("u1", 0, 8), A.add)
-        tt(R("t8"), C("t7", 0, 2, sl(0, 32)), C("t7", 0, 2, sl(32, 64)), A.add)
-        tt(C("t3", 16, 24), R("NG"), R("ENDS", 2 * t), A.mult)
-        tt(R("t9"), C("t8", 0, 2, sl(0, 16)), C("t8", 0, 2, sl(16, 32)), A.add)
-        tt(C("t3", 24, 32), R("NG"), R("ENDS", 2 * t + 1), A.mult)
-        tt(R("PK2"), C("t9", 0, 2, sl(0, 8)), C("t9", 0, 2, sl(8, 16)), A.add)
-        for sd in range(2):
-            tt(C("t3", 8 * sd, 8 * sd + 8), C("t3", 48 + 8 * sd, 56 + 8 * sd), C("PK2", 0, 8), A.add)
-        tt(C("t3", 16, 32), C("t3", 16, 32), R("PK2"), A.add)
-        cp(C("UM0", 0, 32) if t == 0 else R("UY1"), C("t3", 0, 32))
-
-    def parents():
-        tt(C("Dp", 0, 768), C("Dp", 0, 768), C("TN", 16, 784), A.mult)
-        tt(R("N"), C("Dp", 0, 768), C("M", 16, 784), A.add)
-
-    def sources(ix, iy):
-        wrap768("TN")
-        pick768(R("IXf"), 0)
-        tt(R("z1"), R("IXf"), R("D1"), A.mult)
-        tt(R("z2"), R("IXf"), R("DD"), A.mult)
-        tt(R("z1"), R("z1"), R("VD"), A.add)
-        tt(R("z2"), R("z2"), R("TSf"), A.add)
-        cp(ix, R("z1"))
-        cp(iy, R("z2"))
-
-    def xv(nm, ch, pos):
-        return R(nm, sl(896 * ch + pos, 896 * ch + 896, 7))
-
-    def delta(c0, c1):
-        mm(C("Dp", c0, c1), R("Wb"), C("EQ", c0, c1), True, False)
-        mm(C("Dp", c0, c1), R("Wc"), C("PR", c0, c1), False, False)
-        mm(C("Dp", c0, c1), R("Wd"), C("M", 16 + c0, 16 + c1), False, True)
-
-    def limits(ch):
-        c0 = 256 * (ch % 2)
-        qa, qb = C("Qp", c0, c0 + 128), C("Qp", c0 + 128, c0 + 256)
-        cs = sl(896 * ch, 896 * ch + 896)
-        return [lambda: scan(R("C", ch % 2, sl(8, 904)), R("XA", cs), R("XB", cs), 0.0, A.add, A.add),
-                lambda: tt(qa, R("C", ch % 2, sl(14, 904, 7)), R("C", ch % 2, sl(7, 897, 7)), A.subtract),
-                lambda: tt(qa, qa, R("RR", ch), A.mult),
-                lambda: ts(qb, qa, -0.0625, A.add),
-                lambda: ts(qa, qa, 0.0625, A.add)], qa, qb
-
-    first = len(ops)
     for t in range(2):
-        W = "W%d" % t
+        W, CHf = "W%d" % t, "CH%d" % t
         wn = C(W, 0, NEG)
         pk = C("PK", 2 * t, 2 * t + 1)
         for sd in range(2):
             cp(R("CH", 8 * sd, sl(0, 8)), R("ENDS", 2 * t + sd))
-            act(C("CHf", 128 * sd, 128 * sd + 8), R("ENDS", 2 * t + sd))
+            act(C(CHf, 128 * sd, 128 * sd + 8), R("ENDS", 2 * t + sd))
         for s in range(7):
             for sd in range(2):
                 act(R("X", sd, sl(16, 144)), ind(R("Win"), R("CH", 8 * sd + s, sl(0, 8))))
-                if s + sd > 0:
-                    z = 16 * (8 * (1 - sd) + s + sd)
-                    act(C("CHf", z, z + 16), ind(R("TT", 1 - sd), pk))
-                tr(R("TT", sd, sl(0, 128)), R("X", sd, sl(16, 144)))
-                tr(R("TT", sd, sl(128, 288)), R("X", sd))
+                y = 2 * (s % 2) + sd
+                tr(R("TT", y, sl(0, 128)), R("X", sd, sl(16, 144)))
+                tr(R("TT", y, sl(128, 288)), R("X", sd))
                 if s < 6:
-                    cp(R("CH", 8 * sd + s + 1), ind(R("TT", sd), pk))
-        act(C("CHf", 240, 256), ind(R("TT", 1), pk))
-        chw = R("CHf")
+                    cp(R("CH", 8 * sd + s + 1), ind(R("TT", y), pk))
+                z = 16 * (8 * sd + s + 1)
+                act(C(CHf, z, z + 16), ind(R("TT", y), pk))
+        chw = C(CHf, 0, 256)
         for hf in range(2):
-            act(C("AA", 256 * hf, 256 * hf + 256), ind(chw, C("AL", 16 * hf, 16 * hf + 16)))
-        if t == 0:
-            act(R("VI"), R("VI"), bias=cf(9))
-            constants_a()
-        else:
-            arrive("U0", n_relay, "LU0")
-            place(lambda k, b: R("UL", b, p=blk(k)), lambda b: R("UM0", p=blk(b)), lambda k, b: R("LU0", k, p=blk(b)))
-            y_window("W0")
-            y_gather()
-        ts(R("AM"), ind(chw, R("VL")), -float(ZC), A.add)
+            act(C("AA", 256 * hf, 256 * hf + 256), ind(C(CHf, 0, 128), C("AL", 16 * hf, 16 * hf + 16)))
+        act(R("AM"), ind(chw, R("VL")), bias=-float(ZC))
         for hf in range(2):
             tt(C("NE", 256 * hf, 256 * hf + 256), ind(chw, C("BL", 16 * hf, 16 * hf + 16)), C("AA", 256 * hf, 256 * hf + 256), A.not_equal)
-        scan(R("KS"), R("NE"), R("ONES"), 1.0, A.mult, A.add)
-        ks = R("KS", sl(63, 512, 64))
-        ts(C("IJ", 0, 8), ks, -4.5, A.add, 0.125, A.mult)
-        ts(R("k1"), C("IJ", 0, 8), 8.0, A.mult, 1.0, A.add)
-        tt(C("IJ", 8, 16), ks, R("k1"), A.subtract)
-        tt(R("ON"), ind(R("IJ"), R("BJ")), R("POS1"), A.is_ge)
-        tt(R("k2"), C("IJ", 0, 8), C("IJ", 8, 16), A.add)
-        tt(C("LF", 0, 128), R("AM"), R("ON"), A.mult)
-        ts(C("LF", 128, 136), R("k2"), 15.0, A.min, -float(ZC), A.add)
+        scan(R("KS"), R("INC"), R("NE"), 0.0, A.add, A.mult)
+        ts(C("IJ", 0, 8), R("KS", sl(63, 512, 64)), 0.0, A.max)
+        ts(C("IJ", 8, 16), C("IJ", 0, 8), 7, A.bitwise_and)
+        ts(C("LF", 56, 64), C("IJ", 0, 8), -float(ZC), A.add)
+        tt(R("ON"), ind(R("IJ"), R("BJ")), R("POSX"), A.is_ge)
+        for c0 in (0, 64):
+            tt(C("LF", c0, c0 + 56), C("AM", c0, c0 + 56), C("ON", c0, c0 + 56), A.mult)
         sbf, ls = "SB%d" % t, "LS%d" % t
         ts(R(sbf), ind(R("LF"), C("SL", 0, 8)), float(ZC), A.add)
         send("E%d" % t, C(sbf, 0, 120), [(cores[k], T[ls][:, o, 0:120]) for k in peers])
         if t == 0:
-            load_m(0)
-        kept = [
-            lambda: tt(R("t1"), ind(C("CHf", 24, 272), R("VL")), R("TIE"), A.not_equal),
-            lambda: ts(R("k3"), ks, 65.0, A.is_lt),
-            lambda: tt(R("t2"), R("t1"), R("ON"), A.mult),
-            lambda: tt(R("t3"), C("t2", 0, 64), C("t2", 64, 128), A.add),
-            lambda: tt(R("t8", 0), C("t3", 0, 32), C("t3", 32, 64), A.add),
-            lambda: tt(R("u2"), R("t8", 0, sl(0, 16)), R("t8", 0, sl(16, 32)), A.add),
-            lambda: tt(C("u1", 8, 16), C("u2", 0, 8), C("u2", 8, 16), A.add),
-            lambda: tt(R("NG"), C("u1", 8, 16), R("k3"), A.is_lt),
-            lambda: tt(C("IJk", 0, 8), C("IJ", 0, 8), R("NG"), A.mult),
-            lambda: tt(C("IJk", 8, 16), C("IJ", 8, 16), R("NG"), A.mult),
-            lambda: tt(R("ONK"), ind(R("IJk"), R("BJ")), R("POS1"), A.is_ge),
-            lambda: cp(C("GL", 0, 8), R("CH", 8, sl(0, 8))),
-            lambda: tt(R("t2"), R("AM"), R("ONK"), A.mult),
-            lambda: ts(C("GL", 8, 136), R("t2"), float(S), A.add),
-            lambda: cp(C("GL", 64, 72), R("CH", 0, sl(0, 8))),
-            lambda: act(C("MI", 0, 2048), ind(R("Win"), C("GL", 0, 128)))]
-        if t == 0:
-            for x in kept:
-                x()
-            wrap768("M")
-            pick768(R("VD"), 1)
-            for r in range(2):
-                pick768(R("RF", r), 3 - r)
-                pick768(R("RL", r), 3 - r)
+            for b in range(4):
+                dma("y", R("Win", p=rows(b, 2)), R("Df", p=(32, 48)), "res1")
         else:
-            update("W0", "W1", False, kept)
-            ends_out(0)
-        for nm, c0 in (("T1", 128), ("T2", 0)):
+            update(0, "W0", "W1")
+        act(C("XT", 16, 144), ind(R("LF"), T1L))
+        act(R("n1"), ind(C(CHf, 16, 272), VL2))
+
+        def spread():
+            act(R("TP"), ind(C("PR", 0, 544), R("XL")))
             for b in range(4):
                 for b2 in range(4):
-                    dma("y", C(nm, 128 * b, 128 * b + 128, p=blk(b2)), C("MI", c0, c0 + 2048, p=rows(b, 4)), nm + str(t))
+                    dma("y", C("T12", 256 * b, 256 * b + 256, p=blk(b2)), R("TP", p=blk(b)), "T%d" % t)
+        kept = [lambda: tt(C("XT", 144, 272), ind(chw, PVL), R("n1"), A.subtract),
+                lambda: tt(R("t1"), ind(C(CHf, 24, 272), VL2), R("TIE"), A.not_equal),
+                lambda: tr(C("PR", 0, 256), C("XT", 16, 272)),
+                lambda: tr(C("PR", 256, 544), R("XT")),
+                lambda: tt(R("ON2"), ind(R("IJ"), BJ2), R("POS2"), A.is_ge),
+                lambda: tt(R("t2"), R("t1"), R("ON2"), A.mult),
+                lambda: tt(R("t4"), R("ON2"), R("CODW"), A.mult),
+                lambda: scan(R("t5"), R("RS16"), R("t2"), 0.0, A.mult, A.subtract),
+                lambda: tt(R("KW"), ind(R("t5"), REP), R("t4"), A.add)]
+        if t == 0:
+            line[0] = "vst"
+            for x in kept:
+                x()
+            line[0] = None
+            spread()
+            kept = []
         arrive("E%d" % t, n_direct, ls)
-        place(lambda k, b: C("L", 0, 60, sl(2 * b, 2 * b + 2), p=blk(k)), lambda b: C(sbf, 0, 120, p=blk(b)),
+        place(lambda k, b: R("L", sl(b, 480, 4), p=blk(k)), lambda b: C(sbf, 0, 120, p=blk(b)),
               lambda k, b: R(ls, k, sl(0, 120), p=blk(b)))
-        for ch in range(4):
+        seq = list(range(7, 14)) + list(range(7))
+        dq = [C(("Qp", "KE")[ch // 2], 512 * (ch % 2), 512 * (ch % 2) + 128) for ch in range(4)]
+
+        def gather(ch):
+            cut = 7 - CUT[t][ch]
+            for p0, p1 in ((7, 10), (10, 14)):
+                act(xx(ch, p0, p1 - p0), ind(wn, lst(ch, 1 + p0, p1 - p0)), scale=-1.0, bias=0.0625)
+            for p0, p1 in ((0, min(cut, 3)), (3, cut)):
+                if p0 < p1:
+                    act(xx(ch, p0, p1 - p0), ind(wn, lst(ch, p0, p1 - p0)), bias=-0.0625)
+            act(R("RR", ch), ind(R("RC"), lst(ch, 7)))
+
+        def share(ch, p0, p1):
+            return lambda: ts(xx(ch, p0, p1 - p0), ind(wn, lst(ch, p0, p1 - p0)), -0.0625, A.add)
+
+        def sums(ch):
+            for n, x in enumerate(seq[:NPE[ch]]):
+                mm(dq[ch], R("ID"), xx(ch, x), n == 0, n == NPE[ch] - 1)
+
+        def limit(ch):
+            return [lambda x=x: tt(dq[ch], dq[ch], xx(ch, x), A.add) for x in seq[NPE[ch]:]] + \
+                   [lambda: tt(dq[ch], dq[ch], R("RR", ch), A.mult)]
+
+        def compare(ch):
+            return [lambda x=x: tt(R("VT", ch, x), xx(ch, x), dq[ch], A.is_ge if x > 6 else A.is_le)
+                    for pos in range(7) for x in (pos, 7 + pos)]
+
+        def count(ch):
             for pos in range(7):
-                if ch == 0:
-                    cp(xv("XA", ch, pos), ind(wn, R("L", pos)))
-                else:
-                    act(xv("XA", ch, pos), ind(wn, R("L", 7 * ch + pos)))
-                act(xv("XB", ch, pos), ind(wn, R("L", 28 + 7 * ch + pos)), scale=-1.0)
-            act(R("RR", ch), ind(R("RC"), R("L", 56 + ch)))
-        for x in limits(0)[0]:
-            x()
-        for ch in range(4):
-            cb = ch % 2
-            qa, qb = limits(ch)[1:]
-            for pos in range(7):
-                if 0 < ch < 3 and pos >= 2:
-                    limits(ch + 1)[0][pos - 2]()
-                tt(R("VT", cb, 7 + pos), xv("XB", ch, pos), qb, A.is_ge)
-                tt(R("VT", cb, pos), xv("XA", ch, pos), qa, A.is_le)
-                pv = R("PV", sl(4 * pos + ch, 224, 28))
-                mm(pv, R("VT", cb, pos), R("Gs", 0), True, False)
-                mm(pv, R("VT", cb, 7 + pos), R("Gs", 1), False, True)
-            if ch == 0:
-                if t == 0:
-                    constants_b()
-                tt(R("EQ"), ind(R("T1"), R("RL", t)), R("VI"), A.is_equal)
-                mm(C("Pp", 0, 512), R("Wa"), C("EQ", 0, 512), True, True)
-                mm(C("Pp", 512, 768), R("Wa"), C("EQ", 512, 768), True, True)
-                tt(R("PR"), ind(R("T2"), R("RL", t)), R("EQ"), A.mult)
-                for x in limits(1)[0]:
-                    x()
-                delta(0, 256)
-            if ch < 2:
-                delta(256 * ch + 256, 256 * ch + 512)
-        act(C("P2", 16, 784), C("Dp", 0, 768))
-        act(R("P"), C("Pp", 0, 768))
+                pv = R("PV", sl(7 * ch + pos, 224, 28))
+                mm(pv, R("VT", ch, pos), R("Gs", 0), True, False)
+                mm(pv, R("VT", ch, 7 + pos), R("Gs", 1), False, True)
+
+        def weave(chain, fill):
+            for n, x in enumerate(chain):
+                x()
+                for y in fill[n * len(fill) // len(chain):(n + 1) * len(fill) // len(chain)]:
+                    y()
+        line[0] = "vst"
+        for ch in range(3):
+            gather(ch)
+        ones = [share(ch, p, p + 1) for ch in (1, 2) for p in range(7 - CUT[t][ch], 7)]
+        weave([share(0, 0, 3), share(0, 3, 7)] + ones[:EARLY], [])
+        sums(0)
+        weave(limit(0), ones[EARLY:] + kept)
+        if t == 1:
+            spread()
+        gather(3)
+        sums(1)
+        sums(2)
+        weave(limit(1), compare(0))
+        count(0)
+        sums(3)
+        for ch in (1, 2):
+            weave(limit(ch + 1), compare(ch))
+            count(ch)
+        weave(compare(3), [])
+        count(3)
+        line[0] = None
         sv, lv = "SV%d" % t, "LV%d" % t
-        cp(R(sv), C("PV", 0, 224))
+        ts(R(sv), C("PV", 0, 224), -OFS, A.add)
 
         def send_votes(sv=sv, lv=lv, t=t):
             trs = []
@@ -551,131 +603,164 @@ def rank_program(g, core, T, topo):
                 lsum[0] += n
             g.remote_dma_fused(trs, local_sem=T.sem.ls)
         rec("g", send_votes, regs(R(sv)), [], "r", "V%d" % t)
-        act(C(W, NEG, WW), C(W, 0, S), scale=-1.0)
-        if t == 0:
-            constants_c()
-        tt(R("KW"), R("ONK"), R("POS1"), A.mult)
-        ts(C("KW", 0, 64), C("KW", 0, 64), 16.0, A.mult)
-        wrap768("P2")
-        pick768(R("ZW"), 2)
-        pick768(R("D1"), 1)
-        ts(R("Zi"), R("ZW"), 4.0, A.mult)
-        ts(R("z2"), R("ZW"), 0.0, A.is_gt)
-        ts(R("SDi"), R("Zi"), 1, A.bitwise_and)
-        ts(R("z1"), R("SDi"), 512.0, A.mult, -1024.0, A.add)
-        ts(R("DD"), R("SDi"), -1024.0, A.mult, 512.0, A.add)
-        tt(R("z1"), R("z1"), R("RF", t), A.add)
-        tt(R("z1"), R("z1"), R("z2"), A.mult)
-        ts(R("TS"), R("z1"), 1024.0, A.add)
-        ts(R("TSf"), R("z1"), 1024.0, A.add)
+        for j in range(8):
+            act(C(W, NEG + 384 * j, NEG + 384 * j + 384), C(W, 384 * j, 384 * j + 384), scale=-1.0)
+        halves = [(384 * z, 512 * z) for z in range(2)]
+        for c0, z in halves:
+            rl = C("RL", 48 * t + c0 // 16, 48 * t + c0 // 16 + 24)
+            act(C("Dp", z, z + 384), C("VI", c0, c0 + 384))
+            act(C("Yg", c0, c0 + 384), ind(R("T12"), rl))
+            act(C("Yg", 768 + c0, 1152 + c0), ind(C("T12", 128, 1024), rl))
+            act(C("Qp", z, z + 384), C("Yg", 768 + c0, 1152 + c0))
+        for c0, z in halves:
+            tt(C("EQ", c0, c0 + 384), C("Yg", c0, c0 + 384), C("Dp", z, z + 384), A.is_equal)
+            mm(C("Dp", z, z + 384), R("Wa"), C("EQ", c0, c0 + 384), True, True)
+            act(C("P", 16 + c0, 400 + c0), C("Dp", z, z + 384))
+        for c0, z in halves:
+            tt(C("PR", c0, c0 + 384), C("Qp", z, z + 384), C("EQ", c0, c0 + 384), A.mult)
+            mm(C("Qp", z, z + 384), R("Wc"), C("PR", c0, c0 + 384), True, True)
+            act(C("P2", 16 + c0, 400 + c0), C("Qp", z, z + 384))
+        wrap768("P", "TB")
+        act(bus("NB", 0, 3), ind(R("TB"), C("WP", 0, 9)))
+        tt(bus("BV", 0), bus("NB", 0), bus("RF", t), A.add)
+        cp(R("TS"), bus("BV", 0))
+
+        def turned_source():
+            wrap768("P2", "TW", 192)
+            act(bus("NB", 4), ind(R("TW"), C("WT", 0, 3)))
+            tt(bus("ZV", 1), bus("NB", 4), bus("BV", 2) if t == 0 else bus("IX", 2), A.add)
+            tt(bus("ZV", 1), bus("ZV", 1), bus("NB", 1), A.mult)
+            tt(bus("NB", 3), bus("ZV", 1), bus("ZV", 0), A.add)
+        turned_source()
         arrive("V%d" % t, sum(len(topo.engines(cores[k], core)) // 4 for k in peers), lv)
         for u in range(2):
             n = 0
             for k in every:
                 for h in range(2):
-                    mm(R("VS", sl(u, 56, 2)), R("Sel", 2 * u + h), R(sv if k == o else lv, k, sl(28 * h, 28 * h + 28)), n == 0, n == 7)
+                    mm(C("VS", 28 * u, 28 * u + 28), R("Sel", 2 * u + h), R(sv if k == o else lv, k, sl(28 * h, 28 * h + 28)), n == 0, n == 7)
                     n += 1
         vs = C("VS", 0, 56)
-        ts(R("Mi"), vs, -32.0, A.add, 1.0 / 65.0, A.mult)
-        ts(C("Wv", 64, 120), vs, 2145.0, A.is_ge)
-        ts(C("t3", 0, 56), R("Mi"), 65.0, A.mult, 33.0, A.add)
-        tt(C("Wv", 0, 56), vs, C("t3", 0, 56), A.is_ge)
-        tt(R("t7"), R("Wv"), R("KW"), A.mult)
-        tt(R("t4"), C("t7", 0, 2, sl(0, 32)), C("t7", 0, 2, sl(32, 64)), A.max)
-        tt(R("t5"), C("t4", 0, 2, sl(0, 16)), C("t4", 0, 2, sl(16, 32)), A.max)
-        tt(R("u2"), C("t5", 0, 2, sl(0, 8)), C("t5", 0, 2, sl(8, 16)), A.max)
-        tt(R("KP"), C("u2", 0, 8), C("u2", 8, 16), A.subtract)
+        ts(R("Si"), vs, 4 * OFS + 31.0, A.add)
+        ts(R("Wv", sl(1, 16, 2), sl(0, 7)), vs, 33.0 * 128.0 - 4 * OFS, A.is_ge, 64.0, A.mult)
+        ts(R("Wv", sl(0, 16, 2), sl(0, 7)), R("Si"), 64, A.bitwise_and)
+        tt(R("t1"), R("Wv"), R("KW"), A.mult)
+        scan(R("KM"), R("RS8"), R("t1"), 0.0, A.mult, A.max)
+        ka, kb = R("KM", sl(7, 128, 16)), R("KM", sl(15, 128, 16))
+        tt(R("KP"), ka, kb, A.subtract)
         for j in range(8):
-            ts(C("E", 0, 4, sl(16 * j, 16 * j + 16)), R("MK0"), C("KP", j, j + 1), A.mult)
-        ts(C("KK", 0, 8), C("u2", 0, 8), 0.0625, A.mult)
-        ts(C("KK", 8, 16), R("KP"), -1.0, A.mult, 0.0, A.max)
-        for b in range(4):
-            mm(C("KE", 128 * b, 128 * b + 128), R("Hs"), R("E", b), True, True)
-        act(C("CW", 512, 1024), R("KE"), bias=0.5, scale=-1.0)
-        act(C("CW", 0, 512), R("KE"), bias=0.5, scale=0.0625)
-        per_tie_a()
+            if j % 2:
+                act(R("E", j), R("MK0"), scale=C("KP", j, j + 1))
+            else:
+                ts(R("E", j), R("MK0"), C("KP", j, j + 1), A.mult)
+        for sd in range(2):
+            for b in range(4):
+                mm(C("KE", 512 * sd + 128 * b, 512 * sd + 128 * b + 128), R("Hs"), C("E", 0, 8, b), True, True)
+        act(C("CW", 512, 1024), C("KE", 512, 1024), bias=0.5, scale=-2.0)
+        ts(C("CW", 0, 512), C("KE", 0, 512), 0.125, A.mult, 0.5, A.add)
+        uy, ux = "UY%d" % t, "UX%d" % t
+
+        def turns():
+            for c0 in (0, 384):
+                tt(C("TN", 16 + c0, 400 + c0), ind(R("CW"), C("TS", c0 // 16, c0 // 16 + 24)), C("P", 16 + c0, 400 + c0), A.is_gt)
+
+        def opened():
+            tt(R("cm"), ka, kb, A.max)
+            tt(R("t2"), ind(R("cm"), CL), R("CODE"), A.is_equal)
+            tt(C("t6", 0, 128), ind(chw, VL2), R("t2"), A.mult)
+            scan(C("t7", 0, 128), R("RS16"), C("t6", 0, 128), 0.0, A.mult, A.add)
+            ts(C("u1", 0, 8), R("cm"), 0.0, A.is_equal, float(ZC), A.mult)
+            ts(C("u2", 0, 8), R("cm"), 8.0, A.is_ge, float(NEG), A.mult)
+            ts(C("u2", 8, 16), R("KP"), 0.0, A.is_lt, float(NEG), A.mult)
+            for sd in range(2):
+                tt(C("u3", 8 * sd, 8 * sd + 8), C("u2", 8 * sd, 8 * sd + 8), C("u1", 0, 8), A.add)
+                tt(C("t3", 8 * sd, 8 * sd + 8), C("u3", 8 * sd, 8 * sd + 8), R("t7", sl(15, 128, 16)), A.add)
+            cp(R(uy), C("t3", 0, 16))
+            to_all("Y%d" % t, uy, "LY%d" % t)
+
+        def ends():
+            tt(C("t6", 128, 256), R("n1"), R("t2"), A.mult)
+            scan(C("t7", 128, 256), R("RS16"), C("t6", 128, 256), 0.0, A.mult, A.add)
+            ts(C("u1", 8, 16), R("cm"), 0.0, A.is_equal)
+            for sd in range(2):
+                tt(C("u3", 16 + 8 * sd, 24 + 8 * sd), C("u1", 8, 16), R("ENDS", 2 * t + sd), A.mult)
+            tt(C("t3", 16, 32), C("u3", 16, 32), R("t7", sl(15, 256, 16)), A.add)
+            cp(C(ux, 0, 16), C("t3", 16, 32))
+
+        def sources():
+            wrap768("TN", "TB")
+            act(R("TK"), ind(R("TB"), C("WT", 0, 9)))
+            for a, k in ((0, 2), (2, 1)):
+                tt(bus("TK", a, k), bus("TK", a, k), bus("NB", 2 + a, k), A.mult)
+                tt(bus("IX", a, k), bus("TK", a, k), bus("BV", a, k) if a == 0 or t == 0 else bus("IX", 2), A.add)
+            cp(C(ux, 16, 112), bus("IX", 0, 2))
+
+        def parents():
+            for c0, z in halves:
+                tt(C("Qp", z, z + 384), C("Qp", z, z + 384), C("TN", 16 + c0, 400 + c0), A.mult)
+            for c0, z in halves:
+                tt(C("N", c0, c0 + 384), C("Qp", z, z + 384), C("M", 16 + c0, 400 + c0), A.add)
         if t == 0:
-            constants_d()
-        else:
-            per_tie_b(1)
-            to_all("Y1", "UY1", "LY1")
-        tt(C("TN", 16, 784), ind(R("CW"), R("TS")), R("P"), A.is_gt)
-        if t == 0:
+            turns()
             parents()
+            mark = len(ops) - 1
             for z in range(8):
-                dma("ys"[z % 2], C("Win", 0, S, p=(16 * z, 16 * z + 1)), R("N", p=(16 * (z % 2), 128, 32)), "win1")
-            load_m(1)
-            per_tie_b(0)
-            sources(C("UM0", 32, 80), C("UM0", 80, 128))
-            relay("U0", "UM0", "HU0")
-    sources(C("UX1", 0, 48), C("UX1", 48, 96))
+                dma("ys"[z % 2], R("Win", p=(16 * z, 16 * z + 1)), R("N", p=(16 * (z % 2), 128, 32)), "win1")
+            first = len(ops)
+            opened()
+            ops[first + 2]["after"].add(mark)
+            ends()
+            first = len(ops)
+            sources()
+            ops[first]["after"].add(mark)
+            relay("X0", "UX0", "HX0")
+        else:
+            opened()
+            mark = len(ops) - 2
+            turns()
+            ops[-2]["after"].add(mark)
+            ends()
+            sources()
     to_all("X1", "UX1", "LX1")
-    parents()
-    for b in range(4):
-        for h in range(2):
-            dma("ys"[h], R("YB", p=(64 * h + 16 * b, 64 * h + 16 * b + 16)), R("N", p=(32 * b + 16 * h, 32 * b + 16 * h + 1)), "yb")
-    relay("B", "YB", "HB")
-    arrive("Y1", n_direct, "LY1")
-    place(lambda k, b: R("UL", b, sl(0, 32), p=blk(k)), lambda b: R("UY1", p=blk(b)), lambda k, b: R("LY1", k, p=blk(b)))
-    y_window("W1")
-    arrive("X1", n_direct, "LX1")
-    place(lambda k, b: R("UL", b, sl(32, 128), p=blk(k)), lambda b: R("UX1", p=blk(b)), lambda k, b: R("LX1", k, p=blk(b)))
-    ends_out(1)
+    for j in range(3):
+        ts(C("XT", 16 + 16 * j, 32 + 16 * j), R("IX", sl(96 + j, 144, 3)), float(ZC - NEG), A.add)
+    tr(C("PR", 0, 64), C("XT", 16, 80))
+    tr(C("PR", 256, 352), C("XT", 0, 96))
+    act(R("YB"), ind(C("PR", 0, 352), C("XL", 0, 3)))
+    cp(R("UB"), R("YB"))
+    relay("B", "UB", "HB")
+    update(1, "W1", "W0")
     dma("y", T.yt[:], R("YTf"), "out")
-    dma("y", T.yp[2 * o:2 * o + 2, :], R("YB"), "out")
-    y_gather()
     arrive("B", n_relay, "LB")
-    for k in peers:
-        dma("s", T.yp[2 * k:2 * k + 2, :], R("LB", k), "out")
-    update("W1", "W0", True, [])
+    for k in every:
+        if k != o:
+            cp(bus("TK", peers.index(k)), R("LB", k))
+        for b in range(4):
+            src = R("YB", p=blk(b)) if k == o else C("TK", 48 * peers.index(k), 48 * peers.index(k) + 48, p=blk(b))
+            dma("y", T.yp[2 * k:2 * k + 2, 768 * b:768 * b + 768], src, "out")
 
     pre = [dict() for op in ops]
-    last, members, sent = {}, {}, {}
+    members, sent = {}, {}
     for n, op in enumerate(ops):
         if op["kind"] == "d":
             members.setdefault(op["group"], []).append(n)
         if op["kind"] == "r":
             sent[op["group"]] = n
     for n, op in enumerate(ops):
+        for d in op["after"]:
+            pre[n][d] = 0.0
         for d in op["deps"]:
             if ops[d]["kind"] == "d":
                 for m in members[ops[d]["group"]]:
-                    pre[n][m] = 2.2
+                    pre[n][m] = DMA + SLOW.get(ops[d]["group"], 0.4)
             else:
-                pre[n][d] = 0.15
+                pre[n][d] = HOP if ops[d]["kind"] == "c" else 0.0
         if op["kind"] == "a":
             nm = op["group"]
-            pre[n][sent[nm] if nm in sent else sent["h" + nm]] = 3.0 if nm in sent else 6.0
-    soft = [all(ops[d]["kind"] == "c" for d in op["deps"]) and op["kind"] == "c" and n >= first for n, op in enumerate(ops)]
-    todo = {}
-    for n, op in enumerate(ops):
-        todo.setdefault(op["q"], []).append(n)
-    end, free, order = {}, {q: 0.0 for q in todo}, []
-
-    def ready(n):
-        if any(d not in end for d in pre[n]):
-            return None
-        return max([end[d] + pre[n][d] for d in pre[n]] + [0.0])
-    while len(order) < len(ops):
-        best = None
-        for q in todo:
-            if not todo[q]:
-                continue
-            head = ready(todo[q][0])
-            x = None if head is None else (max(head, free[q]), todo[q][0])
-            if q in "vs" and (head is None or head > free[q]):
-                for m in todo[q][1:30]:
-                    r = ready(m) if soft[m] else None
-                    if r is not None and max(r, free[q]) + ops[m]["dur"] <= (free[q] + 0.15 if head is None else head + 0.05):
-                        x = (max(r, free[q]), m)
-                        break
-            if x is not None and (best is None or x < best):
-                best = x
-        n = best[1]
-        q = ops[n]["q"]
-        end[n] = free[q] = best[0] + ops[n]["dur"]
-        todo[q].remove(n)
-        order.append(n)
+            pre[n][sent[nm] if nm in sent else sent["h" + nm]] = (FAR - 0.5 if nm[0] == "Y" else FAR) if nm in sent else 2 * FAR - 0.5
+    tail = len(ops)
+    ops.append({"q": "x", "fn": None, "deps": set(), "after": set(), "kind": "a", "group": "out", "dur": 0.0})
+    pre.append({m: DMA for m in members["out"]})
+    order = [n for n in schedule(ops, pre) if n != tail]
 
     need = set(d for op in ops for d in op["deps"] if ops[d]["kind"] == "c")
     cnt = {q: 0 for q in QS}

@@ -6,9 +6,9 @@ S = 3072
 ZC = S
 NEG = S + 64
 WW = NEG + S
-NPE = (8, 7, 7, 8)
-CUT = ((7, 5, 0, 0), (7, 2, 0, 0))
-EARLY = 2
+NPE = (7, 8, 8, 7)
+CUT = ((7, 6, 0, 0), (7, 6, 0, 0))
+MID = 1536.0
 OFS = 1032.0
 F, B16, H16, I32, U16 = "float32", "bfloat16", "float16", "int32", "uint16"
 
@@ -21,40 +21,40 @@ SCRATCH = {
     "W0": sb([WW]), "W1": sb([WW]), "XX": sb([7168]), "VT": sb([4, 14, 128], B16), "RR": sb([4, 128]),
     "Yg": sb([S]), "Yw": sb([1536]), "CW": sb([1536]), "Win": sb([S]), "X": sb([2, 160]), "TT": sb([4, 288]),
     "XT": sb([288]), "TP": sb([256]), "T12": sb([1024]), "n1": sb([128]),
-    "EQ": sb([768], B16), "PR": sb([768]), "P": sb([800], B16), "P2": sb([800]), "M": sb([800]), "VI": sb([768]),
-    "N": sb([768]), "TN": sb([800], B16), "TW": sb([1568]), "TB": sb([1568], B16),
-    "Di": sb([384], I32), "Df": sb([384]), "tiei": sb([4, 32], I32), "ENDS": sb([4, 8]), "CH": sb([16, 16], U16),
+    "EQ": sb([768], B16), "PR": sb([768], H16), "P": sb([384], B16), "Wl": sb([4, 144], B16), "M": sb([800]), "VI": sb([768]),
+    "N": sb([768]), "TN": sb([768], B16), "TW": sb([1568]),
+    "Di": sb([384], I32), "Dh": sb([384], H16), "SC": sb([10, 128], B16), "tiei": sb([4, 32], I32), "ENDS": sb([4, 8]), "CH": sb([16, 16], U16),
     "CH0": sb([272]), "CH1": sb([272]), "AA": sb([512]), "NE": sb([512]), "INC": sb([512]), "KS": sb([512]),
     "IJ": sb([16], I32), "ON": sb([128]), "AM": sb([128]), "LF": sb([144]), "POSX": sb([128]), "q3": sb([2, 8, 16]),
     "ON2": sb([128]), "POS2": sb([128]), "CODE": sb([128]), "CODW": sb([128]), "TIE": sb([128]), "RS16": sb([128]),
     "RS8": sb([128]), "t1": sb([128]), "t2": sb([128]), "t3": sb([32]), "t4": sb([128]), "t5": sb([128]), "t6": sb([256]),
     "t7": sb([256]), "KW": sb([128]), "Si": sb([56], I32), "Wv": sb([16, 8], I32), "KM": sb([128]),
-    "KP": sb([8]), "cm": sb([8]), "u1": sb([16]), "u2": sb([16]), "u3": sb([32]),
+    "KP": sb([8]), "cm": sb([8]), "u1": sb([64]),
     "RM": sb([144]), "Ri": sb([192], I32), "RF": sb([96]), "RL": sb([96], U16),
-    "NB": sb([240]), "BV": sb([144]), "ZV": sb([96]), "TS": sb([48], U16), "TK": sb([144]),
+    "NB": sb([192]), "DV": sb([3, 48]), "BV": sb([3, 48]), "ZV": sb([96]), "TS": sb([48], U16), "TK": sb([144]),
     "IX": sb([144]), "E": sb([8, 4, 16], B16),
     "LS0": sb([4, 128], U16), "LS1": sb([4, 128], U16), "SB0": sb([128], U16), "SB1": sb([128], U16),
     "L": sb([480], U16),
     "SV0": sb([4, 56], H16), "SV1": sb([4, 56], H16), "LV0": sb([4, 56], H16), "LV1": sb([4, 56], H16),
-    "UY0": sb([16], U16), "LY0": sb([4, 16], U16), "UX0": sb([112], U16), "LX0": sb([4, 112], U16), "HX0": sb([112], U16),
-    "UY1": sb([16], U16), "LY1": sb([4, 16], U16), "UX1": sb([112], U16), "LX1": sb([4, 112], U16),
+    "UX0": sb([128], U16), "LX0": sb([4, 128], U16), "HX0": sb([128], U16), "PM": sb([128]),
+    "UY1": sb([16], U16), "LY1": sb([4, 16], U16), "UX1": sb([64], U16), "LX1": sb([4, 64], U16),
+    "UZ1": sb([48], U16), "LZ1": sb([4, 48], U16),
     "UL": sb([4, 128], U16), "YTf": sb([4, 4, 8]),
     "YB": sb([48]), "UB": sb([48], U16), "HB": sb([48], U16), "LB": sb([4, 48], U16),
     "ci": sb([16], I32), "cf": sb([40]), "cn": sb([896]),
-    "PK": sb([4], U16), "WM": sb([10], U16), "WP": sb([12], U16), "WT": sb([10], U16), "AL": sb([32], U16),
+    "PK": sb([4], U16), "WM": sb([14], U16), "WT": sb([10], U16), "AL": sb([32], U16),
     "BL": sb([32], U16), "BJ": sb([8], U16), "VL": sb([8], U16), "SL": sb([16], U16), "LL": sb([6, 8], U16),
-    "XL": sb([16], U16), "MK0": sb([4, 16]), "Hs": sb([128], B16), "Sel": sb([4, 128], H16), "Gs": sb([2, 8], B16),
-    "Gf": sb([8]), "Wa": sb([128], B16), "Wc": sb([128]), "ID": sb([128]), "RC": sb([64]),
+    "XL": sb([16], U16), "MK0": sb([4, 16]), "Hs": sb([128], B16), "Sel": sb([4, 128], B16), "Gs": sb([2, 8], B16),
+    "Gf": sb([8]), "Wa": sb([128], B16), "Wc": sb([128], B16), "ID": sb([128]), "RC": sb([64]),
     "Qp": ("psum", [128, 1024], F), "PV": ("psum", [128, 512], F), "VS": ("psum", [128, 512], F),
     "KE": ("psum", [128, 1024], F), "Dp": ("psum", [128, 1024], F),
 }
 DSEMS = ["d%d" % k for k in range(20)]
-ARR = ["E0", "E1", "V0", "V1", "Y0", "X0", "Y1", "X1", "B", "hX0", "hB"]
+ARR = ["E0", "E1", "V0", "V1", "X0", "Y1", "X1", "Z1", "B", "hX0", "hB"]
 SEMAPHORES = ["sg", "sv", "ss", "st", "ls"] + DSEMS + ["a" + k for k in ARR]
-BLOCKS = [[(0, 0, 8), (0, 8, 16), (0, 16, 24), (0, 24, 36), (0, 36, 48)] + [(b, c, c + 24) for b in (1, 2, 3) for c in (0, 24)],
-          [(0, 0, 8), (0, 8, 24), (0, 24, 48), (1, 0, 24), (1, 24, 48), (2, 0, 24), (2, 24, 48), (3, 0, 24), (3, 24, 40), (3, 40, 48)]]
+BLOCKS = [(0, 0, 8), (0, 8, 32), (1, 0, 32), (2, 0, 32), (3, 0, 32), (0, 32, 48), (1, 32, 48), (2, 32, 48), (3, 32, 40), (3, 40, 48)]
 CYC, PEC, HOP, DMA, FAR = 0.00085, 0.0005, 0.15, 2.0, 3.2
-SLOW = {"fl": 8.0, "m0": 0.8, "T0": 1.2, "T1": 1.2, "win0": 0.8}
+SLOW = {"fl": 8.0, "m0": 0.8, "m1": 6.0, "T0": 1.2, "T1": 1.2, "win0": 0.8}
 
 
 def helpers(T, topo):
@@ -85,7 +85,7 @@ def bcast(g, T, topo, me, src, dsts, name):
     return neng(topo, me, cs)
 
 
-def schedule(ops, pre):
+def schedule(ops, pre, setup, chain):
     n_ops = len(ops)
     post = [dict() for op in ops]
     for n in range(n_ops):
@@ -117,6 +117,9 @@ def schedule(ops, pre):
     for n in sorted(range(n_ops), key=lambda n: -start[n] - ops[n]["dur"]):
         rank[n] = min([rank[m] - post[n][m] for m in post[n]] + [0.0]) - ops[n]["dur"]
     for turn in range(2):
+        for n in range(setup):
+            if ops[n]["dur"] > 0.1:
+                rank[n] = min(rank[n], rank[chain] + 1e-4 * n)
         start = lay(pre, post, rank)
         span = max(start[n] + ops[n]["dur"] for n in range(n_ops))
         if best is None or span < best[0]:
@@ -221,8 +224,15 @@ def rank_program(g, core, T, topo):
         rec("v", lambda: g.vector.tensor_tensor(out[0], a[0], b[0], op), regs(a, b), regs(out),
             f=fac(a, 1.0 if "psum" in (SCRATCH[a[1][0][0]][0], SCRATCH[b[1][0][0]][0]) else 2.0))
 
+    aside = [False]
+
+    def floats(*xs):
+        return aside[0] and all(len(x) == 2 and SCRATCH[x[1][0][0]][2] in (F, B16) for x in xs)
+
     def ts(out, a, s1, op0, s2=None, op1=None):
-        if s2 is None:
+        if floats(out, a) and (op0, op1) in ((A.mult, A.add), (A.mult, None), (A.add, None)):
+            act(out, a, scale=s1 if op0 == A.mult else 1.0, bias=s1 if op0 == A.add else 0.0 if s2 is None else s2)
+        elif s2 is None:
             rec("v", lambda: g.vector.tensor_scalar(out[0], a[0], val(s1), None, op0), regs(a, s1), regs(out), f=fac(a))
         else:
             rec("v", lambda: g.vector.tensor_scalar(out[0], a[0], val(s1), val(s2), op0, op1), regs(a, s1, s2), regs(out))
@@ -244,8 +254,8 @@ def rank_program(g, core, T, topo):
         rec("t", lambda: g.tensor.matmul(out[0], l[0], r[0], st, sp), regs(l, r), regs(out),
             f=4.0 if SCRATCH[l[1][0][0]][2] == F else 1.0)
 
-    def iota(out, pat, base):
-        rec("g", lambda: g.iota(out[0], pat, base, 0, allow_small_or_imprecise_dtypes=True), [], regs(out))
+    def iota(out, pat, base, step=0):
+        rec("g", lambda: g.iota(out[0], pat, base, step, allow_small_or_imprecise_dtypes=True), [], regs(out))
 
     def dma(q, out, in_, group, also=None):
         if group not in groups:
@@ -313,45 +323,47 @@ def rank_program(g, core, T, topo):
     dma("y", R("Di", p=(0, 16)), T.par[2 * o:2 * o + 2, :], "in")
     dma("s", R("Di", p=(16, 32)), T.res[2 * o:2 * o + 2, 0:S], "in")
     dma("y", R("tiei"), T.tie[:], "tie")
-    dma("s", R("Di", p=(32, 48)), T.res[2 * o:2 * o + 2, S:2 * S], "in2")
+    dma("s", R("Di", p=(32, 48)), T.res[2 * o:2 * o + 2, S:2 * S], "in")
     pi = C("ci", 8, 9)
+    iota(C("t6", 0, 128), [[0, 4], [8, 2], [16, 16]], 0, -1)
     rec("g", lambda: g.iota(pi[0], [[1, 1]], 0, 1), [], regs(pi))
-    ms(C("Yw", 768, 1536), 0.0)
-    ms(C("Win", 0, 1024), 0.0)
-    iota(C("Win", 1024, 1536), [[1, 512]], 0)
-    act(C("Win", 1536, 2304), C("Yw", 768, 1536))
-    act(C("Win", 2304, S), C("Yw", 768, 1536))
-    cp(R("Df", p=(0, 32)), R("Di", p=(0, 32)))
-    cp(R("Df", p=(32, 48)), R("Di", p=(32, 48)))
-    line[0] = "y"
-    for row in range(2):
-        for b in range(4):
-            dma("ys"[b % 2], R("Win", p=rows(b, row)), R("Df", p=(16 * row, 16 * row + 16)), "win0")
-    act(C("M", 0, 768), C("Yw", 768, 1536))
-    ms(C("M", 768, 800), 0.0)
-    for row in range(3):
-        for z in range(8):
-            x = 16 * row + 8 * (z % 2) + 2 * (z // 2)
-            dma("y", C("M", 16, 784, p=(16 * z + row, 16 * z + row + 1)), R("Df", p=(x, x + 2)), "m0")
+    iota(C("t6", 128, 256), [[2, 4], [8, 2], [16, 16]], 0, -1)
+    ms(C("Yw", 1024, 1536), 0.0)
+
+    def fill(out, c):
+        act(out, C("Yw", 1536 - len(out[1][0][5]), 1536), bias=c)
+    banks = [C(nm, z, z + 384) for nm, z in (("KE", 0), ("KE", 512), ("PV", 0), ("VS", 0), ("Dp", 0), ("Dp", 512), ("Qp", 0), ("Qp", 512))]
+
+    for c in range(10):
+        ts(R("SC", c, p=(0, 48)), C("t6", 128 * (c // 8), 128 * (c // 8) + 128, p=(0, 48)), -float(c % 8), A.is_equal)
+    dh = R("Dh", p=(0, 48))
+    ts(dh, R("Di", p=(0, 48)), -MID, A.add)
+    for c in range(8):
+        mm(banks[c], R("SC", c, p=(0, 48)), dh, True, True)
+        (cp if c % 2 else act)(C("Win", 384 * c, 384 * c + 384), banks[c])
+    for z in range(2):
+        mm(banks[z], R("SC", 8 + z, p=(0, 48)), dh, True, True)
+        for c0 in range(0, 384, 128):
+            act(C("M", 16 + 384 * z + c0, 144 + 384 * z + c0), C("KE", 512 * z + c0, 512 * z + c0 + 128))
     for j in range(4):
-        dma("y", C("W0", 768 * j, 768 * j + 768), T.fl[:, 768 * j:768 * j + 768], "fl", C("Win", 0, 8))
-    line[0] = None
+        dma("y", C("W0", 768 * j, 768 * j + 768), T.fl[:, 768 * j:768 * j + 768], "fl", R("Di", p=(0, 48)))
     for k, (sh, mk) in enumerate(((3, 1), (0, 7), (0, 15), (4, 1), (0, 1), (5, 3), (4, 7), (0, 127))):
         ts(C("ci", k, k + 1), pi, sh, A.logical_shift_right, mk, A.bitwise_and)
     cp(C("cf", 0, 8), C("ci", 0, 8))
     ms(R("PK"), 0)
     ms(R("CH"), 0)
-    ms(R("X"), 0.0)
+    fill(R("X"), 0.0)
     tt(cf(8), cf(3), cf(4), A.not_equal)
     ts(cf(10), cf(8), 144.0, A.mult)
     ts(cf(11), cf(1), 16.0, A.mult, cf(10), A.add)
     for t in range(2):
         ts(C("PK", 2 * t, 2 * t + 1), cf(0), 1.0 + t, A.mult, cf(11), A.add)
-        ms(R("CH%d" % t), 0.0)
+        fill(R("CH%d" % t), 0.0)
     for b in range(4):
         cp(R("ENDS", p=blk(b)), R("tiei", sl(0, 4), sl(8 * b, 8 * b + 8), p=blk(o)))
-    ms(C("cn", 0, 16), 0.0)
-    ms(C("cn", 136, 160), 128.0)
+    aside[0] = True
+    fill(C("cn", 0, 16), 0.0)
+    fill(C("cn", 136, 160), 128.0)
     iota(C("cn", 16, 136), [[1, 4], [8, 15], [4, 2]], 0)
     tr(C("TW", 0, 128), C("cn", 16, 144))
     tr(C("TW", 128, 288), C("cn", 0, 160))
@@ -385,22 +397,21 @@ def rank_program(g, core, T, topo):
     cp(R("XL"), C("t1", 16, 32))
     ts(cf(12), cf(8), 784.0, A.mult)
     ts(cf(13), cf(2), 16.0, A.mult, cf(12), A.add)
-    ts(C("WM", 0, 9), pattern([[1, 3], [256, 3]], 0), cf(13), A.add)
-    ts(C("WT", 0, 9), pattern([[0, 3], [256, 3]], 0), cf(13), A.add)
-    ts(C("WP", 0, 9), C("WM", 0, 9), 1.0, A.add)
-    ms(R("INC"), 1.0)
-    ms(R("INC", sl(0, 512, 64)), -1000.0)
+    ts(C("WM", 4, 10), pattern([[1, 2], [256, 3]], 1), cf(13), A.add)
+    ts(C("WT", 0, 3), C("WM", 4, 7), -1.0, A.add)
+    fill(R("INC"), 1.0)
+    fill(R("INC", sl(0, 512, 64)), -1000.0)
     for nm, step in (("RS16", 16), ("RS8", 8)):
-        ms(R(nm), 1.0)
-        ms(R(nm, sl(0, SCRATCH[nm][1][1], step)), 0.0)
+        fill(R(nm), 1.0)
+        fill(R(nm, sl(0, 128, step)), 0.0)
     iota(C("POSX", 64, 128), [[1, 8], [0, 8]], 1)
     iota(C("POSX", 0, 64), [[8, 8], [0, 8]], 8)
     p8 = pattern([[0, 8], [1, 8]], 1)
     for sd, (a, c) in enumerate(((8.0, 8.0), (1.0, 0.5))):
         ts(R("q3", 0, sl(0, 8), sl(8 * sd, 8 * sd + 8)), p8, a, A.mult)
         ts(R("q3", 1, sl(0, 8), sl(8 * sd, 8 * sd + 8)), p8, c, A.mult)
-    cp(R("POS2"), R("q3", 0))
-    cp(R("CODE"), R("q3", 1))
+    act(R("POS2"), R("q3", 0))
+    act(R("CODE"), R("q3", 1))
     ts(R("CODW"), R("CODE"), 1.0 / 64.0, A.mult)
     ts(cf(16), cf(5), 128.0, A.mult, cf(2), A.add)
     iota(R("TIE"), [[16, 8], [0, 16]], 0)
@@ -410,61 +421,79 @@ def rank_program(g, core, T, topo):
     iota(R("VI"), [[1, 768]], -ZC)
     ts(cf(9), cf(5), 768.0, A.mult)
     act(R("VI"), R("VI"), bias=cf(9))
-    ts(bus("BV", 1), pattern([[16, 48]], 0), cf(9), A.add, cf(2), A.add)
-    ts(bus("ZV", 0), bus("BV", 1), -1.0, A.mult, float(ZC), A.add)
-    for nm, a, b, c in (("P", 0, 16, 0.0), ("P", 784, 800, 0.0), ("LF", 120, 144, 0.0), ("P2", 0, 16, 0.0), ("P2", 784, 800, 0.0),
-                        ("TN", 0, 16, 0.0), ("TN", 784, 800, 0.0), ("XT", 0, 16, 0.0), ("XT", 272, 288, 0.0),
+    ts(cf(31), cf(2), cf(9), A.add)
+    ts(R("BV", 1), pattern([[16, 48]], 0), cf(31), A.add)
+    ts(bus("ZV", 0), R("BV", 1), -1.0, A.mult, float(ZC), A.add)
+    for nm, a, b, c in (("M", 0, 16, 0.0), ("M", 784, 800, 0.0), ("LF", 120, 144, 0.0),
+                        ("XT", 0, 16, 0.0), ("XT", 272, 288, 0.0),
                         ("W0", ZC, NEG, 0.0), ("W1", ZC, NEG, 0.0)):
-        ms(C(nm, a, b), c)
-    act(C("CW", 1024, 1536), C("Yw", 1024, 1536), bias=-1.0)
+        fill(C(nm, a, b), c)
+    fill(C("CW", 1024, 1536), -1.0)
     ms(R("Wv"), 0)
     ts(R("Gf"), c8, cf(6), A.is_equal)
-    cp(R("Gs", 0), R("Gf"))
+    act(R("Gs", 0), R("Gf"))
     ts(R("Gs", 1), R("Gf"), 128.0, A.mult)
-    ts(R("ID"), pattern([[1, 128]], 0), cf(7), A.is_equal)
-    for nm in ("Wa", "Wc"):
-        ms(R(nm), 0.0)
-    ts(cf(27), cf(1), 1.0, A.add)
-    ts(cf(28), cf(0), 512.0, A.mult, -1024.0, A.add)
-    ts(cf(29), cf(0), -1024.0, A.mult, 512.0, A.add)
-    ts(cf(30), cf(1), 0.0, A.is_gt)
-    for nm, r, c in (("Wa", 0, 27), ("Wa", 1, 28), ("Wa", 2, 30), ("Wa", 3, 29), ("Wc", 0, 19)):
-        ts(R(nm, sl(r, 128, 16)), R("Gf"), cf(c), A.mult)
-    sel = pattern([[16, 4], [1000, 2], [1, 16]], 0)
+    ones = {F: R("t4"), B16: R("VT", 0, 0)}
+    for x in ones.values():
+        fill(x, 1.0)
+
+    def picker(out, pat, base):
+        one = ones[SCRATCH[out[1][0][0]][2]]
+        rec("g", lambda: g.affine_select(out[0], one[0], pat, A.is_equal, 0.0, base, -1), regs(one), regs(out))
+    picker(R("ID"), [[1, 128]], 0)
     for u in range(2):
         for h in range(2):
-            ts(R("Sel", 2 * u + h), sel, cf(7), A.subtract, 1000.0 * h - 64.0 * u, A.is_equal)
+            picker(R("Sel", 2 * u + h), [[16, 4], [1000, 2], [1, 16]], 64 * u - 1000 * h)
+    picker(R("PM"), [[16, 2], [32, 4], [1, 16]], 0)
+    for x in [R("Wa"), R("Wc")] + [R("Wl", k) for k in range(4)]:
+        fill(x, 0.0)
+    ts(cf(27), cf(1), 1.0, A.add)
+    ts(cf(28), cf(0), 512.0, A.mult, -1024.0, A.add)
+    ts(cf(29), cf(2), 0.0, A.is_equal)
+    ts(cf(30), cf(1), 0.0, A.is_gt)
+    ts(R("Wa", sl(0, 128, 16)), R("Gf"), cf(27), A.mult)
+    ts(R("Wc", sl(0, 128, 16)), R("Gf"), -1.0, A.mult)
+    for k, c in enumerate((cf(28), cf(30), 1.0, cf(29))):
+        ts(R("Wl", k, sl(15, 143, 16)), R("Gf"), c, A.mult)
+
+    def listed(out, k, src, c0=0, c1=48):
+        for r in range(16):
+            mm(out, R("Wl", k, sl(15 - r, 143 - r)), R(src, sl(16 * c0 + r, 16 * c1, 16)), r == 0, r == 15)
     ts(cf(17), cf(3), -16.0, A.mult, cf(7), A.add)
-    ts(R("t2"), sel, 500.0, A.is_gt)
-    ts(R("Hs"), R("t2"), cf(3), A.is_equal)
+    ts(R("Hs"), pattern([[0, 4], [1, 2], [0, 16]], 0), cf(3), A.is_equal)
     ts(R("MK0"), pattern([[32, 4], [1, 16]], 0), cf(17), A.is_equal)
     wrap768("M", "TW", 128)
-    act(R("RM"), ind(R("TW"), C("WM", 0, 9)))
-    ts(bus("BV", 2), bus("RM", 0), float(NEG - ZC), A.add)
+    act(bus("RM", 1, 2), ind(R("TW"), C("WM", 4, 10)), bias=MID)
+    act(R("BV", 2), ind(R("TW"), C("WT", 0, 3)), bias=NEG - ZC + MID)
     ts(R("RF"), bus("RM", 1, 2), 1024.0, A.add)
     cp(bus("Ri", 0, 2), bus("RM", 1, 2))
     ts(bus("Ri", 2, 2), bus("Ri", 0, 2), 7, A.logical_shift_right)
     ts(bus("TK", 0, 2), bus("Ri", 2, 2), 128.0, A.mult)
     tt(bus("IX", 0, 2), bus("TK", 0, 2), bus("RM", 1, 2), A.add)
+    line[0] = "vst"
     cp(R("RL"), bus("IX", 0, 2))
+    line[0] = None
+    aside[0] = False
 
     def update(t, W, dst):
-        for nm, c0, c1, n in (("Y%d" % t, 0, 16, n_direct), ("X%d" % t, 16, 128, n_direct if t else n_relay)):
-            arrive(nm, n, "L" + nm)
+        for nm, c0, c1 in ((("Y1", 0, 16), ("X1", 16, 80), ("Z1", 80, 128)) if t else (("X0", 0, 128),)):
+            arrive(nm, n_direct if t else n_relay, "L" + nm)
             place(lambda k, b: R("UL", b, sl(c0, c1), p=blk(k)), lambda b: R("U" + nm, p=blk(b)),
                   lambda k, b: R("L" + nm, k, p=blk(b)))
         for sd in range(2):
             for b in range(4):
                 act(C("Yw", 512 * sd + 128 * b, 512 * sd + 128 * b + 128), ind(R(W), R("UL", b, sl(8 * sd, 8 * sd + 8))))
-        for b, c0, c1 in BLOCKS[t]:
+        for b, c0, c1 in BLOCKS:
             x0, x1 = 768 * b + 16 * c0, 768 * b + 16 * c1
-            act(C("Yg", x0, x1), ind(R("Yw"), R("UL", b, sl(32 + c0, 32 + c1))))
-            tt(C(dst, x0, x1), ind(R(W), R("UL", b, sl(80 + c0, 80 + c1))), C("Yg", x0, x1), A.add)
+            iy, ix = (16, 48) if c0 < 32 else (64, 80)
+            act(C("Yg", x0, x1), ind(R("Yw"), R("UL", b, sl(iy + c0, iy + c1))))
+            tt(C(dst, x0, x1), ind(R(W), R("UL", b, sl(ix + c0, ix + c1))), C("Yg", x0, x1), A.add)
             if t:
                 dma("y", T.yf[:, x0:x1], C(dst, x0, x1), "out")
         for sd in range(2):
-            cp(R("YTf", 2 * t + sd), C("UL", 0, 4, sl(16 + 8 * sd, 24 + 8 * sd)))
+            cp(R("YTf", 2 * t + sd), C("UL", 0, 4, sl(80 + 8 * sd, 88 + 8 * sd)))
 
+    marks = [len(ops)]
     for t in range(2):
         W, CHf = "W%d" % t, "CH%d" % t
         wn = C(W, 0, NEG)
@@ -479,16 +508,18 @@ def rank_program(g, core, T, topo):
                 tr(R("TT", y, sl(0, 128)), R("X", sd, sl(16, 144)))
                 tr(R("TT", y, sl(128, 288)), R("X", sd))
                 if s < 6:
-                    cp(R("CH", 8 * sd + s + 1), ind(R("TT", y), pk))
+                    ts(R("CH", 8 * sd + s + 1), ind(R("TT", y), pk), MID, A.add)
                 z = 16 * (8 * sd + s + 1)
-                act(C(CHf, z, z + 16), ind(R("TT", y), pk))
+                act(C(CHf, z, z + 16), ind(R("TT", y), pk), bias=MID)
         chw = C(CHf, 0, 256)
         for hf in range(2):
-            act(C("AA", 256 * hf, 256 * hf + 256), ind(C(CHf, 0, 128), C("AL", 16 * hf, 16 * hf + 16)))
+            (cp if hf else act)(C("AA", 256 * hf, 256 * hf + 256), ind(C(CHf, 0, 128), C("AL", 16 * hf, 16 * hf + 16)))
+        ops[-1]["after"].update((len(ops) - 5, len(ops) - 4))
         act(R("AM"), ind(chw, R("VL")), bias=-float(ZC))
         for hf in range(2):
             tt(C("NE", 256 * hf, 256 * hf + 256), ind(chw, C("BL", 16 * hf, 16 * hf + 16)), C("AA", 256 * hf, 256 * hf + 256), A.not_equal)
-        scan(R("KS"), R("INC"), R("NE"), 0.0, A.add, A.mult)
+        for hf in range(2):
+            scan(*[C(nm, 256 * hf, 256 * hf + 256) for nm in ("KS", "INC", "NE")], 0.0, A.add, A.mult)
         ts(C("IJ", 0, 8), R("KS", sl(63, 512, 64)), 0.0, A.max)
         ts(C("IJ", 8, 16), C("IJ", 0, 8), 7, A.bitwise_and)
         ts(C("LF", 56, 64), C("IJ", 0, 8), -float(ZC), A.add)
@@ -499,22 +530,21 @@ def rank_program(g, core, T, topo):
         ts(R(sbf), ind(R("LF"), C("SL", 0, 8)), float(ZC), A.add)
         send("E%d" % t, C(sbf, 0, 120), [(cores[k], T[ls][:, o, 0:120]) for k in peers])
         if t == 0:
-            for b in range(4):
-                dma("y", R("Win", p=rows(b, 2)), R("Df", p=(32, 48)), "res1")
+            marks.append(len(ops) - 1)
         else:
             update(0, "W0", "W1")
         act(C("XT", 16, 144), ind(R("LF"), T1L))
+        act(C("XT", 144, 272), ind(chw, PVL), bias=-MID)
         act(R("n1"), ind(C(CHf, 16, 272), VL2))
 
         def spread():
-            act(R("TP"), ind(C("PR", 0, 544), R("XL")))
+            act(R("TP"), ind(C("TW", 0, 544), R("XL")))
             for b in range(4):
                 for b2 in range(4):
                     dma("y", C("T12", 256 * b, 256 * b + 256, p=blk(b2)), R("TP", p=blk(b)), "T%d" % t)
-        kept = [lambda: tt(C("XT", 144, 272), ind(chw, PVL), R("n1"), A.subtract),
+        kept = [lambda: tr(C("TW", 0, 256), C("XT", 16, 272)),
+                lambda: tr(C("TW", 256, 544), R("XT")),
                 lambda: tt(R("t1"), ind(C(CHf, 24, 272), VL2), R("TIE"), A.not_equal),
-                lambda: tr(C("PR", 0, 256), C("XT", 16, 272)),
-                lambda: tr(C("PR", 256, 544), R("XT")),
                 lambda: tt(R("ON2"), ind(R("IJ"), BJ2), R("POS2"), A.is_ge),
                 lambda: tt(R("t2"), R("t1"), R("ON2"), A.mult),
                 lambda: tt(R("t4"), R("ON2"), R("CODW"), A.mult),
@@ -530,16 +560,16 @@ def rank_program(g, core, T, topo):
         arrive("E%d" % t, n_direct, ls)
         place(lambda k, b: R("L", sl(b, 480, 4), p=blk(k)), lambda b: C(sbf, 0, 120, p=blk(b)),
               lambda k, b: R(ls, k, sl(0, 120), p=blk(b)))
-        seq = list(range(7, 14)) + list(range(7))
+        seq = list(range(7, 14)) + list(range(6, -1, -1))
         dq = [C(("Qp", "KE")[ch // 2], 512 * (ch % 2), 512 * (ch % 2) + 128) for ch in range(4)]
 
         def gather(ch):
             cut = 7 - CUT[t][ch]
-            for p0, p1 in ((7, 10), (10, 14)):
-                act(xx(ch, p0, p1 - p0), ind(wn, lst(ch, 1 + p0, p1 - p0)), scale=-1.0, bias=0.0625)
-            for p0, p1 in ((0, min(cut, 3)), (3, cut)):
+            for p0, p1 in ((0, min(cut, 4)), (4, cut)):
                 if p0 < p1:
                     act(xx(ch, p0, p1 - p0), ind(wn, lst(ch, p0, p1 - p0)), bias=-0.0625)
+            for p0, p1 in ((7, 10), (10, 14)):
+                act(xx(ch, p0, p1 - p0), ind(wn, lst(ch, 1 + p0, p1 - p0)), scale=-1.0, bias=0.0625)
             act(R("RR", ch), ind(R("RC"), lst(ch, 7)))
 
         def share(ch, p0, p1):
@@ -550,8 +580,10 @@ def rank_program(g, core, T, topo):
                 mm(dq[ch], R("ID"), xx(ch, x), n == 0, n == NPE[ch] - 1)
 
         def limit(ch):
-            return [lambda x=x: tt(dq[ch], dq[ch], xx(ch, x), A.add) for x in seq[NPE[ch]:]] + \
-                   [lambda: tt(dq[ch], dq[ch], R("RR", ch), A.mult)]
+            mine, part, last = seq[NPE[ch]:], C("VS", 0, 128), R("t6", sl(0, 128))
+            return [lambda: tt(part, xx(ch, mine[0]), xx(ch, mine[1]), A.add)] + \
+                   [lambda x=x: tt(part if x != mine[-1] else last, part, xx(ch, x), A.add) for x in mine[2:]] + \
+                   [lambda: tt(dq[ch], dq[ch], last, A.add), lambda: tt(dq[ch], dq[ch], R("RR", ch), A.mult)]
 
         def compare(ch):
             return [lambda x=x: tt(R("VT", ch, x), xx(ch, x), dq[ch], A.is_ge if x > 6 else A.is_le)
@@ -569,28 +601,30 @@ def rank_program(g, core, T, topo):
                 for y in fill[n * len(fill) // len(chain):(n + 1) * len(fill) // len(chain)]:
                     y()
         line[0] = "vst"
-        for ch in range(3):
+        for ch in range(2):
             gather(ch)
         ones = [share(ch, p, p + 1) for ch in (1, 2) for p in range(7 - CUT[t][ch], 7)]
-        weave([share(0, 0, 3), share(0, 3, 7)] + ones[:EARLY], [])
         sums(0)
-        weave(limit(0), ones[EARLY:] + kept)
+        weave([share(0, 4, 7), share(0, 2, 4)], [])
+        weave(limit(0), [share(0, 1, 2), share(0, 0, 1)] + kept[:2] + ones)
+        del kept[:2]
         if t == 1:
             spread()
+        gather(2)
         gather(3)
         sums(1)
         sums(2)
-        weave(limit(1), compare(0))
-        count(0)
-        sums(3)
-        for ch in (1, 2):
+        for ch in range(3):
             weave(limit(ch + 1), compare(ch))
             count(ch)
+            if ch == 0:
+                sums(3)
         weave(compare(3), [])
         count(3)
-        line[0] = None
         sv, lv = "SV%d" % t, "LV%d" % t
         ts(R(sv), C("PV", 0, 224), -OFS, A.add)
+        sent_votes = len(ops) - 1
+        line[0] = None
 
         def send_votes(sv=sv, lv=lv, t=t):
             trs = []
@@ -606,32 +640,30 @@ def rank_program(g, core, T, topo):
         for j in range(8):
             act(C(W, NEG + 384 * j, NEG + 384 * j + 384), C(W, 384 * j, 384 * j + 384), scale=-1.0)
         halves = [(384 * z, 512 * z) for z in range(2)]
+        rl = {c0: C("RL", 48 * t + c0 // 16, 48 * t + c0 // 16 + 24) for c0, z in halves}
+        for x in kept:
+            x()
+            ops[-1]["after"].add(sent_votes)
         for c0, z in halves:
-            rl = C("RL", 48 * t + c0 // 16, 48 * t + c0 // 16 + 24)
-            act(C("Dp", z, z + 384), C("VI", c0, c0 + 384))
-            act(C("Yg", c0, c0 + 384), ind(R("T12"), rl))
-            act(C("Yg", 768 + c0, 1152 + c0), ind(C("T12", 128, 1024), rl))
-            act(C("Qp", z, z + 384), C("Yg", 768 + c0, 1152 + c0))
-        for c0, z in halves:
-            tt(C("EQ", c0, c0 + 384), C("Yg", c0, c0 + 384), C("Dp", z, z + 384), A.is_equal)
+            tt(C("EQ", c0, c0 + 384), ind(R("T12"), rl[c0]), C("VI", c0, c0 + 384), A.is_equal)
+            ops[-1]["after"].add(sent_votes)
             mm(C("Dp", z, z + 384), R("Wa"), C("EQ", c0, c0 + 384), True, True)
-            act(C("P", 16 + c0, 400 + c0), C("Dp", z, z + 384))
+        act(R("P"), C("Dp", 0, 384))
+        listed(C("KE", 0, 48), 0, "EQ")
+        tt(R("BV", 0), C("KE", 0, 48), bus("RF", t), A.add)
+        cp(R("TS"), R("BV", 0))
+        act(R("DV", 0), C("KE", 0, 48), scale=-2.0, bias=-1536.0)
+        listed(C("KE", 512, 560), 1, "EQ")
         for c0, z in halves:
-            tt(C("PR", c0, c0 + 384), C("Qp", z, z + 384), C("EQ", c0, c0 + 384), A.mult)
-            mm(C("Qp", z, z + 384), R("Wc"), C("PR", c0, c0 + 384), True, True)
-            act(C("P2", 16 + c0, 400 + c0), C("Qp", z, z + 384))
-        wrap768("P", "TB")
-        act(bus("NB", 0, 3), ind(R("TB"), C("WP", 0, 9)))
-        tt(bus("BV", 0), bus("NB", 0), bus("RF", t), A.add)
-        cp(R("TS"), bus("BV", 0))
-
-        def turned_source():
-            wrap768("P2", "TW", 192)
-            act(bus("NB", 4), ind(R("TW"), C("WT", 0, 3)))
-            tt(bus("ZV", 1), bus("NB", 4), bus("BV", 2) if t == 0 else bus("IX", 2), A.add)
-            tt(bus("ZV", 1), bus("ZV", 1), bus("NB", 1), A.mult)
-            tt(bus("NB", 3), bus("ZV", 1), bus("ZV", 0), A.add)
-        turned_source()
+            tt(C("PR", c0, c0 + 384), ind(C("T12", 128, 1024), rl[c0]), C("EQ", c0, c0 + 384), A.mult)
+            if t == 0:
+                mm(C("Qp", z, z + 384), R("Wc"), C("PR", c0, c0 + 384), True, False)
+                mm(C("Qp", z, z + 384), R("SC", 8 + z // 512, p=(0, 16)), R("Dh", p=(0, 16)), False, True)
+        listed(C("PV", 0, 48), 2, "PR")
+        act(bus("NB", 0), C("PV", 0, 48), bias=NEG - ZC + MID)
+        tt(bus("ZV", 1), C("KE", 512, 560), bus("NB", 0), A.mult)
+        tt(R("DV", 1), bus("ZV", 1), bus("ZV", 0), A.add)
+        tt(R("DV", 2), bus("NB", 0), R("BV", 2) if t == 0 else bus("IX", 2), A.subtract)
         arrive("V%d" % t, sum(len(topo.engines(cores[k], core)) // 4 for k in peers), lv)
         for u in range(2):
             n = 0
@@ -657,11 +689,14 @@ def rank_program(g, core, T, topo):
                 mm(C("KE", 512 * sd + 128 * b, 512 * sd + 128 * b + 128), R("Hs"), C("E", 0, 8, b), True, True)
         act(C("CW", 512, 1024), C("KE", 512, 1024), bias=0.5, scale=-2.0)
         ts(C("CW", 0, 512), C("KE", 0, 512), 0.125, A.mult, 0.5, A.add)
-        uy, ux = "UY%d" % t, "UX%d" % t
 
-        def turns():
-            for c0 in (0, 384):
-                tt(C("TN", 16 + c0, 400 + c0), ind(R("CW"), C("TS", c0 // 16, c0 // 16 + 24)), C("P", 16 + c0, 400 + c0), A.is_gt)
+        def turns(c0, c1):
+            out = C("TN", 16 * c0, 16 * c1)
+            if c0 < 24:
+                tt(out, ind(R("CW"), C("TS", c0, c1)), C("P", 16 * c0, 16 * c1), A.is_gt)
+            else:
+                act(C("Yg", 16 * c0, 16 * c1), ind(R("CW"), C("TS", c0, c1)))
+                tt(out, C("Yg", 16 * c0, 16 * c1), C("Dp", 128 + 16 * c0, 128 + 16 * c1), A.is_gt)
 
         def opened():
             tt(R("cm"), ka, kb, A.max)
@@ -669,38 +704,47 @@ def rank_program(g, core, T, topo):
             tt(C("t6", 0, 128), ind(chw, VL2), R("t2"), A.mult)
             scan(C("t7", 0, 128), R("RS16"), C("t6", 0, 128), 0.0, A.mult, A.add)
             ts(C("u1", 0, 8), R("cm"), 0.0, A.is_equal, float(ZC), A.mult)
-            ts(C("u2", 0, 8), R("cm"), 8.0, A.is_ge, float(NEG), A.mult)
-            ts(C("u2", 8, 16), R("KP"), 0.0, A.is_lt, float(NEG), A.mult)
+            ts(C("u1", 16, 24), R("cm"), 8.0, A.is_ge, float(NEG), A.mult)
+            ts(C("u1", 24, 32), R("KP"), 0.0, A.is_lt, float(NEG), A.mult)
             for sd in range(2):
-                tt(C("u3", 8 * sd, 8 * sd + 8), C("u2", 8 * sd, 8 * sd + 8), C("u1", 0, 8), A.add)
-                tt(C("t3", 8 * sd, 8 * sd + 8), C("u3", 8 * sd, 8 * sd + 8), R("t7", sl(15, 128, 16)), A.add)
-            cp(R(uy), C("t3", 0, 16))
-            to_all("Y%d" % t, uy, "LY%d" % t)
+                tt(C("u1", 32 + 8 * sd, 40 + 8 * sd), C("u1", 16 + 8 * sd, 24 + 8 * sd), C("u1", 0, 8), A.add)
+                tt(C("t3", 8 * sd, 8 * sd + 8), C("u1", 32 + 8 * sd, 40 + 8 * sd), R("t7", sl(15, 128, 16)), A.add)
+            if t == 0:
+                cp(C("UX0", 0, 16), C("t3", 0, 16))
+            else:
+                cp(R("UY1"), C("t3", 0, 16))
+                to_all("Y1", "UY1", "LY1")
 
         def ends():
             tt(C("t6", 128, 256), R("n1"), R("t2"), A.mult)
             scan(C("t7", 128, 256), R("RS16"), C("t6", 128, 256), 0.0, A.mult, A.add)
             ts(C("u1", 8, 16), R("cm"), 0.0, A.is_equal)
             for sd in range(2):
-                tt(C("u3", 16 + 8 * sd, 24 + 8 * sd), C("u1", 8, 16), R("ENDS", 2 * t + sd), A.mult)
-            tt(C("t3", 16, 32), C("u3", 16, 32), R("t7", sl(15, 256, 16)), A.add)
-            cp(C(ux, 0, 16), C("t3", 16, 32))
+                tt(C("u1", 48 + 8 * sd, 56 + 8 * sd), C("u1", 8, 16), R("ENDS", 2 * t + sd), A.mult)
+            tt(C("t3", 16, 32), C("u1", 48, 64), R("t7", sl(15, 256, 16)), A.add)
+            cp(C("UX0", 80, 96) if t == 0 else C("UZ1", 0, 16), C("t3", 16, 32))
 
-        def sources():
-            wrap768("TN", "TB")
-            act(R("TK"), ind(R("TB"), C("WT", 0, 9)))
-            for a, k in ((0, 2), (2, 1)):
-                tt(bus("TK", a, k), bus("TK", a, k), bus("NB", 2 + a, k), A.mult)
-                tt(bus("IX", a, k), bus("TK", a, k), bus("BV", a, k) if a == 0 or t == 0 else bus("IX", 2), A.add)
-            cp(C(ux, 16, 112), bus("IX", 0, 2))
+        def sources(part):
+            c0, c1 = (0, 32, 48)[part:part + 2]
+            n, turn = c1 - c0, C(("VS", "PV")[part], 0, c1 - c0)
+            listed(turn, 3, "TN", c0, c1)
+            for k in range(2):
+                tt(C("TK", 2 * c0 + k * n, 2 * c0 + k * n + n), turn, R("DV", k, sl(c0, c1)), A.mult)
+            tt(C("IX", 2 * c0, 2 * c1), C("TK", 2 * c0, 2 * c1), C("BV", 0, 2, sl(c0, c1)), A.add)
+            cp((C("UX0", 16, 80), C("UX0", 96, 128), R("UX1"), C("UZ1", 16, 48))[2 * t + part], C("IX", 2 * c0, 2 * c1))
+            tt(C("TK", 96 + c0, 96 + c1), turn, R("DV", 2, sl(c0, c1)), A.mult)
+
+        def listed_parents():
+            tt(bus("IX", 2), bus("TK", 2), R("BV", 2) if t == 0 else bus("IX", 2), A.add)
 
         def parents():
             for c0, z in halves:
-                tt(C("Qp", z, z + 384), C("Qp", z, z + 384), C("TN", 16 + c0, 400 + c0), A.mult)
+                tt(C("Qp", z, z + 384), C("Qp", z, z + 384), C("TN", c0, c0 + 384), A.mult)
             for c0, z in halves:
-                tt(C("N", c0, c0 + 384), C("Qp", z, z + 384), C("M", 16 + c0, 400 + c0), A.add)
+                tt(C("N", c0, c0 + 384), C("M", 16 + c0, 400 + c0), C("Qp", z, z + 384), A.subtract)
         if t == 0:
-            turns()
+            turns(0, 24)
+            turns(24, 48)
             parents()
             mark = len(ops) - 1
             for z in range(8):
@@ -710,33 +754,37 @@ def rank_program(g, core, T, topo):
             ops[first + 2]["after"].add(mark)
             ends()
             first = len(ops)
-            sources()
-            ops[first]["after"].add(mark)
+            sources(0)
+            ops[first + 16]["after"].add(mark)
+            sources(1)
             relay("X0", "UX0", "HX0")
         else:
             opened()
             mark = len(ops) - 2
-            turns()
-            ops[-2]["after"].add(mark)
+            turns(0, 24)
+            ops[-1]["after"].add(mark)
+            turns(24, 32)
+            sources(0)
+            to_all("X1", "UX1", "LX1")
+            turns(32, 48)
             ends()
-            sources()
-    to_all("X1", "UX1", "LX1")
+            sources(1)
+            to_all("Z1", "UZ1", "LZ1")
+        listed_parents()
     for j in range(3):
         ts(C("XT", 16 + 16 * j, 32 + 16 * j), R("IX", sl(96 + j, 144, 3)), float(ZC - NEG), A.add)
-    tr(C("PR", 0, 64), C("XT", 16, 80))
-    tr(C("PR", 256, 352), C("XT", 0, 96))
-    act(R("YB"), ind(C("PR", 0, 352), C("XL", 0, 3)))
-    cp(R("UB"), R("YB"))
+    tr(C("TW", 0, 64), C("XT", 16, 80))
+    tr(C("TW", 256, 352), C("XT", 0, 96))
+    act(R("YB"), ind(C("TW", 0, 352), C("XL", 0, 3)))
+    mm(C("VS", 0, 48), R("PM"), R("YB"), True, True)
+    cp(R("UB"), C("VS", 0, 48))
     relay("B", "UB", "HB")
     update(1, "W1", "W0")
     dma("y", T.yt[:], R("YTf"), "out")
     arrive("B", n_relay, "LB")
     for k in every:
-        if k != o:
-            cp(bus("TK", peers.index(k)), R("LB", k))
-        for b in range(4):
-            src = R("YB", p=blk(b)) if k == o else C("TK", 48 * peers.index(k), 48 * peers.index(k) + 48, p=blk(b))
-            dma("y", T.yp[2 * k:2 * k + 2, 768 * b:768 * b + 768], src, "out")
+        cp(bus("NB", k), R("LB", k) if k != o else R("UB"))
+        dma("y", T.yp[2 * k:2 * k + 2, :], bus("NB", k), "out")
 
     pre = [dict() for op in ops]
     members, sent = {}, {}
@@ -760,7 +808,7 @@ def rank_program(g, core, T, topo):
     tail = len(ops)
     ops.append({"q": "x", "fn": None, "deps": set(), "after": set(), "kind": "a", "group": "out", "dur": 0.0})
     pre.append({m: DMA for m in members["out"]})
-    order = [n for n in schedule(ops, pre) if n != tail]
+    order = [n for n in schedule(ops, pre, *marks) if n != tail]
 
     need = set(d for op in ops for d in op["deps"] if ops[d]["kind"] == "c")
     cnt = {q: 0 for q in QS}

import numpy as np
from concourse.bass import DstId, RemoteDMATransfer
from concourse.mybir import AluOpType, ActivationFunctionType

S = 3072
ZC = S
NEG = S + 64
WW = NEG + S
NPE = (7, 8, 8, 7)
CUT = ((7, 6, 0, 0), (7, 6, 0, 0))
MID = 1536.0
OFS = 1032.0
F, B16, H16, I32, U16 = "float32", "bfloat16", "float16", "int32", "uint16"


def sb(shape, d=F):
    return ("sbuf", [128] + list(shape), d)


SCRATCH = {
    "W0": sb([WW]), "W1": sb([WW]), "XX": sb([7168]), "VT": sb([4, 14, 128], B16), "RR": sb([4, 128]),
    "Yg": sb([S]), "Yw": sb([1536]), "CW": sb([1536]), "Win": sb([S]), "X": sb([2, 160]), "TT": sb([4, 288]),
    "XT": sb([288]), "TP": sb([256]), "T12": sb([1024]), "n1": sb([128]),
    "EQ": sb([768], B16), "PR": sb([768], H16), "P": sb([384], B16), "Wl": sb([4, 144], B16), "M": sb([800]), "VI": sb([768]),
    "N": sb([768]), "TN": sb([768], B16), "TW": sb([1568]),
    "Di": sb([384], I32), "Dh": sb([384], H16), "SC": sb([10, 128], B16), "tiei": sb([4, 32], I32), "ENDS": sb([4, 8]), "CH": sb([16, 16], U16),
    "CH0": sb([272]), "CH1": sb([272]), "AA": sb([512]), "NE": sb([512]), "INC": sb([512]), "KS": sb([512]),
    "IJ": sb([16], I32), "ON": sb([128]), "AM": sb([128]), "LF": sb([144]), "POSX": sb([128]), "q3": sb([2, 8, 16]),
    "ON2": sb([128]), "POS2": sb([128]), "CODE": sb([128]), "CODW": sb([128]), "TIE": sb([128]), "RS16": sb([128]),
    "RS8": sb([128]), "t1": sb([128]), "t2": sb([128]), "t3": sb([32]), "t4": sb([128]), "t5": sb([128]), "t6": sb([256]),
    "t7": sb([256]), "KW": sb([128]), "Si": sb([56], I32), "Wv": sb([16, 8], I32), "KM": sb([128]),
    "KP": sb([8]), "cm": sb([8]), "u1": sb([64]),
    "RM": sb([144]), "Ri": sb([192], I32), "RF": sb([96]), "RL": sb([96], U16),
    "NB": sb([192]), "DV": sb([3, 48]), "BV": sb([3, 48]), "ZV": sb([96]), "TS": sb([48], U16), "TK": sb([144]),
    "IX": sb([144]), "E": sb([8, 4, 16], B16),
    "LS0": sb([4, 128], U16), "LS1": sb([4, 128], U16), "SB0": sb([128], U16), "SB1": sb([128], U16),
    "L": sb([480], U16),
    "SV0": sb([4, 56], H16), "SV1": sb([4, 56], H16), "LV0": sb([4, 56], H16), "LV1": sb([4, 56], H16),
    "UX0": sb([128], U16), "LX0": sb([4, 128], U16), "HX0": sb([128], U16), "PM": sb([128]),
    "UY1": sb([16], U16), "LY1": sb([4, 16], U16), "UX1": sb([64], U16), "LX1": sb([4, 64], U16),
    "UZ1": sb([48], U16), "LZ1": sb([4, 48], U16),
    "UL": sb([4, 128], U16), "YTf": sb([4, 4, 8]),
    "YB": sb([48]), "UB": sb([48], U16), "HB": sb([48], U16), "LB": sb([4, 48], U16),
    "ci": sb([16], I32), "cf": sb([40]), "cn": sb([896]),
    "PK": sb([4], U16), "WM": sb([14], U16), "WT": sb([10], U16), "AL": sb([32], U16),
    "BL": sb([32], U16), "BJ": sb([8], U16), "VL": sb([8], U16), "SL": sb([16], U16), "LL": sb([6, 8], U16),
    "XL": sb([16], U16), "MK0": sb([4, 16]), "Hs": sb([128], B16), "Sel": sb([4, 128], B16), "Gs": sb([2, 8], B16),
    "Gf": sb([8]), "Wa": sb([128], B16), "Wc": sb([128], B16), "ID": sb([128]), "RC": sb([64]),
    "Qp": ("psum", [128, 1024], F), "PV": ("psum", [128, 512], F), "VS": ("psum", [128, 512], F),
    "KE": ("psum", [128, 1024], F), "Dp": ("psum", [128, 1024], F),
}
DSEMS = ["d%d" % k for k in range(20)]
ARR = ["E0", "E1", "V0", "V1", "X0", "Y1", "X1", "Z1", "B", "hX0", "hB"]
SEMAPHORES = ["sg", "sv", "ss", "st", "ls"] + DSEMS + ["a" + k for k in ARR]
BLOCKS = [(0, 0, 8), (0, 8, 32), (1, 0, 32), (2, 0, 32), (3, 0, 32), (0, 32, 48), (1, 32, 48), (2, 32, 48), (3, 32, 40), (3, 40, 48)]
CYC, PEC, HOP, DMA, FAR = 0.00085, 0.0005, 0.15, 2.0, 3.2
SLOW = {"fl": 8.0, "m0": 0.8, "m1": 6.0, "T0": 1.2, "T1": 1.2, "win0": 0.8}


def helpers(T, topo):
    out = []
    for c in T.cores:
        free = [x for x in topo.cores_of(c) if x not in T.cores and x not in out and topo.may_write(c, x)]
        near = [x for x in free if topo.die(x) == topo.die(c)]
        out.append((near or free)[0])
    return out


def common(topo, me, cs):
    m = -1
    for c in cs:
        m &= topo.mask(me, c)
    return m


def neng(topo, me, cs):
    return bin(common(topo, me, cs)).count("1")


def bcast(g, T, topo, me, src, dsts, name):
    cs = [c for c, _ in dsts]
    ids = [DstId(rid=topo.addr(c)[0], pnc=topo.addr(c)[1]) for c in cs]
    g.remote_dma_fused([RemoteDMATransfer(dst_ids=ids, dma_engine_mask=common(topo, me, cs), remote_sem=T.sem["a" + name],
                                          srcs=[src], dsts=[a for _, a in dsts])], local_sem=T.sem.ls)
    return neng(topo, me, cs)


def schedule(ops, pre, setup, chain):
    n_ops = len(ops)
    post = [dict() for op in ops]
    for n in range(n_ops):
        for d in pre[n]:
            post[d][n] = pre[n][d]

    def lay(before, after, rank):
        left = [len(x) for x in before]
        start, busy = [0.0] * n_ops, {}
        heap = sorted([(rank[n], n) for n in range(n_ops) if left[n] == 0], reverse=True)
        while heap:
            n = heap.pop()[1]
            at = max([start[d] + ops[d]["dur"] + before[n][d] for d in before[n]] + [0.0])
            row = busy.setdefault(ops[n]["q"], [])
            k = int(np.searchsorted([e for _, e in row], at, "right"))
            while k < len(row) and row[k][0] < at + ops[n]["dur"] - 1e-9:
                at = max(at, row[k][1])
                k += 1
            row.insert(k, (at, at + ops[n]["dur"]))
            start[n] = at
            for m in after[n]:
                left[m] -= 1
                if left[m] == 0:
                    heap.append((rank[m], m))
                    heap.sort(reverse=True)
        return start
    start = lay(pre, post, [float(n) for n in range(n_ops)])
    best, rank = None, [0.0] * n_ops
    for n in sorted(range(n_ops), key=lambda n: -start[n] - ops[n]["dur"]):
        rank[n] = min([rank[m] - post[n][m] for m in post[n]] + [0.0]) - ops[n]["dur"]
    for turn in range(2):
        for n in range(setup):
            if ops[n]["dur"] > 0.1:
                rank[n] = min(rank[n], rank[chain] + 1e-4 * n)
        start = lay(pre, post, rank)
        span = max(start[n] + ops[n]["dur"] for n in range(n_ops))
        if best is None or span < best[0]:
            best = (span, start)
        back = lay(post, pre, [-start[n] - ops[n]["dur"] for n in range(n_ops)])
        rank = [-back[n] - ops[n]["dur"] for n in range(n_ops)]
    return sorted(range(n_ops), key=lambda n: (best[1][n], n))


def rank_program(g, core, T, topo):
    o = T.rank_of(core)
    cores = list(T.cores)
    hl = helpers(T, topo)
    if o is None:
        if core in hl:
            r = hl.index(core)
            tot = 0
            for nm, hb, lb in (("X0", "HX0", "LX0"), ("B", "HB", "LB")):
                g.wait_ge(T.sem["ah" + nm], neng(topo, cores[r], [core]))
                tot += bcast(g, T, topo, core, T[hb][:], [(cores[k], T[lb][:, r]) for k in range(4) if k != r], nm)
            g.wait_ge(T.sem.ls, tot)
        return
    peers = [k for k in range(4) if k != o]
    every = [o] + peers
    Q = {"g": g, "v": g.vector, "s": g.scalar, "t": g.tensor, "y": g.sync}
    QS = {"g": "sg", "v": "sv", "s": "ss", "t": "st"}
    A = AluOpType
    AF = ActivationFunctionType
    ops, acc, groups, lsum, bank, line = [], {}, {}, [0], {}, [None]
    sl = slice

    def R(name, *idx, p=(0, 128, 1)):
        sh = SCRATCH[name][1]
        if len(idx) == 0:
            idx = (sl(0, sh[1]),)
        ar = np.arange(int(np.prod(sh[1:]))).reshape(sh[1:])[idx]
        lo, hi = int(ar.min()), int(ar.max()) + 1
        p0, p1 = p[0], p[1]
        if SCRATCH[name][0] == "psum":
            lo, hi, p0, p1 = lo // 512 * 512, (hi + 511) // 512 * 512, 0, 128
        ps = sl(p[0], p[1], p[2]) if len(p) > 2 and p[2] != 1 else sl(p[0], p[1])
        return (T[name][(ps,) + idx], [(name, p0, p1, lo, hi, ar.ravel())])

    def C(name, a, b, *idx, p=(0, 128, 1)):
        return R(name, sl(a, b), *idx, p=p)

    def ind(w, off):
        return (w[0].indirect(off[0]), w[1] + off[1], True)

    def regs(*xs):
        return [r for x in xs if isinstance(x, tuple) for r in x[1]]

    def val(x):
        return x[0] if isinstance(x, tuple) else x

    def rec(q, fn, rr, ww, kind="c", group=None, f=1.0):
        n = len(ops)
        deps, after = set(), set()
        for reg, isw in [(x, False) for x in rr] + [(x, True) for x in ww]:
            ps = SCRATCH[reg[0]][0] == "psum"
            for (r2, m, w2) in acc.get(reg[0], []):
                if m not in deps and r2[1] < reg[2] and reg[1] < r2[2] and r2[3] < reg[4] and reg[3] < r2[4]:
                    o2 = ops[m]
                    if o2["q"] == q and o2["kind"] == "c" and kind == "c":
                        if (w2 or isw) and q != "t" and len(np.intersect1d(reg[5], r2[5])):
                            deps.add(m)
                    elif (w2 or isw or ps) and not (kind == "d" and o2["kind"] == "d" and o2["group"] == group):
                        deps.add(m)
        if q == "t":
            key = (ww[0][0], ww[0][3])
            if key in bank:
                after.add(bank[key])
            bank[key] = n
        if line[0] and q in line[0]:
            if (line[0], q) in bank:
                after.add(bank[(line[0], q)])
            bank[(line[0], q)] = n
        for reg in rr:
            acc.setdefault(reg[0], []).append((reg, n, False))
        for reg in ww:
            acc.setdefault(reg[0], []).append((reg, n, True))
        dur = 0.08
        if kind == "c":
            e = len(ww[0][5])
            dur = f * e * CYC + 0.06 if f == 1.56 else max(64, f * e) * CYC
            if q == "t":
                dur = f * max(64, e) * PEC
            if q == "g":
                dur = 0.13 + 2 * e * CYC
        ops.append({"q": q, "fn": fn, "deps": deps, "after": after, "kind": kind, "group": group, "dur": dur})

    def short(*xs):
        return all(SCRATCH[x[1][0][0]][2] in (B16, H16, U16) for x in xs)

    def fac(a, f=1.0):
        return 1.56 if len(a) > 2 else f

    def cp(out, in_):
        rec("v", lambda: g.vector.tensor_copy(out[0], in_[0]), regs(in_), regs(out), f=fac(in_, 0.5 if short(out, in_) else 1.0))

    def tt(out, a, b, op):
        rec("v", lambda: g.vector.tensor_tensor(out[0], a[0], b[0], op), regs(a, b), regs(out),
            f=fac(a, 1.0 if "psum" in (SCRATCH[a[1][0][0]][0], SCRATCH[b[1][0][0]][0]) else 2.0))

    aside = [False]

    def floats(*xs):
        return aside[0] and all(len(x) == 2 and SCRATCH[x[1][0][0]][2] in (F, B16) for x in xs)

    def ts(out, a, s1, op0, s2=None, op1=None):
        if floats(out, a) and (op0, op1) in ((A.mult, A.add), (A.mult, None), (A.add, None)):
            act(out, a, scale=s1 if op0 == A.mult else 1.0, bias=s1 if op0 == A.add else 0.0 if s2 is None else s2)
        elif s2 is None:
            rec("v", lambda: g.vector.tensor_scalar(out[0], a[0], val(s1), None, op0), regs(a, s1), regs(out), f=fac(a))
        else:
            rec("v", lambda: g.vector.tensor_scalar(out[0], a[0], val(s1), val(s2), op0, op1), regs(a, s1, s2), regs(out))

    def scan(out, d0, d1, init, op0, op1):
        rec("v", lambda: g.vector.tensor_tensor_scan(out[0], d0[0], d1[0], init, op0, op1), regs(d0, d1), regs(out))

    def tr(out, in_):
        rec("v", lambda: g.vector.transpose(out[0], in_[0]), regs(in_), regs(out), f=0.5 if short(out, in_) else 1.0)

    def ms(out, c):
        rec("v", lambda: g.vector.memset(out[0], c), [], regs(out), f=0.5 if short(out) else 1.0)

    def act(out, in_, bias=0.0, scale=1.0):
        rec("s", lambda: g.scalar.activation(out[0], in_[0], AF.Identity, bias=val(bias), scale=val(scale)),
            regs(in_, bias, scale), regs(out), f=fac(in_))

    def mm(out, l, r, st, sp):
        rec("t", lambda: g.tensor.matmul(out[0], l[0], r[0], st, sp), regs(l, r), regs(out),
            f=4.0 if SCRATCH[l[1][0][0]][2] == F else 1.0)

    def iota(out, pat, base, step=0):
        rec("g", lambda: g.iota(out[0], pat, base, step, allow_small_or_imprecise_dtypes=True), [], regs(out))

    def dma(q, out, in_, group, also=None):
        if group not in groups:
            groups[group] = [DSEMS[len([x for x in groups if x not in ARR])], 0]
        groups[group][1] += 16
        rec(q, lambda: Q[q].dma_start(val(out), val(in_)), regs(in_, also), regs(out), "d", group)

    def arrive(name, n, land):
        groups[name] = ["a" + name, n]
        rec("x", None, [], regs(*[R(land, k) for k in peers]), "a", name)

    def send(name, src, dsts):
        def fn():
            lsum[0] += bcast(g, T, topo, core, src[0], dsts, name)
        rec("g", fn, regs(src), [], "r", name)

    def to_all(name, src, land):
        send(name, R(src), [(cores[k], T[land][:, o]) for k in peers])

    def relay(name, src, hb):
        send("h" + name, R(src), [(hl[o], T[hb][:])])

    n_direct = sum(neng(topo, cores[k], [cores[j] for j in range(4) if j != k]) for k in peers)
    n_relay = sum(neng(topo, hl[k], [cores[j] for j in range(4) if j != k]) for k in peers)

    def cf(k):
        return C("cf", k, k + 1)

    used = [160]

    def pattern(pat, base):
        n = int(np.prod([c for _, c in pat]))
        x = C("cn", used[0], used[0] + n)
        used[0] += n
        iota(x, pat, base)
        return x

    def bus(name, a, n=1):
        return C(name, 48 * a, 48 * (a + n))

    def xx(ch, a, n=1):
        return C("XX", 128 * (14 * ch + a), 128 * (14 * ch + a + n))

    def lst(ch, a, n=1):
        return C("L", 8 * (15 * ch + a), 8 * (15 * ch + a + n))

    def blk(b):
        return (32 * b, 32 * b + 32)

    def rows(b, r):
        return (32 * b + r, 32 * b + 32, 16)

    def wrap768(src, dst, step=384):
        for c0 in range(0, 768, step):
            tr(C(dst, c0, c0 + step), C(src, 16 + c0, 16 + step + c0))
        for c0 in range(0, 768, step):
            c1 = c0 + step if c0 + step < 768 else 800
            tr(C(dst, 768 + c0, 768 + c1), C(src, c0, c1))

    def place(dst, own, land):
        for b in range(4):
            for k in every:
                cp(dst(k, b), own(b) if k == o else land(k, b))

    dma("y", R("Di", p=(0, 16)), T.par[2 * o:2 * o + 2, :], "in")
    dma("s", R("Di", p=(16, 32)), T.res[2 * o:2 * o + 2, 0:S], "in")
    dma("y", R("tiei"), T.tie[:], "tie")
    dma("s", R("Di", p=(32, 48)), T.res[2 * o:2 * o + 2, S:2 * S], "in")
    pi = C("ci", 8, 9)
    iota(C("t6", 0, 128), [[0, 4], [8, 2], [16, 16]], 0, -1)
    rec("g", lambda: g.iota(pi[0], [[1, 1]], 0, 1), [], regs(pi))
    iota(C("t6", 128, 256), [[2, 4], [8, 2], [16, 16]], 0, -1)
    ms(C("Yw", 1024, 1536), 0.0)

    def fill(out, c):
        act(out, C("Yw", 1536 - len(out[1][0][5]), 1536), bias=c)
    banks = [C(nm, z, z + 384) for nm, z in (("KE", 0), ("KE", 512), ("PV", 0), ("VS", 0), ("Dp", 0), ("Dp", 512), ("Qp", 0), ("Qp", 512))]

    for c in range(10):
        ts(R("SC", c, p=(0, 48)), C("t6", 128 * (c // 8), 128 * (c // 8) + 128, p=(0, 48)), -float(c % 8), A.is_equal)
    dh = R("Dh", p=(0, 48))
    ts(dh, R("Di", p=(0, 48)), -MID, A.add)
    for c in range(8):
        mm(banks[c], R("SC", c, p=(0, 48)), dh, True, True)
        (cp if c % 2 else act)(C("Win", 384 * c, 384 * c + 384), banks[c])
    for z in range(2):
        mm(banks[z], R("SC", 8 + z, p=(0, 48)), dh, True, True)
        for c0 in range(0, 384, 128):
            act(C("M", 16 + 384 * z + c0, 144 + 384 * z + c0), C("KE", 512 * z + c0, 512 * z + c0 + 128))
    for j in range(4):
        dma("y", C("W0", 768 * j, 768 * j + 768), T.fl[:, 768 * j:768 * j + 768], "fl", R("Di", p=(0, 48)))
    for k, (sh, mk) in enumerate(((3, 1), (0, 7), (0, 15), (4, 1), (0, 1), (5, 3), (4, 7), (0, 127))):
        ts(C("ci", k, k + 1), pi, sh, A.logical_shift_right, mk, A.bitwise_and)
    cp(C("cf", 0, 8), C("ci", 0, 8))
    ms(R("PK"), 0)
    ms(R("CH"), 0)
    fill(R("X"), 0.0)
    tt(cf(8), cf(3), cf(4), A.not_equal)
    ts(cf(10), cf(8), 144.0, A.mult)
    ts(cf(11), cf(1), 16.0, A.mult, cf(10), A.add)
    for t in range(2):
        ts(C("PK", 2 * t, 2 * t + 1), cf(0), 1.0 + t, A.mult, cf(11), A.add)
        fill(R("CH%d" % t), 0.0)
    for b in range(4):
        cp(R("ENDS", p=blk(b)), R("tiei", sl(0, 4), sl(8 * b, 8 * b + 8), p=blk(o)))
    aside[0] = True
    fill(C("cn", 0, 16), 0.0)
    fill(C("cn", 136, 160), 128.0)
    iota(C("cn", 16, 136), [[1, 4], [8, 15], [4, 2]], 0)
    tr(C("TW", 0, 128), C("cn", 16, 144))
    tr(C("TW", 128, 288), C("cn", 0, 160))
    cp(R("SL"), ind(C("TW", 0, 288), C("PK", 0, 1)))
    ts(cf(14), cf(0), -16.0, A.mult)
    ts(cf(15), cf(1), -16.0, A.mult)
    ts(R("AL"), pattern([[1, 8], [-32, 4]], 112), cf(14), A.add)
    ts(R("BL"), pattern([[1, 8], [0, 4]], 240), cf(15), A.add)
    ts(R("BJ"), pattern([[8, 2], [0, 4]], 0), cf(1), A.add)
    ts(R("VL"), pattern([[32, 8]], 0), cf(14), A.subtract, cf(1), A.add)
    c8, c16 = pattern([[1, 8]], 0), pattern([[16, 16]], 0)
    ts(cf(19), cf(1), 7.0, A.is_lt)
    ts(cf(20), cf(0), 8.0, A.mult)
    ts(cf(21), cf(2), 16.0, A.mult)
    ts(cf(22), cf(2), 8.0, A.mult, -128.0, A.add)
    ts(cf(22), cf(22), cf(19), A.mult, 128.0, A.add)
    ts(cf(23), cf(2), 0.0, A.is_equal, 144.0, A.mult)
    ts(cf(24), cf(2), 8.0, A.is_equal, -112.0, A.mult)
    ts(cf(23), cf(23), cf(24), A.add, cf(21), A.add)
    BJ2, VL2, REP, CL, T1L, PVL = [R("LL", k) for k in range(6)]
    ts(BJ2, c8, cf(20), A.add)
    ts(VL2, c8, cf(21), A.add)
    cp(REP, pattern([[16, 8]], 15))
    cp(CL, c8)
    ts(T1L, c8, cf(19), A.mult, cf(22), A.add)
    ts(PVL, c8, cf(23), A.add, -16.0, A.add)
    ts(cf(25), cf(3), -544.0, A.mult, 272.0, A.add)
    ts(cf(26), cf(3), 272.0, A.mult, cf(2), A.add)
    ts(C("t1", 0, 16), pattern([[0, 8], [1, 2]], 0), cf(25), A.mult, cf(26), A.add)
    tt(C("t1", 16, 32), C("t1", 0, 16), c16, A.add)
    cp(R("XL"), C("t1", 16, 32))
    ts(cf(12), cf(8), 784.0, A.mult)
    ts(cf(13), cf(2), 16.0, A.mult, cf(12), A.add)
    ts(C("WM", 4, 10), pattern([[1, 2], [256, 3]], 1), cf(13), A.add)
    ts(C("WT", 0, 3), C("WM", 4, 7), -1.0, A.add)
    fill(R("INC"), 1.0)
    fill(R("INC", sl(0, 512, 64)), -1000.0)
    for nm, step in (("RS16", 16), ("RS8", 8)):
        fill(R(nm), 1.0)
        fill(R(nm, sl(0, 128, step)), 0.0)
    iota(C("POSX", 64, 128), [[1, 8], [0, 8]], 1)
    iota(C("POSX", 0, 64), [[8, 8], [0, 8]], 8)
    p8 = pattern([[0, 8], [1, 8]], 1)
    for sd, (a, c) in enumerate(((8.0, 8.0), (1.0, 0.5))):
        ts(R("q3", 0, sl(0, 8), sl(8 * sd, 8 * sd + 8)), p8, a, A.mult)
        ts(R("q3", 1, sl(0, 8), sl(8 * sd, 8 * sd + 8)), p8, c, A.mult)
    act(R("POS2"), R("q3", 0))
    act(R("CODE"), R("q3", 1))
    ts(R("CODW"), R("CODE"), 1.0 / 64.0, A.mult)
    ts(cf(16), cf(5), 128.0, A.mult, cf(2), A.add)
    iota(R("TIE"), [[16, 8], [0, 16]], 0)
    ts(R("TIE"), R("TIE"), cf(16), A.add)
    rc = pattern([[1, 8], [1, 8]], 1)
    rec("v", lambda: g.vector.reciprocal(T.RC[:], rc[0]), regs(rc), regs(R("RC")), f=10.0)
    iota(R("VI"), [[1, 768]], -ZC)
    ts(cf(9), cf(5), 768.0, A.mult)
    act(R("VI"), R("VI"), bias=cf(9))
    ts(cf(31), cf(2), cf(9), A.add)
    ts(R("BV", 1), pattern([[16, 48]], 0), cf(31), A.add)
    ts(bus("ZV", 0), R("BV", 1), -1.0, A.mult, float(ZC), A.add)
    for nm, a, b, c in (("M", 0, 16, 0.0), ("M", 784, 800, 0.0), ("LF", 120, 144, 0.0),
                        ("XT", 0, 16, 0.0), ("XT", 272, 288, 0.0),
                        ("W0", ZC, NEG, 0.0), ("W1", ZC, NEG, 0.0)):
        fill(C(nm, a, b), c)
    fill(C("CW", 1024, 1536), -1.0)
    ms(R("Wv"), 0)
    ts(R("Gf"), c8, cf(6), A.is_equal)
    act(R("Gs", 0), R("Gf"))
    ts(R("Gs", 1), R("Gf"), 128.0, A.mult)
    ones = {F: R("t4"), B16: R("VT", 0, 0)}
    for x in ones.values():
        fill(x, 1.0)

    def picker(out, pat, base):
        one = ones[SCRATCH[out[1][0][0]][2]]
        rec("g", lambda: g.affine_select(out[0], one[0], pat, A.is_equal, 0.0, base, -1), regs(one), regs(out))
    picker(R("ID"), [[1, 128]], 0)
    for u in range(2):
        for h in range(2):
            picker(R("Sel", 2 * u + h), [[16, 4], [1000, 2], [1, 16]], 64 * u - 1000 * h)
    picker(R("PM"), [[16, 2], [32, 4], [1, 16]], 0)
    for x in [R("Wa"), R("Wc")] + [R("Wl", k) for k in range(4)]:
        fill(x, 0.0)
    ts(cf(27), cf(1), 1.0, A.add)
    ts(cf(28), cf(0), 512.0, A.mult, -1024.0, A.add)
    ts(cf(29), cf(2), 0.0, A.is_equal)
    ts(cf(30), cf(1), 0.0, A.is_gt)
    ts(R("Wa", sl(0, 128, 16)), R("Gf"), cf(27), A.mult)
    ts(R("Wc", sl(0, 128, 16)), R("Gf"), -1.0, A.mult)
    for k, c in enumerate((cf(28), cf(30), 1.0, cf(29))):
        ts(R("Wl", k, sl(15, 143, 16)), R("Gf"), c, A.mult)

    def listed(out, k, src, c0=0, c1=48):
        for r in range(16):
            mm(out, R("Wl", k, sl(15 - r, 143 - r)), R(src, sl(16 * c0 + r, 16 * c1, 16)), r == 0, r == 15)
    ts(cf(17), cf(3), -16.0, A.mult, cf(7), A.add)
    ts(R("Hs"), pattern([[0, 4], [1, 2], [0, 16]], 0), cf(3), A.is_equal)
    ts(R("MK0"), pattern([[32, 4], [1, 16]], 0), cf(17), A.is_equal)
    wrap768("M", "TW", 128)
    act(bus("RM", 1, 2), ind(R("TW"), C("WM", 4, 10)), bias=MID)
    act(R("BV", 2), ind(R("TW"), C("WT", 0, 3)), bias=NEG - ZC + MID)
    ts(R("RF"), bus("RM", 1, 2), 1024.0, A.add)
    cp(bus("Ri", 0, 2), bus("RM", 1, 2))
    ts(bus("Ri", 2, 2), bus("Ri", 0, 2), 7, A.logical_shift_right)
    ts(bus("TK", 0, 2), bus("Ri", 2, 2), 128.0, A.mult)
    tt(bus("IX", 0, 2), bus("TK", 0, 2), bus("RM", 1, 2), A.add)
    line[0] = "vst"
    cp(R("RL"), bus("IX", 0, 2))
    line[0] = None
    aside[0] = False

    def update(t, W, dst):
        for nm, c0, c1 in ((("Y1", 0, 16), ("X1", 16, 80), ("Z1", 80, 128)) if t else (("X0", 0, 128),)):
            arrive(nm, n_direct if t else n_relay, "L" + nm)
            place(lambda k, b: R("UL", b, sl(c0, c1), p=blk(k)), lambda b: R("U" + nm, p=blk(b)),
                  lambda k, b: R("L" + nm, k, p=blk(b)))
        for sd in range(2):
            for b in range(4):
                act(C("Yw", 512 * sd + 128 * b, 512 * sd + 128 * b + 128), ind(R(W), R("UL", b, sl(8 * sd, 8 * sd + 8))))
        for b, c0, c1 in BLOCKS:
            x0, x1 = 768 * b + 16 * c0, 768 * b + 16 * c1
            iy, ix = (16, 48) if c0 < 32 else (64, 80)
            act(C("Yg", x0, x1), ind(R("Yw"), R("UL", b, sl(iy + c0, iy + c1))))
            tt(C(dst, x0, x1), ind(R(W), R("UL", b, sl(ix + c0, ix + c1))), C("Yg", x0, x1), A.add)
            if t:
                dma("y", T.yf[:, x0:x1], C(dst, x0, x1), "out")
        for sd in range(2):
            cp(R("YTf", 2 * t + sd), C("UL", 0, 4, sl(80 + 8 * sd, 88 + 8 * sd)))

    marks = [len(ops)]
    for t in range(2):
        W, CHf = "W%d" % t, "CH%d" % t
        wn = C(W, 0, NEG)
        pk = C("PK", 2 * t, 2 * t + 1)
        for sd in range(2):
            cp(R("CH", 8 * sd, sl(0, 8)), R("ENDS", 2 * t + sd))
            act(C(CHf, 128 * sd, 128 * sd + 8), R("ENDS", 2 * t + sd))
        for s in range(7):
            for sd in range(2):
                act(R("X", sd, sl(16, 144)), ind(R("Win"), R("CH", 8 * sd + s, sl(0, 8))))
                y = 2 * (s % 2) + sd
                tr(R("TT", y, sl(0, 128)), R("X", sd, sl(16, 144)))
                tr(R("TT", y, sl(128, 288)), R("X", sd))
                if s < 6:
                    ts(R("CH", 8 * sd + s + 1), ind(R("TT", y), pk), MID, A.add)
                z = 16 * (8 * sd + s + 1)
                act(C(CHf, z, z + 16), ind(R("TT", y), pk), bias=MID)
        chw = C(CHf, 0, 256)
        for hf in range(2):
            (cp if hf else act)(C("AA", 256 * hf, 256 * hf + 256), ind(C(CHf, 0, 128), C("AL", 16 * hf, 16 * hf + 16)))
        ops[-1]["after"].update((len(ops) - 5, len(ops) - 4))
        act(R("AM"), ind(chw, R("VL")), bias=-float(ZC))
        for hf in range(2):
            tt(C("NE", 256 * hf, 256 * hf + 256), ind(chw, C("BL", 16 * hf, 16 * hf + 16)), C("AA", 256 * hf, 256 * hf + 256), A.not_equal)
        for hf in range(2):
            scan(*[C(nm, 256 * hf, 256 * hf + 256) for nm in ("KS", "INC", "NE")], 0.0, A.add, A.mult)
        ts(C("IJ", 0, 8), R("KS", sl(63, 512, 64)), 0.0, A.max)
        ts(C("IJ", 8, 16), C("IJ", 0, 8), 7, A.bitwise_and)
        ts(C("LF", 56, 64), C("IJ", 0, 8), -float(ZC), A.add)
        tt(R("ON"), ind(R("IJ"), R("BJ")), R("POSX"), A.is_ge)
        for c0 in (0, 64):
            tt(C("LF", c0, c0 + 56), C("AM", c0, c0 + 56), C("ON", c0, c0 + 56), A.mult)
        sbf, ls = "SB%d" % t, "LS%d" % t
        ts(R(sbf), ind(R("LF"), C("SL", 0, 8)), float(ZC), A.add)
        send("E%d" % t, C(sbf, 0, 120), [(cores[k], T[ls][:, o, 0:120]) for k in peers])
        if t == 0:
            marks.append(len(ops) - 1)
        else:
            update(0, "W0", "W1")
        act(C("XT", 16, 144), ind(R("LF"), T1L))
        act(C("XT", 144, 272), ind(chw, PVL), bias=-MID)
        act(R("n1"), ind(C(CHf, 16, 272), VL2))

        def spread():
            act(R("TP"), ind(C("TW", 0, 544), R("XL")))
            for b in range(4):
                for b2 in range(4):
                    dma("y", C("T12", 256 * b, 256 * b + 256, p=blk(b2)), R("TP", p=blk(b)), "T%d" % t)
        kept = [lambda: tr(C("TW", 0, 256), C("XT", 16, 272)),
                lambda: tr(C("TW", 256, 544), R("XT")),
                lambda: tt(R("t1"), ind(C(CHf, 24, 272), VL2), R("TIE"), A.not_equal),
                lambda: tt(R("ON2"), ind(R("IJ"), BJ2), R("POS2"), A.is_ge),
                lambda: tt(R("t2"), R("t1"), R("ON2"), A.mult),
                lambda: tt(R("t4"), R("ON2"), R("CODW"), A.mult),
                lambda: scan(R("t5"), R("RS16"), R("t2"), 0.0, A.mult, A.subtract),
                lambda: tt(R("KW"), ind(R("t5"), REP), R("t4"), A.add)]
        if t == 0:
            line[0] = "vst"
            for x in kept:
                x()
            line[0] = None
            spread()
            kept = []
        arrive("E%d" % t, n_direct, ls)
        place(lambda k, b: R("L", sl(b, 480, 4), p=blk(k)), lambda b: C(sbf, 0, 120, p=blk(b)),
              lambda k, b: R(ls, k, sl(0, 120), p=blk(b)))
        seq = list(range(7, 14)) + list(range(6, -1, -1))
        dq = [C(("Qp", "KE")[ch // 2], 512 * (ch % 2), 512 * (ch % 2) + 128) for ch in range(4)]

        def gather(ch):
            cut = 7 - CUT[t][ch]
            for p0, p1 in ((0, min(cut, 4)), (4, cut)):
                if p0 < p1:
                    act(xx(ch, p0, p1 - p0), ind(wn, lst(ch, p0, p1 - p0)), bias=-0.0625)
            for p0, p1 in ((7, 10), (10, 14)):
                act(xx(ch, p0, p1 - p0), ind(wn, lst(ch, 1 + p0, p1 - p0)), scale=-1.0, bias=0.0625)
            act(R("RR", ch), ind(R("RC"), lst(ch, 7)))

        def share(ch, p0, p1):
            return lambda: ts(xx(ch, p0, p1 - p0), ind(wn, lst(ch, p0, p1 - p0)), -0.0625, A.add)

        def sums(ch):
            for n, x in enumerate(seq[:NPE[ch]]):
                mm(dq[ch], R("ID"), xx(ch, x), n == 0, n == NPE[ch] - 1)

        def limit(ch):
            mine, part, last = seq[NPE[ch]:], C("VS", 0, 128), R("t6", sl(0, 128))
            return [lambda: tt(part, xx(ch, mine[0]), xx(ch, mine[1]), A.add)] + \
                   [lambda x=x: tt(part if x != mine[-1] else last, part, xx(ch, x), A.add) for x in mine[2:]] + \
                   [lambda: tt(dq[ch], dq[ch], last, A.add), lambda: tt(dq[ch], dq[ch], R("RR", ch), A.mult)]

        def compare(ch):
            return [lambda x=x: tt(R("VT", ch, x), xx(ch, x), dq[ch], A.is_ge if x > 6 else A.is_le)
                    for pos in range(7) for x in (pos, 7 + pos)]

        def count(ch):
            for pos in range(7):
                pv = R("PV", sl(7 * ch + pos, 224, 28))
                mm(pv, R("VT", ch, pos), R("Gs", 0), True, False)
                mm(pv, R("VT", ch, 7 + pos), R("Gs", 1), False, True)

        def weave(chain, fill):
            for n, x in enumerate(chain):
                x()
                for y in fill[n * len(fill) // len(chain):(n + 1) * len(fill) // len(chain)]:
                    y()
        line[0] = "vst"
        for ch in range(2):
            gather(ch)
        ones = [share(ch, p, p + 1) for ch in (1, 2) for p in range(7 - CUT[t][ch], 7)]
        sums(0)
        weave([share(0, 4, 7), share(0, 2, 4)], [])
        weave(limit(0), [share(0, 1, 2), share(0, 0, 1)] + kept[:2] + ones)
        del kept[:2]
        if t == 1:
            spread()
        gather(2)
        gather(3)
        sums(1)
        sums(2)
        for ch in range(3):
            weave(limit(ch + 1), compare(ch))
            count(ch)
            if ch == 0:
                sums(3)
        weave(compare(3), [])
        count(3)
        sv, lv = "SV%d" % t, "LV%d" % t
        ts(R(sv), C("PV", 0, 224), -OFS, A.add)
        sent_votes = len(ops) - 1
        line[0] = None

        def send_votes(sv=sv, lv=lv, t=t):
            trs = []
            for j, k in enumerate(peers):
                es = topo.engines(core, cores[k])
                n = len(es) // 4
                ad = topo.addr(cores[k])
                trs.append(RemoteDMATransfer(dst_ids=[DstId(rid=ad[0], pnc=ad[1])], dma_engine_mask=sum(1 << e for e in es[n * j:n * j + n]),
                                             remote_sem=T.sem["aV%d" % t], src=T[sv][:, k], dst=T[lv][:, o]))
                lsum[0] += n
            g.remote_dma_fused(trs, local_sem=T.sem.ls)
        rec("g", send_votes, regs(R(sv)), [], "r", "V%d" % t)
        for j in range(8):
            act(C(W, NEG + 384 * j, NEG + 384 * j + 384), C(W, 384 * j, 384 * j + 384), scale=-1.0)
        halves = [(384 * z, 512 * z) for z in range(2)]
        rl = {c0: C("RL", 48 * t + c0 // 16, 48 * t + c0 // 16 + 24) for c0, z in halves}
        for x in kept:
            x()
            ops[-1]["after"].add(sent_votes)
        for c0, z in halves:
            tt(C("EQ", c0, c0 + 384), ind(R("T12"), rl[c0]), C("VI", c0, c0 + 384), A.is_equal)
            ops[-1]["after"].add(sent_votes)
            mm(C("Dp", z, z + 384), R("Wa"), C("EQ", c0, c0 + 384), True, True)
        act(R("P"), C("Dp", 0, 384))
        listed(C("KE", 0, 48), 0, "EQ")
        tt(R("BV", 0), C("KE", 0, 48), bus("RF", t), A.add)
        cp(R("TS"), R("BV", 0))
        act(R("DV", 0), C("KE", 0, 48), scale=-2.0, bias=-1536.0)
        listed(C("KE", 512, 560), 1, "EQ")
        for c0, z in halves:
            tt(C("PR", c0, c0 + 384), ind(C("T12", 128, 1024), rl[c0]), C("EQ", c0, c0 + 384), A.mult)
            if t == 0:
                mm(C("Qp", z, z + 384), R("Wc"), C("PR", c0, c0 + 384), True, False)
                mm(C("Qp", z, z + 384), R("SC", 8 + z // 512, p=(0, 16)), R("Dh", p=(0, 16)), False, True)
        listed(C("PV", 0, 48), 2, "PR")
        act(bus("NB", 0), C("PV", 0, 48), bias=NEG - ZC + MID)
        tt(bus("ZV", 1), C("KE", 512, 560), bus("NB", 0), A.mult)
        tt(R("DV", 1), bus("ZV", 1), bus("ZV", 0), A.add)
        tt(R("DV", 2), bus("NB", 0), R("BV", 2) if t == 0 else bus("IX", 2), A.subtract)
        arrive("V%d" % t, sum(len(topo.engines(cores[k], core)) // 4 for k in peers), lv)
        for u in range(2):
            n = 0
            for k in every:
                for h in range(2):
                    mm(C("VS", 28 * u, 28 * u + 28), R("Sel", 2 * u + h), R(sv if k == o else lv, k, sl(28 * h, 28 * h + 28)), n == 0, n == 7)
                    n += 1
        vs = C("VS", 0, 56)
        ts(R("Si"), vs, 4 * OFS + 31.0, A.add)
        ts(R("Wv", sl(1, 16, 2), sl(0, 7)), vs, 33.0 * 128.0 - 4 * OFS, A.is_ge, 64.0, A.mult)
        ts(R("Wv", sl(0, 16, 2), sl(0, 7)), R("Si"), 64, A.bitwise_and)
        tt(R("t1"), R("Wv"), R("KW"), A.mult)
        scan(R("KM"), R("RS8"), R("t1"), 0.0, A.mult, A.max)
        ka, kb = R("KM", sl(7, 128, 16)), R("KM", sl(15, 128, 16))
        tt(R("KP"), ka, kb, A.subtract)
        for j in range(8):
            if j % 2:
                act(R("E", j), R("MK0"), scale=C("KP", j, j + 1))
            else:
                ts(R("E", j), R("MK0"), C("KP", j, j + 1), A.mult)
        for sd in range(2):
            for b in range(4):
                mm(C("KE", 512 * sd + 128 * b, 512 * sd + 128 * b + 128), R("Hs"), C("E", 0, 8, b), True, True)
        act(C("CW", 512, 1024), C("KE", 512, 1024), bias=0.5, scale=-2.0)
        ts(C("CW", 0, 512), C("KE", 0, 512), 0.125, A.mult, 0.5, A.add)

        def turns(c0, c1):
            out = C("TN", 16 * c0, 16 * c1)
            if c0 < 24:
                tt(out, ind(R("CW"), C("TS", c0, c1)), C("P", 16 * c0, 16 * c1), A.is_gt)
            else:
                act(C("Yg", 16 * c0, 16 * c1), ind(R("CW"), C("TS", c0, c1)))
                tt(out, C("Yg", 16 * c0, 16 * c1), C("Dp", 128 + 16 * c0, 128 + 16 * c1), A.is_gt)

        def opened():
            tt(R("cm"), ka, kb, A.max)
            tt(R("t2"), ind(R("cm"), CL), R("CODE"), A.is_equal)
            tt(C("t6", 0, 128), ind(chw, VL2), R("t2"), A.mult)
            scan(C("t7", 0, 128), R("RS16"), C("t6", 0, 128), 0.0, A.mult, A.add)
            ts(C("u1", 0, 8), R("cm"), 0.0, A.is_equal, float(ZC), A.mult)
            ts(C("u1", 16, 24), R("cm"), 8.0, A.is_ge, float(NEG), A.mult)
            ts(C("u1", 24, 32), R("KP"), 0.0, A.is_lt, float(NEG), A.mult)
            for sd in range(2):
                tt(C("u1", 32 + 8 * sd, 40 + 8 * sd), C("u1", 16 + 8 * sd, 24 + 8 * sd), C("u1", 0, 8), A.add)
                tt(C("t3", 8 * sd, 8 * sd + 8), C("u1", 32 + 8 * sd, 40 + 8 * sd), R("t7", sl(15, 128, 16)), A.add)
            if t == 0:
                cp(C("UX0", 0, 16), C("t3", 0, 16))
            else:
                cp(R("UY1"), C("t3", 0, 16))
                to_all("Y1", "UY1", "LY1")

        def ends():
            tt(C("t6", 128, 256), R("n1"), R("t2"), A.mult)
            scan(C("t7", 128, 256), R("RS16"), C("t6", 128, 256), 0.0, A.mult, A.add)
            ts(C("u1", 8, 16), R("cm"), 0.0, A.is_equal)
            for sd in range(2):
                tt(C("u1", 48 + 8 * sd, 56 + 8 * sd), C("u1", 8, 16), R("ENDS", 2 * t + sd), A.mult)
            tt(C("t3", 16, 32), C("u1", 48, 64), R("t7", sl(15, 256, 16)), A.add)
            cp(C("UX0", 80, 96) if t == 0 else C("UZ1", 0, 16), C("t3", 16, 32))

        def sources(part):
            c0, c1 = (0, 32, 48)[part:part + 2]
            n, turn = c1 - c0, C(("VS", "PV")[part], 0, c1 - c0)
            listed(turn, 3, "TN", c0, c1)
            for k in range(2):
                tt(C("TK", 2 * c0 + k * n, 2 * c0 + k * n + n), turn, R("DV", k, sl(c0, c1)), A.mult)
            tt(C("IX", 2 * c0, 2 * c1), C("TK", 2 * c0, 2 * c1), C("BV", 0, 2, sl(c0, c1)), A.add)
            cp((C("UX0", 16, 80), C("UX0", 96, 128), R("UX1"), C("UZ1", 16, 48))[2 * t + part], C("IX", 2 * c0, 2 * c1))
            tt(C("TK", 96 + c0, 96 + c1), turn, R("DV", 2, sl(c0, c1)), A.mult)

        def listed_parents():
            tt(bus("IX", 2), bus("TK", 2), R("BV", 2) if t == 0 else bus("IX", 2), A.add)

        def parents():
            for c0, z in halves:
                tt(C("Qp", z, z + 384), C("Qp", z, z + 384), C("TN", c0, c0 + 384), A.mult)
            for c0, z in halves:
                tt(C("N", c0, c0 + 384), C("M", 16 + c0, 400 + c0), C("Qp", z, z + 384), A.subtract)
        if t == 0:
            turns(0, 24)
            turns(24, 48)
            parents()
            mark = len(ops) - 1
            for z in range(8):
                dma("ys"[z % 2], R("Win", p=(16 * z, 16 * z + 1)), R("N", p=(16 * (z % 2), 128, 32)), "win1")
            first = len(ops)
            opened()
            ops[first + 2]["after"].add(mark)
            ends()
            first = len(ops)
            sources(0)
            ops[first + 16]["after"].add(mark)
            sources(1)
            relay("X0", "UX0", "HX0")
        else:
            opened()
            mark = len(ops) - 2
            turns(0, 24)
            ops[-1]["after"].add(mark)
            turns(24, 32)
            sources(0)
            to_all("X1", "UX1", "LX1")
            turns(32, 48)
            ends()
            sources(1)
            to_all("Z1", "UZ1", "LZ1")
        listed_parents()
    for j in range(3):
        ts(C("XT", 16 + 16 * j, 32 + 16 * j), R("IX", sl(96 + j, 144, 3)), float(ZC - NEG), A.add)
    tr(C("TW", 0, 64), C("XT", 16, 80))
    tr(C("TW", 256, 352), C("XT", 0, 96))
    act(R("YB"), ind(C("TW", 0, 352), C("XL", 0, 3)))
    mm(C("VS", 0, 48), R("PM"), R("YB"), True, True)
    cp(R("UB"), C("VS", 0, 48))
    relay("B", "UB", "HB")
    update(1, "W1", "W0")
    dma("y", T.yt[:], R("YTf"), "out")
    arrive("B", n_relay, "LB")
    for k in every:
        cp(bus("NB", k), R("LB", k) if k != o else R("UB"))
        dma("y", T.yp[2 * k:2 * k + 2, :], bus("NB", k), "out")

    pre = [dict() for op in ops]
    members, sent = {}, {}
    for n, op in enumerate(ops):
        if op["kind"] == "d":
            members.setdefault(op["group"], []).append(n)
        if op["kind"] == "r":
            sent[op["group"]] = n
    for n, op in enumerate(ops):
        for d in op["after"]:
            pre[n][d] = 0.0
        for d in op["deps"]:
            if ops[d]["kind"] == "d":
                for m in members[ops[d]["group"]]:
                    pre[n][m] = DMA + SLOW.get(ops[d]["group"], 0.4)
            else:
                pre[n][d] = HOP if ops[d]["kind"] == "c" else 0.0
        if op["kind"] == "a":
            nm = op["group"]
            pre[n][sent[nm] if nm in sent else sent["h" + nm]] = (FAR - 0.5 if nm[0] == "Y" else FAR) if nm in sent else 2 * FAR - 0.5
    tail = len(ops)
    ops.append({"q": "x", "fn": None, "deps": set(), "after": set(), "kind": "a", "group": "out", "dur": 0.0})
    pre.append({m: DMA for m in members["out"]})
    order = [n for n in schedule(ops, pre, *marks) if n != tail]

    need = set(d for op in ops for d in op["deps"] if ops[d]["kind"] == "c")
    cnt = {q: 0 for q in QS}
    tok = {}
    for n in order:
        op = ops[n]
        if n in need:
            cnt[op["q"]] += 1
            tok[n] = (QS[op["q"]], cnt[op["q"]])
        elif op["kind"] in "da":
            tok[n] = tuple(groups[op["group"]])
    seen = {q: {} for q in Q}
    for n in order:
        op = ops[n]
        q = op["q"]
        if op["kind"] == "a":
            continue
        want = {}
        for d in op["deps"]:
            if d in tok:
                want[tok[d][0]] = max(want.get(tok[d][0], 0), tok[d][1])
        for sname, c in want.items():
            if seen[q].get(sname, 0) < c:
                Q[q].wait_ge(T.sem[sname], c)
                seen[q][sname] = c
        ins = op["fn"]()
        if op["kind"] == "d":
            ins.then_inc(T.sem[groups[op["group"]][0]], 16)
        elif n in tok:
            ins.then_inc(T.sem[tok[n][0]], 1)
    for q in QS:
        if cnt[q]:
            g.wait_ge(T.sem[QS[q]], cnt[q])
    for nm in groups:
        g.wait_ge(T.sem[groups[nm][0]], groups[nm][1])
    g.wait_ge(T.sem.ls, lsum[0])
